import numpy as np
import ml_dtypes


def mxq(x, axis, fmt="e4m3"):
    dtype, down = {"e4m3": (ml_dtypes.float8_e4m3fn, 7), "e5m2": (ml_dtypes.float8_e5m2, 14)}[fmt]
    v = np.moveaxis(np.asarray(x, np.float32).astype(ml_dtypes.bfloat16).astype(np.float64), axis, -1)
    blocks = v.reshape(v.shape[:-1] + (-1, 32))
    amax = np.abs(blocks).max(-1, keepdims=True)
    byte = np.maximum(np.where(amax > 0, np.frexp(amax)[1] - 1 + 127, 0) - down, 1)
    scale = np.exp2(byte - 127.0)
    codes = (blocks / scale).astype(np.float32).astype(dtype).astype(np.float64)
    return np.moveaxis((codes * scale).reshape(v.shape), -1, axis)


WIDE = False


def mx_kscale(k):
    if not WIDE:
        return np.ones(k)
    levels = np.array([18, -18])
    if k % 512:
        return np.exp2(np.random.permutation(np.resize(levels, k // 32))).repeat(32)
    a = np.empty((k // 512, 16))
    for p in range(k // 512):
        a[p, :8] = np.random.permutation(np.resize(levels, 8))
        for g in range(8):
            far = levels[np.abs(levels - a[p, g]) >= 10]
            a[p, g + 8] = far[np.random.randint(len(far))]
    return np.exp2(a.ravel()).repeat(32)


def f64(x):
    return np.asarray(x).astype(np.float64)


def striped(idx):
    return np.tile(np.asarray(idx).reshape(-1, 16).T, (8, 1)).astype(np.uint16)


def unstriped(offs):
    return offs[:16].T.reshape(-1).astype(np.int64)

def planes(y):
    n, m = y.shape
    v = y.astype(np.float32).astype(ml_dtypes.bfloat16).astype(np.float64).reshape(n // 32, 32, m)
    top = np.abs(v).max(1)
    byte = np.clip(np.where(top > 0, np.frexp(top)[1] - 1 + 127 - 7, 1), 1, 254)
    codes = (v * np.exp2(127.0 - byte)[:, None, :]).reshape(n, m).astype(np.float32).astype(ml_dtypes.float8_e4m3fn).view(np.uint8)
    words = codes.reshape(n // 512, 128, 4, m).transpose(0, 1, 3, 2)
    return np.ascontiguousarray(words), np.ascontiguousarray(byte.astype(np.uint8).reshape(n // 512, 16, m))


def setup_inputs():
    n = np.random.standard_normal
    uni = np.random.uniform
    idx = np.random.permutation(2048)[:512]
    f_m = mx_kscale(512)
    return {
        "xT": (n((512, 2048)) / np.sqrt(512)).astype(np.float32),
        "sc": np.tile(n(2048), (128, 1)).astype(np.float32),
        "W": (n((512, 512)) / np.sqrt(512) * f_m[:, None]).astype(np.float32),
        "dz": (n((512, 512)) / f_m[:, None]).astype(np.float32),
        "offs": striped(idx),
    }


def reference(xT, sc, W, dz, offs):
    idx = unstriped(offs)
    x = f64(xT)[:, idx]
    s = f64(sc)[:1][:, idx]
    u = mxq(f64(W), 0, "e4m3").T @ mxq(f64(dz), 0, "e5m2")
    t = np.tanh(s)
    dx = t * u
    out_0 = np.zeros((512, 2048))
    out_0[:, idx] = dx
    q = x * u
    qt = q.T
    c = (qt).sum(-1, keepdims=True)
    cr = c.T
    out_1 = cr * (1.0 - np.square(t))
    return (out_0, out_1,) + planes(out_0)

@@ -1,0 +1,201 @@
+from contextlib import ExitStack
+
+import concourse.mybir as mybir
+from concourse.masks import make_identity
+
+F32 = mybir.dt.float32
+BF16 = mybir.dt.bfloat16
+I32 = mybir.dt.int32
+U32 = mybir.dt.uint32
+U16 = mybir.dt.uint16
+U8 = mybir.dt.uint8
+E4M3X4 = mybir.dt.float8_e4m3fn_x4
+E5M2X4 = mybir.dt.float8_e5m2_x4
+MULT = mybir.AluOpType.mult
+ADD = mybir.AluOpType.add
+COPY = mybir.ActivationFunctionType.Copy
+SQUARE = mybir.ActivationFunctionType.Square
+TANH = mybir.ActivationFunctionType.Tanh
+
+P = 128
+PACK = 4
+SLOTS = 512
+NODES = 2048
+FEATS = 512
+OUTS = 512
+CHUNK = 512
+W_VECTOR_COLS = 64
+
+FLOPS = 2 * OUTS * FEATS * SLOTS
+BYTES = 4 * (2 * FEATS * NODES + NODES + OUTS * FEATS + OUTS * SLOTS + SLOTS) + 2 * P * SLOTS // 16 + FEATS * NODES + FEATS * NODES // 32
+
+
+def tile_attend_gtopk_pl_kernel(tc, xT, sc, W, dz, offs, out_0, out_1, out_2, out_3):
+    nc = tc.nc
+    chunks = NODES // CHUNK
+    with ExitStack() as ctx:
+        sb = ctx.enter_context(tc.tile_pool(name="sb", bufs=1))
+        ps = ctx.enter_context(tc.psum_pool(name="ps", bufs=1))
+
+        offsets = sb.tile([P, SLOTS // 16], U16, name="offsets")
+        nc.sync.dma_start(offsets[:], offs)
+        score_cols = sb.tile([P, NODES // P], F32, name="score_cols")
+        nc.sync.dma_start(out=score_cols[:], in_=sc[0:1, :].rearrange("o (p k) -> (o p) k", p=P))
+        dz_raw = sb.tile([P, PACK, SLOTS], F32, name="dz_raw")
+        nc.sync.dma_start(out=dz_raw[:], in_=dz.rearrange("(p j) i -> p j i", j=PACK))
+        w_raw = sb.tile([P, PACK, FEATS], F32, name="w_raw")
+        nc.sync.dma_start(out=w_raw[:], in_=W.rearrange("(p j) d -> p j d", j=PACK))
+        x_rows = xT.rearrange("(p j) c -> p j c", j=PACK)
+        x_planes = []
+        for j in range(PACK):
+            plane = sb.tile([P, NODES], F32, name=f"x_plane{j}")
+            nc.sync.dma_start(out=plane[:], in_=x_rows[:, j, :])
+            x_planes.append(plane)
+
+        ident = sb.tile([P, P], F32, name="ident")
+        make_identity(nc, ident[:])
+        result_cols = sb.tile([P, P], F32, name="result_cols")
+        nc.scalar.activation(result_cols[:], ident[:], TANH, scale=0.0)
+
+        windows = []
+        for j in range(PACK - 1):
+            window = sb.tile([P, NODES], F32, name=f"window{j}")
+            nc.vector.memset(window[:].bitcast(I32), 0)
+            windows.append(window)
+
+        scores = sb.tile([P, NODES], F32, name="scores")
+        scores_by_col = scores[:].rearrange("p (n k) -> p n k", k=NODES // P)
+        for b in range(4):
+            spread = ps.tile([P, 4, P], F32, name=f"spread{b}", tag=f"acc{b}")
+            for k in range(4):
+                col = 4 * b + k
+                nc.tensor.transpose(spread[:, k, :], score_cols[:, col : col + 1].to_broadcast([P, P]), ident[:])
+            nc.scalar.activation(scores_by_col[:, :, 4 * b : 4 * b + 4], spread[:].rearrange("p k n -> p n k"), COPY)
+
+        dz_grouped = sb.tile([P, SLOTS, PACK], BF16, name="dz_grouped", align_bytes=64)
+        nc.vector.tensor_copy(
+            dz_grouped[:].rearrange("p (c i) j -> p c j i", i=4),
+            dz_raw[:].rearrange("p j (c i) -> p c j i", i=4),
+        )
+        dz_codes = sb.tile([P, SLOTS], U32, name="dz_codes", align_bytes=64)
+        dz_scales = sb.tile([P, SLOTS], U8, name="dz_scales", align_bytes=64)
+        nc.vector.quantize_mx(
+            out=dz_codes[:].bitcast(E5M2X4), scales=dz_scales[:], in_=dz_grouped[:].rearrange("p c j -> p (c j)")
+        )
+
+        kept = sb.tile([P, SLOTS], F32, name="kept")
+        nc.vector.tensor_copy(kept[:], scores[:].indirect(offsets[:]))
+        t_rows = sb.tile([P, SLOTS], F32, name="t_rows", tag="after_scatter")
+        nc.scalar.activation(t_rows[:], kept[:], TANH)
+
+        w_grouped = sb.tile([P, PACK, P, PACK], BF16, name="w_grouped", tag="late2", align_bytes=64)
+        for engine_copy, lo, hi in ((nc.vector.tensor_copy, 0, W_VECTOR_COLS), (nc.scalar.copy, W_VECTOR_COLS, P)):
+            engine_copy(
+                w_grouped[:, :, lo:hi, :].rearrange("p t m j -> p m j t"),
+                w_raw[:, :, PACK * lo : PACK * hi].rearrange("p j (m t) -> p m j t", t=PACK),
+            )
+        u_planes = []
+        for t in range(PACK):
+            w_codes = sb.tile([P, P], U32, name=f"w_codes{t}", align_bytes=64)
+            w_scales = sb.tile([P, P], U8, name=f"w_scales{t}", align_bytes=64)
+            nc.vector.quantize_mx(
+                out=w_codes[:].bitcast(E4M3X4), scales=w_scales[:], in_=w_grouped[:, t, :, :].rearrange("p m j -> p (m j)")
+            )
+            acc = ps.tile([P, SLOTS], F32, name=f"acc{t}", tag=f"acc{t}")
+            nc.tensor.matmul_mx(
+                out=acc[:],
+                lhsT=w_codes[:].bitcast(E4M3X4),
+                lhsT_scale=w_scales[:],
+                rhs=dz_codes[:].bitcast(E5M2X4),
+                rhs_scale=dz_scales[:],
+                start=True,
+                stop=True,
+            )
+            u = sb.tile([P, SLOTS], F32, name=f"u{t}")
+            nc.scalar.copy(u[:], acc[:])
+            u_planes.append(u)
+
+        window = sb.tile([P, NODES], F32, name="window3", tag="late2", align_bytes=64)
+        nc.vector.memset(window[:].bitcast(I32), 0)
+        windows.append(window)
+
+        t_cols = ps.tile([P, PACK, P], F32, name="t_cols", tag="bank_b")
+        for k in range(PACK):
+            nc.tensor.transpose(t_cols[:, k, :], t_rows[:, k * P : (k + 1) * P], ident[:])
+        t_sq = sb.tile([P, PACK], F32, name="t_sq")
+        nc.scalar.activation(t_sq[:], t_cols[:, :, 0], SQUARE)
+        slope = sb.tile([P, PACK], F32, name="slope")
+        nc.scalar.activation(slope[:], t_sq[:], COPY, bias=1.0, scale=-1.0)
+
+        out_rows = out_0.rearrange("(p j) c -> p j c", j=PACK)
+        pairs = [sb.tile([P, 2, CHUNK, 2], BF16, name=f"pairs{c}") for c in range(chunks)]
+
+        def round_plane(j, c):
+            nc.scalar.copy(pairs[c][:, j // 2, :, j % 2], windows[j][:, c * CHUNK : (c + 1) * CHUNK])
+
+        for j in range(PACK):
+            nc.vector.tensor_tensor(windows[j][:].indirect(offsets[:]), u_planes[j][:], t_rows[:], MULT)
+            nc.sync.dma_start(out=out_rows[:, j, :], in_=windows[j][:])
+            if j < PACK - 1:
+                for c in range(chunks):
+                    round_plane(j, c)
+
+        grouped = [sb.tile([P, CHUNK, PACK], BF16, name=f"grouped{c}", align_bytes=64) for c in range(chunks)]
+
+        def merge(c):
+            nc.scalar.copy(
+                grouped[c][:].rearrange("p c t -> p (c t)").bitcast(F32).rearrange("p (c h) -> p c h", h=2),
+                pairs[c][:].rearrange("p h c e -> p (h c e)").bitcast(F32).rearrange("p (h c) -> p c h", h=2),
+            )
+
+        round_plane(PACK - 1, 0)
+        for c in range(chunks):
+            if c + 1 < chunks:
+                round_plane(PACK - 1, c + 1)
+            merge(c)
+
+        q = sb.tile([P, PACK, SLOTS], F32, name="q", tag="after_scatter")
+        q_t = ps.tile([P, PACK, P], F32, name="q_t", tag="bank_a")
+        for j in range(PACK):
+            nc.vector.tensor_tensor(q[:, j, :], x_planes[j][:].indirect(offsets[:]), u_planes[j][:], MULT)
+            for k in range(PACK):
+                nc.tensor.matmul(
+                    q_t[:, k, :],
+                    q[:, j, k * P : (k + 1) * P],
+                    ident[:],
+                    start=(j == 0 and k == 0),
+                    stop=(j == PACK - 1 and k == PACK - 1),
+                    is_transpose=True,
+                )
+
+        words_out = out_2.rearrange("o p c l -> p (o c l)").bitcast(I32)
+        out_scales = sb.tile([P, NODES], U8, name="out_scales", align_bytes=64)
+
+        def quantise(c):
+            cols = slice(c * CHUNK, (c + 1) * CHUNK)
+            codes = sb.tile([P, CHUNK], U32, name=f"out_codes{c}", align_bytes=64)
+            nc.vector.quantize_mx(
+                out=codes[:].bitcast(E4M3X4), scales=out_scales[:, cols], in_=grouped[c][:].rearrange("p c t -> p (c t)")
+            )
+            nc.sync.dma_start(out=words_out[:, cols], in_=codes[:].bitcast(I32))
+
+        quantise(0)
+        sums = sb.tile([P, PACK], F32, name="sums")
+        nc.vector.tensor_reduce(sums[:], q_t[:], mybir.AxisListType.X, ADD)
+        quantise(1)
+        nc.vector.tensor_tensor(result_cols[:, 0:PACK], sums[:], slope[:], MULT)
+        result_t = ps.tile([P, P], F32, name="result_t", tag="bank_b")
+        nc.tensor.transpose(result_t[:], result_cols[:], ident[:])
+        result_rows = sb.tile([32, P], F32, name="result_rows")
+        nc.vector.tensor_copy(result_rows[:], result_t[0:32, :])
+        nc.sync.dma_start(out=out_1.rearrange("o (k n) -> (o k) n", k=PACK), in_=result_rows[0:PACK, :])
+        for c in range(2, chunks):
+            quantise(c)
+
+        scales_out = out_3.rearrange("o r c -> (o r) c").bitcast(I32)
+        for quadrant in range(4):
+            queue = nc.sync if quadrant % 2 == 0 else nc.scalar
+            queue.dma_start(
+                out=scales_out[4 * quadrant : 4 * quadrant + 4, :],
+                in_=out_scales[32 * quadrant : 32 * quadrant + 4, :].bitcast(I32),
+            )

@@ -1,7 +1,6 @@
 from contextlib import ExitStack
 
 import concourse.mybir as mybir
-from concourse.masks import make_identity
 
 F32 = mybir.dt.float32
 BF16 = mybir.dt.bfloat16
@@ -23,8 +22,9 @@ SLOTS = 512
 NODES = 2048
 FEATS = 512
 OUTS = 512
-CHUNK = 512
-W_VECTOR_COLS = 64
+SCALAR_CHUNKS = ((256, 768), (768, 1280), (1280, 1792), (1792, 2048))
+VECTOR_CHUNK = (0, 256)
+EARLY_SCALES = 1280
 
 FLOPS = 2 * OUTS * FEATS * SLOTS
 BYTES = 4 * (2 * FEATS * NODES + NODES + OUTS * FEATS + OUTS * SLOTS + SLOTS) + 2 * P * SLOTS // 16 + FEATS * NODES + FEATS * NODES // 32
@@ -32,14 +32,13 @@ BYTES = 4 * (2 * FEATS * NODES + NODES + OUTS * FEATS + OUTS * SLOTS + SLOTS) + 
 
 def tile_attend_gtopk_pl_kernel(tc, xT, sc, W, dz, offs, out_0, out_1, out_2, out_3):
     nc = tc.nc
-    chunks = NODES // CHUNK
     with ExitStack() as ctx:
         sb = ctx.enter_context(tc.tile_pool(name="sb", bufs=1))
         ps = ctx.enter_context(tc.psum_pool(name="ps", bufs=1))
 
         offsets = sb.tile([P, SLOTS // 16], U16, name="offsets")
         nc.sync.dma_start(offsets[:], offs)
-        score_cols = sb.tile([P, NODES // P], F32, name="score_cols")
+        score_cols = sb.tile([P, NODES // P], F32, name="score_cols", tag="late2", align_bytes=64)
         nc.sync.dma_start(out=score_cols[:], in_=sc[0:1, :].rearrange("o (p k) -> (o p) k", p=P))
         dz_raw = sb.tile([P, PACK, SLOTS], F32, name="dz_raw")
         nc.sync.dma_start(out=dz_raw[:], in_=dz.rearrange("(p j) i -> p j i", j=PACK))
@@ -52,16 +51,24 @@ def tile_attend_gtopk_pl_kernel(tc, xT, sc, W, dz, offs, out_0, out_1, out_2, ou
             nc.sync.dma_start(out=plane[:], in_=x_rows[:, j, :])
             x_planes.append(plane)
 
+        blank = sb.tile([P, P], F32, name="blank", tag="window1")
+        nc.gpsimd.memset(blank[:], 0.0)
         ident = sb.tile([P, P], F32, name="ident")
-        make_identity(nc, ident[:])
+        nc.gpsimd.affine_select(
+            out=ident[:],
+            in_=blank[:],
+            compare_op=mybir.AluOpType.not_equal,
+            fill=1.0,
+            base=0,
+            pattern=[[-1, P]],
+            channel_multiplier=1,
+        )
         result_cols = sb.tile([P, P], F32, name="result_cols")
         nc.scalar.activation(result_cols[:], ident[:], TANH, scale=0.0)
 
-        windows = []
-        for j in range(PACK - 1):
-            window = sb.tile([P, NODES], F32, name=f"window{j}")
-            nc.vector.memset(window[:].bitcast(I32), 0)
-            windows.append(window)
+        windows = [sb.tile([P, NODES], F32, name="window0"), sb.tile([P, NODES], F32, name="window1", tag="window1")]
+        nc.vector.memset(windows[0][:], 0.0)
+        nc.gpsimd.memset(windows[1][:], 0.0)
 
         scores = sb.tile([P, NODES], F32, name="scores")
         scores_by_col = scores[:].rearrange("p (n k) -> p n k", k=NODES // P)
@@ -77,7 +84,7 @@ def tile_attend_gtopk_pl_kernel(tc, xT, sc, W, dz, offs, out_0, out_1, out_2, ou
             dz_grouped[:].rearrange("p (c i) j -> p c j i", i=4),
             dz_raw[:].rearrange("p j (c i) -> p c j i", i=4),
         )
-        dz_codes = sb.tile([P, SLOTS], U32, name="dz_codes", align_bytes=64)
+        dz_codes = sb.tile([P, SLOTS], U32, name="dz_codes", tag="late3", align_bytes=64)
         dz_scales = sb.tile([P, SLOTS], U8, name="dz_scales", align_bytes=64)
         nc.vector.quantize_mx(
             out=dz_codes[:].bitcast(E5M2X4), scales=dz_scales[:], in_=dz_grouped[:].rearrange("p c j -> p (c j)")
@@ -88,18 +95,19 @@ def tile_attend_gtopk_pl_kernel(tc, xT, sc, W, dz, offs, out_0, out_1, out_2, ou
         t_rows = sb.tile([P, SLOTS], F32, name="t_rows", tag="after_scatter")
         nc.scalar.activation(t_rows[:], kept[:], TANH)
 
-        w_grouped = sb.tile([P, PACK, P, PACK], BF16, name="w_grouped", tag="late2", align_bytes=64)
-        for engine_copy, lo, hi in ((nc.vector.tensor_copy, 0, W_VECTOR_COLS), (nc.scalar.copy, W_VECTOR_COLS, P)):
-            engine_copy(
-                w_grouped[:, :, lo:hi, :].rearrange("p t m j -> p m j t"),
-                w_raw[:, :, PACK * lo : PACK * hi].rearrange("p j (m t) -> p m j t", t=PACK),
-            )
+        w_grouped = [
+            sb.tile([P, 2, P, PACK], BF16, name="w_grouped0", align_bytes=64),
+            sb.tile([P, 2, P, PACK], BF16, name="w_grouped1", tag="late2", align_bytes=64),
+        ]
+        w_dealt = w_raw[:].rearrange("p j (m t) -> p m j t", t=PACK)
+        for half, copy in enumerate((nc.vector.tensor_copy, nc.scalar.copy)):
+            copy(w_grouped[half][:].rearrange("p t m j -> p m j t"), w_dealt[:, :, :, 2 * half : 2 * half + 2])
         u_planes = []
         for t in range(PACK):
             w_codes = sb.tile([P, P], U32, name=f"w_codes{t}", align_bytes=64)
             w_scales = sb.tile([P, P], U8, name=f"w_scales{t}", align_bytes=64)
             nc.vector.quantize_mx(
-                out=w_codes[:].bitcast(E4M3X4), scales=w_scales[:], in_=w_grouped[:, t, :, :].rearrange("p m j -> p (m j)")
+                out=w_codes[:].bitcast(E4M3X4), scales=w_scales[:], in_=w_grouped[t // 2][:, t % 2, :, :].rearrange("p m j -> p (m j)")
             )
             acc = ps.tile([P, SLOTS], F32, name=f"acc{t}", tag=f"acc{t}")
             nc.tensor.matmul_mx(
@@ -115,9 +123,10 @@ def tile_attend_gtopk_pl_kernel(tc, xT, sc, W, dz, offs, out_0, out_1, out_2, ou
             nc.scalar.copy(u[:], acc[:])
             u_planes.append(u)
 
-        window = sb.tile([P, NODES], F32, name="window3", tag="late2", align_bytes=64)
-        nc.vector.memset(window[:].bitcast(I32), 0)
-        windows.append(window)
+        for j in (2, 3):
+            window = sb.tile([P, NODES], F32, name=f"window{j}", tag=f"late{j}", align_bytes=64)
+            nc.gpsimd.memset(window[:], 0.0)
+            windows.append(window)
 
         t_cols = ps.tile([P, PACK, P], F32, name="t_cols", tag="bank_b")
         for k in range(PACK):
@@ -128,31 +137,32 @@ def tile_attend_gtopk_pl_kernel(tc, xT, sc, W, dz, offs, out_0, out_1, out_2, ou
         nc.scalar.activation(slope[:], t_sq[:], COPY, bias=1.0, scale=-1.0)
 
         out_rows = out_0.rearrange("(p j) c -> p j c", j=PACK)
-        pairs = [sb.tile([P, 2, CHUNK, 2], BF16, name=f"pairs{c}") for c in range(chunks)]
+        chunks = SCALAR_CHUNKS + (VECTOR_CHUNK,)
+        rounded = [sb.tile([P, PACK, hi - lo], BF16, name=f"rounded{lo}") for lo, hi in chunks]
+        grouped = [sb.tile([P, hi - lo, PACK], BF16, name=f"grouped{lo}", align_bytes=64) for lo, hi in chunks]
 
-        def round_plane(j, c):
-            nc.scalar.copy(pairs[c][:, j // 2, :, j % 2], windows[j][:, c * CHUNK : (c + 1) * CHUNK])
+        def round_plane(copy, j, c):
+            lo, hi = chunks[c]
+            copy(rounded[c][:, j, :], windows[j][:, lo:hi])
+
+        def regroup(copy, c):
+            copy(
+                grouped[c][:].rearrange("p (c i) j -> p c j i", i=4),
+                rounded[c][:].rearrange("p j (c i) -> p c j i", i=4),
+            )
 
         for j in range(PACK):
             nc.vector.tensor_tensor(windows[j][:].indirect(offsets[:]), u_planes[j][:], t_rows[:], MULT)
             nc.sync.dma_start(out=out_rows[:, j, :], in_=windows[j][:])
             if j < PACK - 1:
-                for c in range(chunks):
-                    round_plane(j, c)
+                for c in range(len(chunks)):
+                    round_plane(nc.scalar.copy, j, c)
 
-        grouped = [sb.tile([P, CHUNK, PACK], BF16, name=f"grouped{c}", align_bytes=64) for c in range(chunks)]
-
-        def merge(c):
-            nc.scalar.copy(
-                grouped[c][:].rearrange("p c t -> p (c t)").bitcast(F32).rearrange("p (c h) -> p c h", h=2),
-                pairs[c][:].rearrange("p h c e -> p (h c e)").bitcast(F32).rearrange("p (h c) -> p c h", h=2),
-            )
-
-        round_plane(PACK - 1, 0)
-        for c in range(chunks):
-            if c + 1 < chunks:
-                round_plane(PACK - 1, c + 1)
-            merge(c)
+        round_plane(nc.scalar.copy, PACK - 1, 0)
+        for c in range(len(SCALAR_CHUNKS)):
+            if c + 1 < len(SCALAR_CHUNKS):
+                round_plane(nc.scalar.copy, PACK - 1, c + 1)
+            regroup(nc.scalar.copy, c)
 
         q = sb.tile([P, PACK, SLOTS], F32, name="q", tag="after_scatter")
         q_t = ps.tile([P, PACK, P], F32, name="q_t", tag="bank_a")
@@ -172,30 +182,37 @@ def tile_attend_gtopk_pl_kernel(tc, xT, sc, W, dz, offs, out_0, out_1, out_2, ou
         out_scales = sb.tile([P, NODES], U8, name="out_scales", align_bytes=64)
 
         def quantise(c):
-            cols = slice(c * CHUNK, (c + 1) * CHUNK)
-            codes = sb.tile([P, CHUNK], U32, name=f"out_codes{c}", align_bytes=64)
+            lo, hi = chunks[c]
+            codes = sb.tile([P, hi - lo], U32, name=f"out_codes{lo}", align_bytes=64)
             nc.vector.quantize_mx(
-                out=codes[:].bitcast(E4M3X4), scales=out_scales[:, cols], in_=grouped[c][:].rearrange("p c t -> p (c t)")
+                out=codes[:].bitcast(E4M3X4), scales=out_scales[:, lo:hi], in_=grouped[c][:].rearrange("p c t -> p (c t)")
             )
-            nc.sync.dma_start(out=words_out[:, cols], in_=codes[:].bitcast(I32))
+            nc.sync.dma_start(out=words_out[:, lo:hi], in_=codes[:].bitcast(I32))
 
+        scales_out = out_3.rearrange("o r c -> (o r) c").bitcast(I32)
+
+        def store_scales(lo, hi, queues):
+            for quadrant in range(4):
+                queues[quadrant % len(queues)].dma_start(
+                    out=scales_out[4 * quadrant : 4 * quadrant + 4, lo // 4 : hi // 4],
+                    in_=out_scales[32 * quadrant : 32 * quadrant + 4, lo:hi].bitcast(I32),
+                )
+
+        own = len(SCALAR_CHUNKS)
+        round_plane(nc.vector.tensor_copy, PACK - 1, own)
         quantise(0)
+        regroup(nc.vector.tensor_copy, own)
         sums = sb.tile([P, PACK], F32, name="sums")
         nc.vector.tensor_reduce(sums[:], q_t[:], mybir.AxisListType.X, ADD)
-        quantise(1)
-        nc.vector.tensor_tensor(result_cols[:, 0:PACK], sums[:], slope[:], MULT)
+        nc.gpsimd.tensor_tensor(result_cols[:, 0:PACK], sums[:], slope[:], MULT)
         result_t = ps.tile([P, P], F32, name="result_t", tag="bank_b")
         nc.tensor.transpose(result_t[:], result_cols[:], ident[:])
         result_rows = sb.tile([32, P], F32, name="result_rows")
-        nc.vector.tensor_copy(result_rows[:], result_t[0:32, :])
+        nc.scalar.copy(result_rows[:], result_t[0:32, :])
         nc.sync.dma_start(out=out_1.rearrange("o (k n) -> (o k) n", k=PACK), in_=result_rows[0:PACK, :])
-        for c in range(2, chunks):
+        quantise(own)
+        quantise(1)
+        store_scales(0, EARLY_SCALES, (nc.sync,))
+        for c in range(2, own):
             quantise(c)
-
-        scales_out = out_3.rearrange("o r c -> (o r) c").bitcast(I32)
-        for quadrant in range(4):
-            queue = nc.sync if quadrant % 2 == 0 else nc.scalar
-            queue.dma_start(
-                out=scales_out[4 * quadrant : 4 * quadrant + 4, :],
-                in_=out_scales[32 * quadrant : 32 * quadrant + 4, :].bitcast(I32),
-            )
+        store_scales(EARLY_SCALES, NODES, (nc.sync, nc.scalar))

@@ -22,9 +22,8 @@ SLOTS = 512
 NODES = 2048
 FEATS = 512
 OUTS = 512
-SCALAR_CHUNKS = ((256, 768), (768, 1280), (1280, 1792), (1792, 2048))
-VECTOR_CHUNK = (0, 256)
-EARLY_SCALES = 1280
+CHUNKS = ((0, 512), (512, 1024), (1024, 1536), (1536, 1792), (1792, 2048))
+STORES = {1: (0, 1024), 2: (1024, 1536), 4: (1536, 2048)}
 
 FLOPS = 2 * OUTS * FEATS * SLOTS
 BYTES = 4 * (2 * FEATS * NODES + NODES + OUTS * FEATS + OUTS * SLOTS + SLOTS) + 2 * P * SLOTS // 16 + FEATS * NODES + FEATS * NODES // 32
@@ -37,13 +36,13 @@ def tile_attend_gtopk_pl_kernel(tc, xT, sc, W, dz, offs, out_0, out_1, out_2, ou
         ps = ctx.enter_context(tc.psum_pool(name="ps", bufs=1))
 
         offsets = sb.tile([P, SLOTS // 16], U16, name="offsets")
-        nc.sync.dma_start(offsets[:], offs)
         score_cols = sb.tile([P, NODES // P], F32, name="score_cols", tag="late2", align_bytes=64)
         nc.sync.dma_start(out=score_cols[:], in_=sc[0:1, :].rearrange("o (p k) -> (o p) k", p=P))
         dz_raw = sb.tile([P, PACK, SLOTS], F32, name="dz_raw")
         nc.sync.dma_start(out=dz_raw[:], in_=dz.rearrange("(p j) i -> p j i", j=PACK))
         w_raw = sb.tile([P, PACK, FEATS], F32, name="w_raw")
         nc.sync.dma_start(out=w_raw[:], in_=W.rearrange("(p j) d -> p j d", j=PACK))
+        nc.sync.dma_start(offsets[:], offs)
         x_rows = xT.rearrange("(p j) c -> p j c", j=PACK)
         x_planes = []
         for j in range(PACK):
@@ -90,19 +89,17 @@ def tile_attend_gtopk_pl_kernel(tc, xT, sc, W, dz, offs, out_0, out_1, out_2, ou
             out=dz_codes[:].bitcast(E5M2X4), scales=dz_scales[:], in_=dz_grouped[:].rearrange("p c j -> p (c j)")
         )
 
-        kept = sb.tile([P, SLOTS], F32, name="kept")
-        nc.vector.tensor_copy(kept[:], scores[:].indirect(offsets[:]))
-        t_rows = sb.tile([P, SLOTS], F32, name="t_rows", tag="after_scatter")
-        nc.scalar.activation(t_rows[:], kept[:], TANH)
-
         w_grouped = [
-            sb.tile([P, 2, P, PACK], BF16, name="w_grouped0", align_bytes=64),
+            sb.tile([P, 2, P, PACK], BF16, name="w_grouped0", tag="kept", align_bytes=64),
             sb.tile([P, 2, P, PACK], BF16, name="w_grouped1", tag="late2", align_bytes=64),
         ]
         w_dealt = w_raw[:].rearrange("p j (m t) -> p m j t", t=PACK)
         for half, copy in enumerate((nc.vector.tensor_copy, nc.scalar.copy)):
             copy(w_grouped[half][:].rearrange("p t m j -> p m j t"), w_dealt[:, :, :, 2 * half : 2 * half + 2])
         u_planes = []
+        accs = []
+        whole = [(slice(0, SLOTS), slice(0, SLOTS // 16))]
+        halves = [(slice(h * SLOTS // 2, (h + 1) * SLOTS // 2), slice(h * SLOTS // 32, (h + 1) * SLOTS // 32)) for h in range(2)]
         for t in range(PACK):
             w_codes = sb.tile([P, P], U32, name=f"w_codes{t}", align_bytes=64)
             w_scales = sb.tile([P, P], U8, name=f"w_scales{t}", align_bytes=64)
@@ -119,8 +116,19 @@ def tile_attend_gtopk_pl_kernel(tc, xT, sc, W, dz, offs, out_0, out_1, out_2, ou
                 start=True,
                 stop=True,
             )
+            accs.append(acc)
+            if t == 1:
+                kept = sb.tile([P, SLOTS], F32, name="kept", tag="kept", align_bytes=64)
+                t_rows = sb.tile([P, SLOTS], F32, name="t_rows", tag="after_scatter")
+                u = sb.tile([P, SLOTS], F32, name="u0")
+                for slots, entries in halves:
+                    nc.vector.tensor_copy(kept[:, slots], scores[:].indirect(offsets[:, entries]))
+                    nc.scalar.copy(u[:, slots], accs[0][:, slots])
+                    nc.scalar.activation(t_rows[:, slots], kept[:, slots], TANH)
+                u_planes.append(u)
+        for t in range(1, PACK):
             u = sb.tile([P, SLOTS], F32, name=f"u{t}")
-            nc.scalar.copy(u[:], acc[:])
+            nc.scalar.copy(u[:], accs[t][:])
             u_planes.append(u)
 
         for j in (2, 3):
@@ -137,32 +145,32 @@ def tile_attend_gtopk_pl_kernel(tc, xT, sc, W, dz, offs, out_0, out_1, out_2, ou
         nc.scalar.activation(slope[:], t_sq[:], COPY, bias=1.0, scale=-1.0)
 
         out_rows = out_0.rearrange("(p j) c -> p j c", j=PACK)
-        chunks = SCALAR_CHUNKS + (VECTOR_CHUNK,)
-        rounded = [sb.tile([P, PACK, hi - lo], BF16, name=f"rounded{lo}") for lo, hi in chunks]
-        grouped = [sb.tile([P, hi - lo, PACK], BF16, name=f"grouped{lo}", align_bytes=64) for lo, hi in chunks]
+        pairs = [sb.tile([P, 2, hi - lo, 2], BF16, name=f"pairs{lo}") for lo, hi in CHUNKS]
+        grouped = [sb.tile([P, hi - lo, PACK], BF16, name=f"grouped{lo}", align_bytes=64) for lo, hi in CHUNKS]
 
-        def round_plane(copy, j, c):
-            lo, hi = chunks[c]
-            copy(rounded[c][:, j, :], windows[j][:, lo:hi])
+        def round_plane(j, c):
+            lo, hi = CHUNKS[c]
+            nc.scalar.copy(pairs[c][:, j // 2, :, j % 2], windows[j][:, lo:hi])
 
-        def regroup(copy, c):
-            copy(
-                grouped[c][:].rearrange("p (c i) j -> p c j i", i=4),
-                rounded[c][:].rearrange("p j (c i) -> p c j i", i=4),
+        def regroup(c):
+            nc.scalar.copy(
+                grouped[c][:].rearrange("p c t -> p (c t)").bitcast(F32).rearrange("p (c i h) -> p c h i", i=4, h=2),
+                pairs[c][:].rearrange("p h c e -> p (h c e)").bitcast(F32).rearrange("p (h c i) -> p c h i", h=2, i=4),
             )
 
         for j in range(PACK):
-            nc.vector.tensor_tensor(windows[j][:].indirect(offsets[:]), u_planes[j][:], t_rows[:], MULT)
+            for slots, entries in halves if j == 0 else whole:
+                nc.vector.tensor_tensor(windows[j][:].indirect(offsets[:, entries]), u_planes[j][:, slots], t_rows[:, slots], MULT)
             nc.sync.dma_start(out=out_rows[:, j, :], in_=windows[j][:])
             if j < PACK - 1:
-                for c in range(len(chunks)):
-                    round_plane(nc.scalar.copy, j, c)
+                for c in range(len(CHUNKS)):
+                    round_plane(j, c)
 
-        round_plane(nc.scalar.copy, PACK - 1, 0)
-        for c in range(len(SCALAR_CHUNKS)):
-            if c + 1 < len(SCALAR_CHUNKS):
-                round_plane(nc.scalar.copy, PACK - 1, c + 1)
-            regroup(nc.scalar.copy, c)
+        round_plane(PACK - 1, 0)
+        for c in range(len(CHUNKS)):
+            if c + 1 < len(CHUNKS):
+                round_plane(PACK - 1, c + 1)
+            regroup(c)
 
         q = sb.tile([P, PACK, SLOTS], F32, name="q", tag="after_scatter")
         q_t = ps.tile([P, PACK, P], F32, name="q_t", tag="bank_a")
@@ -181,27 +189,20 @@ def tile_attend_gtopk_pl_kernel(tc, xT, sc, W, dz, offs, out_0, out_1, out_2, ou
         words_out = out_2.rearrange("o p c l -> p (o c l)").bitcast(I32)
         out_scales = sb.tile([P, NODES], U8, name="out_scales", align_bytes=64)
 
+        out_codes = sb.tile([P, NODES], U32, name="out_codes", align_bytes=64)
+
         def quantise(c):
-            lo, hi = chunks[c]
-            codes = sb.tile([P, hi - lo], U32, name=f"out_codes{lo}", align_bytes=64)
+            lo, hi = CHUNKS[c]
             nc.vector.quantize_mx(
-                out=codes[:].bitcast(E4M3X4), scales=out_scales[:, lo:hi], in_=grouped[c][:].rearrange("p c t -> p (c t)")
+                out=out_codes[:, lo:hi].bitcast(E4M3X4),
+                scales=out_scales[:, lo:hi],
+                in_=grouped[c][:].rearrange("p c t -> p (c t)"),
             )
-            nc.sync.dma_start(out=words_out[:, lo:hi], in_=codes[:].bitcast(I32))
+            if c in STORES:
+                lo, hi = STORES[c]
+                nc.sync.dma_start(out=words_out[:, lo:hi], in_=out_codes[:, lo:hi].bitcast(I32))
 
-        scales_out = out_3.rearrange("o r c -> (o r) c").bitcast(I32)
-
-        def store_scales(lo, hi, queues):
-            for quadrant in range(4):
-                queues[quadrant % len(queues)].dma_start(
-                    out=scales_out[4 * quadrant : 4 * quadrant + 4, lo // 4 : hi // 4],
-                    in_=out_scales[32 * quadrant : 32 * quadrant + 4, lo:hi].bitcast(I32),
-                )
-
-        own = len(SCALAR_CHUNKS)
-        round_plane(nc.vector.tensor_copy, PACK - 1, own)
         quantise(0)
-        regroup(nc.vector.tensor_copy, own)
         sums = sb.tile([P, PACK], F32, name="sums")
         nc.vector.tensor_reduce(sums[:], q_t[:], mybir.AxisListType.X, ADD)
         nc.gpsimd.tensor_tensor(result_cols[:, 0:PACK], sums[:], slope[:], MULT)
@@ -210,9 +211,12 @@ def tile_attend_gtopk_pl_kernel(tc, xT, sc, W, dz, offs, out_0, out_1, out_2, ou
         result_rows = sb.tile([32, P], F32, name="result_rows")
         nc.scalar.copy(result_rows[:], result_t[0:32, :])
         nc.sync.dma_start(out=out_1.rearrange("o (k n) -> (o k) n", k=PACK), in_=result_rows[0:PACK, :])
-        quantise(own)
-        quantise(1)
-        store_scales(0, EARLY_SCALES, (nc.sync,))
-        for c in range(2, own):
+        for c in range(1, len(CHUNKS)):
             quantise(c)
-        store_scales(EARLY_SCALES, NODES, (nc.sync, nc.scalar))
+        scales_out = out_3.rearrange("o r c -> (o r) c").bitcast(I32)
+        for quadrant in range(4):
+            queue = nc.scalar if quadrant % 2 == 0 else nc.sync
+            queue.dma_start(
+                out=scales_out[4 * quadrant : 4 * quadrant + 4, :],
+                in_=out_scales[32 * quadrant : 32 * quadrant + 4, :].bitcast(I32),
+            )

@@ -14,7 +14,7 @@ MULT = mybir.AluOpType.mult
 ADD = mybir.AluOpType.add
 COPY = mybir.ActivationFunctionType.Copy
 SQUARE = mybir.ActivationFunctionType.Square
-TANH = mybir.ActivationFunctionType.Tanh
+SIGMOID = mybir.ActivationFunctionType.Sigmoid
 
 P = 128
 PACK = 4
@@ -23,7 +23,8 @@ NODES = 2048
 FEATS = 512
 OUTS = 512
 CHUNKS = ((0, 512), (512, 1024), (1024, 1536), (1536, 1792), (1792, 2048))
-STORES = {1: (0, 1024), 2: (1024, 1536), 4: (1536, 2048)}
+STORES = {1: (0, 1024), 3: (1024, 1792), 4: (1792, 2048)}
+BAND = 512
 
 FLOPS = 2 * OUTS * FEATS * SLOTS
 BYTES = 4 * (2 * FEATS * NODES + NODES + OUTS * FEATS + OUTS * SLOTS + SLOTS) + 2 * P * SLOTS // 16 + FEATS * NODES + FEATS * NODES // 32
@@ -36,13 +37,13 @@ def tile_attend_gtopk_pl_kernel(tc, xT, sc, W, dz, offs, out_0, out_1, out_2, ou
         ps = ctx.enter_context(tc.psum_pool(name="ps", bufs=1))
 
         offsets = sb.tile([P, SLOTS // 16], U16, name="offsets")
-        score_cols = sb.tile([P, NODES // P], F32, name="score_cols", tag="late2", align_bytes=64)
+        score_cols = sb.tile([P, NODES // P], F32, name="score_cols")
         nc.sync.dma_start(out=score_cols[:], in_=sc[0:1, :].rearrange("o (p k) -> (o p) k", p=P))
         dz_raw = sb.tile([P, PACK, SLOTS], F32, name="dz_raw")
         nc.sync.dma_start(out=dz_raw[:], in_=dz.rearrange("(p j) i -> p j i", j=PACK))
+        nc.sync.dma_start(offsets[:], offs)
         w_raw = sb.tile([P, PACK, FEATS], F32, name="w_raw")
         nc.sync.dma_start(out=w_raw[:], in_=W.rearrange("(p j) d -> p j d", j=PACK))
-        nc.sync.dma_start(offsets[:], offs)
         x_rows = xT.rearrange("(p j) c -> p j c", j=PACK)
         x_planes = []
         for j in range(PACK):
@@ -50,7 +51,7 @@ def tile_attend_gtopk_pl_kernel(tc, xT, sc, W, dz, offs, out_0, out_1, out_2, ou
             nc.sync.dma_start(out=plane[:], in_=x_rows[:, j, :])
             x_planes.append(plane)
 
-        blank = sb.tile([P, P], F32, name="blank", tag="window1")
+        blank = sb.tile([P, P], F32, name="blank")
         nc.gpsimd.memset(blank[:], 0.0)
         ident = sb.tile([P, P], F32, name="ident")
         nc.gpsimd.affine_select(
@@ -63,11 +64,11 @@ def tile_attend_gtopk_pl_kernel(tc, xT, sc, W, dz, offs, out_0, out_1, out_2, ou
             channel_multiplier=1,
         )
         result_cols = sb.tile([P, P], F32, name="result_cols")
-        nc.scalar.activation(result_cols[:], ident[:], TANH, scale=0.0)
+        nc.scalar.activation(result_cols[:], ident[:], SIGMOID, scale=0.0)
 
-        windows = [sb.tile([P, NODES], F32, name="window0"), sb.tile([P, NODES], F32, name="window1", tag="window1")]
-        nc.vector.memset(windows[0][:], 0.0)
-        nc.gpsimd.memset(windows[1][:], 0.0)
+        windows = [sb.tile([P, NODES], F32, name="window0"), sb.tile([P, NODES], F32, name="window1")]
+        for window in windows:
+            nc.vector.memset(window[:].bitcast(I32), 0)
 
         scores = sb.tile([P, NODES], F32, name="scores")
         scores_by_col = scores[:].rearrange("p (n k) -> p n k", k=NODES // P)
@@ -83,58 +84,53 @@ def tile_attend_gtopk_pl_kernel(tc, xT, sc, W, dz, offs, out_0, out_1, out_2, ou
             dz_grouped[:].rearrange("p (c i) j -> p c j i", i=4),
             dz_raw[:].rearrange("p j (c i) -> p c j i", i=4),
         )
-        dz_codes = sb.tile([P, SLOTS], U32, name="dz_codes", tag="late3", align_bytes=64)
+        dz_codes = sb.tile([P, SLOTS], U32, name="dz_codes", align_bytes=64)
         dz_scales = sb.tile([P, SLOTS], U8, name="dz_scales", align_bytes=64)
         nc.vector.quantize_mx(
             out=dz_codes[:].bitcast(E5M2X4), scales=dz_scales[:], in_=dz_grouped[:].rearrange("p c j -> p (c j)")
         )
 
-        w_grouped = [
-            sb.tile([P, 2, P, PACK], BF16, name="w_grouped0", tag="kept", align_bytes=64),
-            sb.tile([P, 2, P, PACK], BF16, name="w_grouped1", tag="late2", align_bytes=64),
-        ]
-        w_dealt = w_raw[:].rearrange("p j (m t) -> p m j t", t=PACK)
-        for half, copy in enumerate((nc.vector.tensor_copy, nc.scalar.copy)):
-            copy(w_grouped[half][:].rearrange("p t m j -> p m j t"), w_dealt[:, :, :, 2 * half : 2 * half + 2])
-        u_planes = []
-        accs = []
         whole = [(slice(0, SLOTS), slice(0, SLOTS // 16))]
         halves = [(slice(h * SLOTS // 2, (h + 1) * SLOTS // 2), slice(h * SLOTS // 32, (h + 1) * SLOTS // 32)) for h in range(2)]
-        for t in range(PACK):
-            w_codes = sb.tile([P, P], U32, name=f"w_codes{t}", align_bytes=64)
-            w_scales = sb.tile([P, P], U8, name=f"w_scales{t}", align_bytes=64)
+
+        gate = sb.tile([P, SLOTS], F32, name="gate", tag="before_u")
+        t_rows = sb.tile([P, SLOTS], F32, name="t_rows", tag="after_scatter")
+        for slots, entries in halves:
+            nc.scalar.activation(gate[:, slots], scores[:].indirect(offsets[:, entries]), SIGMOID, scale=2.0)
+            nc.scalar.activation(t_rows[:, slots], gate[:, slots], COPY, bias=-1.0, scale=2.0)
+
+        w_dealt = w_raw[:].rearrange("p j (m t) -> p m j t", t=PACK)
+        w_codes = sb.tile([P, FEATS], U32, name="w_codes", align_bytes=64)
+        w_scales = sb.tile([P, FEATS], U8, name="w_scales", align_bytes=64)
+        for half in range(2):
+            w_grouped = sb.tile([P, 2, P, PACK], BF16, name=f"w_grouped{half}", tag="w_grouped", align_bytes=64)
+            nc.vector.tensor_copy(w_grouped[:].rearrange("p t m j -> p m j t"), w_dealt[:, :, :, 2 * half : 2 * half + 2])
+            cols = slice(2 * half * P, 2 * (half + 1) * P)
             nc.vector.quantize_mx(
-                out=w_codes[:].bitcast(E4M3X4), scales=w_scales[:], in_=w_grouped[t // 2][:, t % 2, :, :].rearrange("p m j -> p (m j)")
+                out=w_codes[:, cols].bitcast(E4M3X4), scales=w_scales[:, cols], in_=w_grouped[:].rearrange("p t m j -> p (t m j)")
             )
+        u_all = sb.tile([P, PACK, SLOTS], F32, name="u_all", tag="before_u")
+        u_planes = []
+        for t in range(PACK):
             acc = ps.tile([P, SLOTS], F32, name=f"acc{t}", tag=f"acc{t}")
             nc.tensor.matmul_mx(
                 out=acc[:],
-                lhsT=w_codes[:].bitcast(E4M3X4),
-                lhsT_scale=w_scales[:],
+                lhsT=w_codes[:, t * P : (t + 1) * P].bitcast(E4M3X4),
+                lhsT_scale=w_scales[:, t * P : (t + 1) * P],
                 rhs=dz_codes[:].bitcast(E5M2X4),
                 rhs_scale=dz_scales[:],
                 start=True,
                 stop=True,
             )
-            accs.append(acc)
-            if t == 1:
-                kept = sb.tile([P, SLOTS], F32, name="kept", tag="kept", align_bytes=64)
-                t_rows = sb.tile([P, SLOTS], F32, name="t_rows", tag="after_scatter")
-                u = sb.tile([P, SLOTS], F32, name="u0")
-                for slots, entries in halves:
-                    nc.vector.tensor_copy(kept[:, slots], scores[:].indirect(offsets[:, entries]))
-                    nc.scalar.copy(u[:, slots], accs[0][:, slots])
-                    nc.scalar.activation(t_rows[:, slots], kept[:, slots], TANH)
-                u_planes.append(u)
-        for t in range(1, PACK):
-            u = sb.tile([P, SLOTS], F32, name=f"u{t}")
-            nc.scalar.copy(u[:], accs[t][:])
+            u = u_all[:, t, :]
+            for slots, entries in halves if t == 0 else whole:
+                nc.scalar.copy(u[:, slots], acc[:, slots])
             u_planes.append(u)
 
-        for j in (2, 3):
-            window = sb.tile([P, NODES], F32, name=f"window{j}", tag=f"late{j}", align_bytes=64)
-            nc.gpsimd.memset(window[:], 0.0)
-            windows.append(window)
+        window = sb.tile([P, NODES], F32, name="window2", tag="w_grouped", align_bytes=64)
+        nc.gpsimd.memset(window[:], 0.0)
+        windows.append(window)
+        windows.append(windows[0])
 
         t_cols = ps.tile([P, PACK, P], F32, name="t_cols", tag="bank_b")
         for k in range(PACK):
@@ -175,7 +171,7 @@ def tile_attend_gtopk_pl_kernel(tc, xT, sc, W, dz, offs, out_0, out_1, out_2, ou
         q = sb.tile([P, PACK, SLOTS], F32, name="q", tag="after_scatter")
         q_t = ps.tile([P, PACK, P], F32, name="q_t", tag="bank_a")
         for j in range(PACK):
-            nc.vector.tensor_tensor(q[:, j, :], x_planes[j][:].indirect(offsets[:]), u_planes[j][:], MULT)
+            nc.vector.tensor_tensor(q[:, j, :], x_planes[j][:].indirect(offsets[:]), u_planes[j], MULT)
             for k in range(PACK):
                 nc.tensor.matmul(
                     q_t[:, k, :],
@@ -187,7 +183,7 @@ def tile_attend_gtopk_pl_kernel(tc, xT, sc, W, dz, offs, out_0, out_1, out_2, ou
                 )
 
         words_out = out_2.rearrange("o p c l -> p (o c l)").bitcast(I32)
-        out_scales = sb.tile([P, NODES], U8, name="out_scales", align_bytes=64)
+        out_scales = sb.tile([P, BAND], U8, name="out_scales", align_bytes=64)
 
         out_codes = sb.tile([P, NODES], U32, name="out_codes", align_bytes=64)
 
@@ -195,7 +191,7 @@ def tile_attend_gtopk_pl_kernel(tc, xT, sc, W, dz, offs, out_0, out_1, out_2, ou
             lo, hi = CHUNKS[c]
             nc.vector.quantize_mx(
                 out=out_codes[:, lo:hi].bitcast(E4M3X4),
-                scales=out_scales[:, lo:hi],
+                scales=out_scales[4 * (lo // BAND) :, lo % BAND : lo % BAND + hi - lo],
                 in_=grouped[c][:].rearrange("p c t -> p (c t)"),
             )
             if c in STORES:
@@ -205,7 +201,7 @@ def tile_attend_gtopk_pl_kernel(tc, xT, sc, W, dz, offs, out_0, out_1, out_2, ou
         quantise(0)
         sums = sb.tile([P, PACK], F32, name="sums")
         nc.vector.tensor_reduce(sums[:], q_t[:], mybir.AxisListType.X, ADD)
-        nc.gpsimd.tensor_tensor(result_cols[:, 0:PACK], sums[:], slope[:], MULT)
+        nc.vector.tensor_tensor(result_cols[:, 0:PACK], sums[:], slope[:], MULT)
         result_t = ps.tile([P, P], F32, name="result_t", tag="bank_b")
         nc.tensor.transpose(result_t[:], result_cols[:], ident[:])
         result_rows = sb.tile([32, P], F32, name="result_rows")
@@ -213,10 +209,10 @@ def tile_attend_gtopk_pl_kernel(tc, xT, sc, W, dz, offs, out_0, out_1, out_2, ou
         nc.sync.dma_start(out=out_1.rearrange("o (k n) -> (o k) n", k=PACK), in_=result_rows[0:PACK, :])
         for c in range(1, len(CHUNKS)):
             quantise(c)
-        scales_out = out_3.rearrange("o r c -> (o r) c").bitcast(I32)
+        scales_out = out_3.bitcast(I32).rearrange("o r (b c) -> b (o r) c", b=NODES // BAND)
         for quadrant in range(4):
             queue = nc.scalar if quadrant % 2 == 0 else nc.sync
             queue.dma_start(
-                out=scales_out[4 * quadrant : 4 * quadrant + 4, :],
-                in_=out_scales[32 * quadrant : 32 * quadrant + 4, :].bitcast(I32),
+                out=scales_out[:, 4 * quadrant : 4 * quadrant + 4, :],
+                in_=out_scales[32 * quadrant : 32 * quadrant + 16, :].bitcast(I32),
             )

@@ -22,8 +22,8 @@ SLOTS = 512
 NODES = 2048
 FEATS = 512
 OUTS = 512
-CHUNKS = ((0, 512), (512, 1024), (1024, 1536), (1536, 1792), (1792, 2048))
-STORES = {1: (0, 1024), 3: (1024, 1792), 4: (1792, 2048)}
+CHUNKS = ((0, 512), (512, 1024), (1024, 1536), (1536, 2048))
+STORES = {1024: 0, 1792: 1024, 2048: 1792}
 BAND = 512
 
 FLOPS = 2 * OUTS * FEATS * SLOTS
@@ -148,8 +148,8 @@ def tile_attend_gtopk_pl_kernel(tc, xT, sc, W, dz, offs, out_0, out_1, out_2, ou
             lo, hi = CHUNKS[c]
             nc.scalar.copy(pairs[c][:, j // 2, :, j % 2], windows[j][:, lo:hi])
 
-        def regroup(c):
-            nc.scalar.copy(
+        def regroup(c, copy):
+            copy(
                 grouped[c][:].rearrange("p c t -> p (c t)").bitcast(F32).rearrange("p (c i h) -> p c h i", i=4, h=2),
                 pairs[c][:].rearrange("p h c e -> p (h c e)").bitcast(F32).rearrange("p (h c i) -> p c h i", h=2, i=4),
             )
@@ -163,10 +163,9 @@ def tile_attend_gtopk_pl_kernel(tc, xT, sc, W, dz, offs, out_0, out_1, out_2, ou
                     round_plane(j, c)
 
         round_plane(PACK - 1, 0)
-        for c in range(len(CHUNKS)):
-            if c + 1 < len(CHUNKS):
-                round_plane(PACK - 1, c + 1)
-            regroup(c)
+        for c in range(len(CHUNKS) - 1):
+            round_plane(PACK - 1, c + 1)
+            regroup(c, nc.scalar.copy)
 
         q = sb.tile([P, PACK, SLOTS], F32, name="q", tag="after_scatter")
         q_t = ps.tile([P, PACK, P], F32, name="q_t", tag="bank_a")
@@ -187,18 +186,18 @@ def tile_attend_gtopk_pl_kernel(tc, xT, sc, W, dz, offs, out_0, out_1, out_2, ou
 
         out_codes = sb.tile([P, NODES], U32, name="out_codes", align_bytes=64)
 
-        def quantise(c):
-            lo, hi = CHUNKS[c]
+        def quantise(lo, hi):
+            c = lo // BAND
             nc.vector.quantize_mx(
                 out=out_codes[:, lo:hi].bitcast(E4M3X4),
-                scales=out_scales[4 * (lo // BAND) :, lo % BAND : lo % BAND + hi - lo],
-                in_=grouped[c][:].rearrange("p c t -> p (c t)"),
+                scales=out_scales[4 * c :, lo % BAND : lo % BAND + hi - lo],
+                in_=grouped[c][:, lo % BAND : lo % BAND + hi - lo, :].rearrange("p c t -> p (c t)"),
             )
-            if c in STORES:
-                lo, hi = STORES[c]
+            if hi in STORES:
+                lo = STORES[hi]
                 nc.sync.dma_start(out=words_out[:, lo:hi], in_=out_codes[:, lo:hi].bitcast(I32))
 
-        quantise(0)
+        quantise(0, 512)
         sums = sb.tile([P, PACK], F32, name="sums")
         nc.vector.tensor_reduce(sums[:], q_t[:], mybir.AxisListType.X, ADD)
         nc.vector.tensor_tensor(result_cols[:, 0:PACK], sums[:], slope[:], MULT)
@@ -207,8 +206,11 @@ def tile_attend_gtopk_pl_kernel(tc, xT, sc, W, dz, offs, out_0, out_1, out_2, ou
         result_rows = sb.tile([32, P], F32, name="result_rows")
         nc.scalar.copy(result_rows[:], result_t[0:32, :])
         nc.sync.dma_start(out=out_1.rearrange("o (k n) -> (o k) n", k=PACK), in_=result_rows[0:PACK, :])
-        for c in range(1, len(CHUNKS)):
-            quantise(c)
+        quantise(512, 1024)
+        regroup(3, nc.vector.tensor_copy)
+        quantise(1024, 1536)
+        quantise(1536, 1792)
+        quantise(1792, 2048)
         scales_out = out_3.bitcast(I32).rearrange("o r (b c) -> b (o r) c", b=NODES // BAND)
         for quadrant in range(4):
             queue = nc.scalar if quadrant % 2 == 0 else nc.sync

@@ -11,7 +11,6 @@ U8 = mybir.dt.uint8
 E4M3X4 = mybir.dt.float8_e4m3fn_x4
 E5M2X4 = mybir.dt.float8_e5m2_x4
 MULT = mybir.AluOpType.mult
-ADD = mybir.AluOpType.add
 COPY = mybir.ActivationFunctionType.Copy
 SQUARE = mybir.ActivationFunctionType.Square
 SIGMOID = mybir.ActivationFunctionType.Sigmoid
@@ -22,9 +21,10 @@ SLOTS = 512
 NODES = 2048
 FEATS = 512
 OUTS = 512
-CHUNKS = ((0, 512), (512, 1024), (1024, 1536), (1536, 2048))
+CHUNKS = ((0, 512), (512, 1024), (1024, 1280), (1280, 2048))
 STORES = {1024: 0, 1792: 1024, 2048: 1792}
 BAND = 512
+HALF = SLOTS // 2
 
 FLOPS = 2 * OUTS * FEATS * SLOTS
 BYTES = 4 * (2 * FEATS * NODES + NODES + OUTS * FEATS + OUTS * SLOTS + SLOTS) + 2 * P * SLOTS // 16 + FEATS * NODES + FEATS * NODES // 32
@@ -39,11 +39,16 @@ def tile_attend_gtopk_pl_kernel(tc, xT, sc, W, dz, offs, out_0, out_1, out_2, ou
         offsets = sb.tile([P, SLOTS // 16], U16, name="offsets")
         score_cols = sb.tile([P, NODES // P], F32, name="score_cols")
         nc.sync.dma_start(out=score_cols[:], in_=sc[0:1, :].rearrange("o (p k) -> (o p) k", p=P))
-        dz_raw = sb.tile([P, PACK, SLOTS], F32, name="dz_raw")
-        nc.sync.dma_start(out=dz_raw[:], in_=dz.rearrange("(p j) i -> p j i", j=PACK))
-        nc.sync.dma_start(offsets[:], offs)
-        w_raw = sb.tile([P, PACK, FEATS], F32, name="w_raw")
-        nc.sync.dma_start(out=w_raw[:], in_=W.rearrange("(p j) d -> p j d", j=PACK))
+        w_rows = W.rearrange("(p j) d -> p j d", j=PACK)
+        dz_rows = dz.rearrange("(p j) i -> p j i", j=PACK)
+        w_raw, dz_raw = [], []
+        for h in range(2):
+            for name, rows, tiles in (("w", w_rows, w_raw), ("dz", dz_rows, dz_raw)):
+                raw = sb.tile([P, PACK, HALF], F32, name=f"{name}_raw{h}")
+                nc.sync.dma_start(out=raw[:], in_=rows[:, :, h * HALF : (h + 1) * HALF])
+                tiles.append(raw)
+            if h == 0:
+                nc.sync.dma_start(offsets[:], offs)
         x_rows = xT.rearrange("(p j) c -> p j c", j=PACK)
         x_planes = []
         for j in range(PACK):
@@ -51,7 +56,7 @@ def tile_attend_gtopk_pl_kernel(tc, xT, sc, W, dz, offs, out_0, out_1, out_2, ou
             nc.sync.dma_start(out=plane[:], in_=x_rows[:, j, :])
             x_planes.append(plane)
 
-        blank = sb.tile([P, P], F32, name="blank")
+        blank = sb.tile([P, P], F32, name="blank", tag="window1")
         nc.gpsimd.memset(blank[:], 0.0)
         ident = sb.tile([P, P], F32, name="ident")
         nc.gpsimd.affine_select(
@@ -66,9 +71,10 @@ def tile_attend_gtopk_pl_kernel(tc, xT, sc, W, dz, offs, out_0, out_1, out_2, ou
         result_cols = sb.tile([P, P], F32, name="result_cols")
         nc.scalar.activation(result_cols[:], ident[:], SIGMOID, scale=0.0)
 
-        windows = [sb.tile([P, NODES], F32, name="window0"), sb.tile([P, NODES], F32, name="window1")]
-        for window in windows:
-            nc.vector.memset(window[:].bitcast(I32), 0)
+        windows = [sb.tile([P, NODES], F32, name="window0"), None]
+        nc.vector.memset(windows[0][:].bitcast(I32), 0)
+        windows[1] = sb.tile([P, NODES], F32, name="window1", tag="window1")
+        nc.gpsimd.memset(windows[1][:].bitcast(I32), 0)
 
         scores = sb.tile([P, NODES], F32, name="scores")
         scores_by_col = scores[:].rearrange("p (n k) -> p n k", k=NODES // P)
@@ -79,40 +85,51 @@ def tile_attend_gtopk_pl_kernel(tc, xT, sc, W, dz, offs, out_0, out_1, out_2, ou
                 nc.tensor.transpose(spread[:, k, :], score_cols[:, col : col + 1].to_broadcast([P, P]), ident[:])
             nc.scalar.activation(scores_by_col[:, :, 4 * b : 4 * b + 4], spread[:].rearrange("p k n -> p n k"), COPY)
 
-        dz_grouped = sb.tile([P, SLOTS, PACK], BF16, name="dz_grouped", align_bytes=64)
-        nc.vector.tensor_copy(
-            dz_grouped[:].rearrange("p (c i) j -> p c j i", i=4),
-            dz_raw[:].rearrange("p j (c i) -> p c j i", i=4),
-        )
-        dz_codes = sb.tile([P, SLOTS], U32, name="dz_codes", align_bytes=64)
-        dz_scales = sb.tile([P, SLOTS], U8, name="dz_scales", align_bytes=64)
-        nc.vector.quantize_mx(
-            out=dz_codes[:].bitcast(E5M2X4), scales=dz_scales[:], in_=dz_grouped[:].rearrange("p c j -> p (c j)")
-        )
-
         whole = [(slice(0, SLOTS), slice(0, SLOTS // 16))]
-        halves = [(slice(h * SLOTS // 2, (h + 1) * SLOTS // 2), slice(h * SLOTS // 32, (h + 1) * SLOTS // 32)) for h in range(2)]
+        halves = [(slice(h * HALF, (h + 1) * HALF), slice(h * HALF // 16, (h + 1) * HALF // 16)) for h in range(2)]
 
-        gate = sb.tile([P, SLOTS], F32, name="gate", tag="before_u")
-        t_rows = sb.tile([P, SLOTS], F32, name="t_rows", tag="after_scatter")
-        for slots, entries in halves:
-            nc.scalar.activation(gate[:, slots], scores[:].indirect(offsets[:, entries]), SIGMOID, scale=2.0)
-            nc.scalar.activation(t_rows[:, slots], gate[:, slots], COPY, bias=-1.0, scale=2.0)
-
-        w_dealt = w_raw[:].rearrange("p j (m t) -> p m j t", t=PACK)
+        w_grouped = sb.tile([P, PACK, P, PACK], BF16, name="w_grouped", tag="vector_order", align_bytes=64)
         w_codes = sb.tile([P, FEATS], U32, name="w_codes", align_bytes=64)
         w_scales = sb.tile([P, FEATS], U8, name="w_scales", align_bytes=64)
-        for half in range(2):
-            w_grouped = sb.tile([P, 2, P, PACK], BF16, name=f"w_grouped{half}", tag="w_grouped", align_bytes=64)
-            nc.vector.tensor_copy(w_grouped[:].rearrange("p t m j -> p m j t"), w_dealt[:, :, :, 2 * half : 2 * half + 2])
-            cols = slice(2 * half * P, 2 * (half + 1) * P)
-            nc.vector.quantize_mx(
-                out=w_codes[:, cols].bitcast(E4M3X4), scales=w_scales[:, cols], in_=w_grouped[:].rearrange("p t m j -> p (t m j)")
+        dz_codes = sb.tile([P, SLOTS], U32, name="dz_codes", tag="before_window2", align_bytes=64)
+        dz_scales = sb.tile([P, SLOTS], U8, name="dz_scales", align_bytes=64)
+        nc.vector.memset(dz_codes[:, HALF:SLOTS].bitcast(I32), 0)
+        nc.vector.memset(dz_scales[:, HALF:SLOTS].bitcast(I32), 0)
+        t_rows = sb.tile([P, SLOTS], F32, name="t_rows", tag="after_scatter")
+
+        def regroup_w(h):
+            nc.vector.tensor_copy(
+                w_grouped[:, :, h * P // 2 : (h + 1) * P // 2, :].rearrange("p t m j -> p m j t"),
+                w_raw[h][:].rearrange("p j (m t) -> p m j t", t=PACK),
             )
-        u_all = sb.tile([P, PACK, SLOTS], F32, name="u_all", tag="before_u")
-        u_planes = []
-        for t in range(PACK):
-            acc = ps.tile([P, SLOTS], F32, name=f"acc{t}", tag=f"acc{t}")
+
+        def quantise_w(lo, hi):
+            cols = slice(lo * P, hi * P)
+            nc.vector.quantize_mx(
+                out=w_codes[:, cols].bitcast(E4M3X4),
+                scales=w_scales[:, cols],
+                in_=w_grouped[:, lo:hi, :, :].rearrange("p t m j -> p (t m j)"),
+            )
+
+        def quantise_dz(h, tag):
+            dz_grouped = sb.tile([P, HALF, PACK], BF16, name=f"dz_grouped{h}", tag=tag, align_bytes=64)
+            nc.vector.tensor_copy(
+                dz_grouped[:].rearrange("p (c i) j -> p c j i", i=4),
+                dz_raw[h][:].rearrange("p j (c i) -> p c j i", i=4),
+            )
+            cols = slice(h * HALF, (h + 1) * HALF)
+            nc.vector.quantize_mx(
+                out=dz_codes[:, cols].bitcast(E5M2X4), scales=dz_scales[:, cols], in_=dz_grouped[:].rearrange("p c j -> p (c j)")
+            )
+
+        def tanh_of_scores(h, tag):
+            slots, entries = halves[h]
+            gate = sb.tile([P, HALF], F32, name=f"gate{h}", tag=tag, align_bytes=64)
+            nc.scalar.activation(gate[:], scores[:].indirect(offsets[:, entries]), SIGMOID, scale=2.0)
+            nc.scalar.activation(t_rows[:, slots], gate[:], COPY, bias=-1.0, scale=2.0)
+
+        def multiply(t, tag):
+            acc = ps.tile([P, SLOTS], F32, name=f"acc{t}_{tag}", tag=tag)
             nc.tensor.matmul_mx(
                 out=acc[:],
                 lhsT=w_codes[:, t * P : (t + 1) * P].bitcast(E4M3X4),
@@ -122,12 +139,29 @@ def tile_attend_gtopk_pl_kernel(tc, xT, sc, W, dz, offs, out_0, out_1, out_2, ou
                 start=True,
                 stop=True,
             )
-            u = u_all[:, t, :]
-            for slots, entries in halves if t == 0 else whole:
-                nc.scalar.copy(u[:, slots], acc[:, slots])
-            u_planes.append(u)
+            return acc
 
-        window = sb.tile([P, NODES], F32, name="window2", tag="w_grouped", align_bytes=64)
+        tanh_of_scores(0, "before_u0")
+        regroup_w(0)
+        quantise_dz(0, "dz_grouped0")
+        regroup_w(1)
+        quantise_w(0, 1)
+        early = multiply(0, "acc3")
+        quantise_w(1, 2)
+        quantise_w(2, 4)
+        u_first = sb.tile([P, SLOTS], F32, name="u_first", tag="before_u0", align_bytes=64)
+        nc.scalar.copy(u_first[:, 0:HALF], early[:, 0:HALF])
+        quantise_dz(1, "vector_order")
+        tanh_of_scores(1, "before_u_rest")
+        accs = [multiply(t, f"acc{t}" if t < 3 else "acc4") for t in range(PACK)]
+        nc.scalar.copy(u_first[:, HALF:SLOTS], accs[0][:, HALF:SLOTS])
+        u_rest = sb.tile([P, PACK - 1, SLOTS], F32, name="u_rest", tag="before_u_rest", align_bytes=64)
+        u_planes = [u_first[:]]
+        for t in range(1, PACK):
+            nc.scalar.copy(u_rest[:, t - 1, :], accs[t][:])
+            u_planes.append(u_rest[:, t - 1, :])
+
+        window = sb.tile([P, NODES], F32, name="window2", tag="before_window2", align_bytes=64)
         nc.gpsimd.memset(window[:], 0.0)
         windows.append(window)
         windows.append(windows[0])
@@ -163,9 +197,12 @@ def tile_attend_gtopk_pl_kernel(tc, xT, sc, W, dz, offs, out_0, out_1, out_2, ou
                     round_plane(j, c)
 
         round_plane(PACK - 1, 0)
-        for c in range(len(CHUNKS) - 1):
-            round_plane(PACK - 1, c + 1)
-            regroup(c, nc.scalar.copy)
+        round_plane(PACK - 1, 1)
+        regroup(0, nc.scalar.copy)
+        round_plane(PACK - 1, 3)
+        round_plane(PACK - 1, 2)
+        regroup(1, nc.scalar.copy)
+        regroup(2, nc.scalar.copy)
 
         q = sb.tile([P, PACK, SLOTS], F32, name="q", tag="after_scatter")
         q_t = ps.tile([P, PACK, P], F32, name="q_t", tag="bank_a")
@@ -187,28 +224,30 @@ def tile_attend_gtopk_pl_kernel(tc, xT, sc, W, dz, offs, out_0, out_1, out_2, ou
         out_codes = sb.tile([P, NODES], U32, name="out_codes", align_bytes=64)
 
         def quantise(lo, hi):
-            c = lo // BAND
+            c = max(k for k, chunk in enumerate(CHUNKS) if chunk[0] <= lo)
+            first = CHUNKS[c][0]
             nc.vector.quantize_mx(
                 out=out_codes[:, lo:hi].bitcast(E4M3X4),
-                scales=out_scales[4 * c :, lo % BAND : lo % BAND + hi - lo],
-                in_=grouped[c][:, lo % BAND : lo % BAND + hi - lo, :].rearrange("p c t -> p (c t)"),
+                scales=out_scales[4 * (lo // BAND) :, lo % BAND : lo % BAND + hi - lo],
+                in_=grouped[c][:, lo - first : hi - first, :].rearrange("p c t -> p (c t)"),
             )
             if hi in STORES:
                 lo = STORES[hi]
                 nc.sync.dma_start(out=words_out[:, lo:hi], in_=out_codes[:, lo:hi].bitcast(I32))
 
-        quantise(0, 512)
-        sums = sb.tile([P, PACK], F32, name="sums")
-        nc.vector.tensor_reduce(sums[:], q_t[:], mybir.AxisListType.X, ADD)
-        nc.vector.tensor_tensor(result_cols[:, 0:PACK], sums[:], slope[:], MULT)
+        scaled = sb.tile([P, PACK, P], F32, name="scaled")
+        for k in range(PACK):
+            nc.scalar.activation(scaled[:, k, :], q_t[:, k, :], COPY, scale=slope[:, k : k + 1], accum_out=result_cols[:, k : k + 1])
         result_t = ps.tile([P, P], F32, name="result_t", tag="bank_b")
         nc.tensor.transpose(result_t[:], result_cols[:], ident[:])
         result_rows = sb.tile([32, P], F32, name="result_rows")
         nc.scalar.copy(result_rows[:], result_t[0:32, :])
         nc.sync.dma_start(out=out_1.rearrange("o (k n) -> (o k) n", k=PACK), in_=result_rows[0:PACK, :])
-        quantise(512, 1024)
+        quantise(0, 512)
         regroup(3, nc.vector.tensor_copy)
-        quantise(1024, 1536)
+        quantise(512, 1024)
+        quantise(1024, 1280)
+        quantise(1280, 1536)
         quantise(1536, 1792)
         quantise(1792, 2048)
         scales_out = out_3.bitcast(I32).rearrange("o r (b c) -> b (o r) c", b=NODES // BAND)

@@ -184,8 +184,8 @@ def tile_attend_gtopk_pl_kernel(tc, xT, sc, W, dz, offs, out_0, out_1, out_2, ou
 
         def regroup(c, copy):
             copy(
-                grouped[c][:].rearrange("p c t -> p (c t)").bitcast(F32).rearrange("p (c i h) -> p c h i", i=4, h=2),
-                pairs[c][:].rearrange("p h c e -> p (h c e)").bitcast(F32).rearrange("p (h c i) -> p c h i", h=2, i=4),
+                grouped[c][:].rearrange("p c t -> p (c t)").bitcast(F32).rearrange("p (c h) -> p c h", h=2),
+                pairs[c][:].rearrange("p h c e -> p (h c e)").bitcast(F32).rearrange("p (h c) -> p c h", h=2),
             )
 
         for j in range(PACK):

@@ -22,7 +22,7 @@ NODES = 2048
 FEATS = 512
 OUTS = 512
 CHUNKS = ((0, 512), (512, 1024), (1024, 1280), (1280, 2048))
-STORES = {1024: 0, 1792: 1024, 2048: 1792}
+STORES = {1024: 0, 1536: 1024, 2048: 1536}
 BAND = 512
 HALF = SLOTS // 2
 
@@ -43,7 +43,7 @@ def tile_attend_gtopk_pl_kernel(tc, xT, sc, W, dz, offs, out_0, out_1, out_2, ou
         dz_rows = dz.rearrange("(p j) i -> p j i", j=PACK)
         w_raw, dz_raw = [], []
         for h in range(2):
-            for name, rows, tiles in (("w", w_rows, w_raw), ("dz", dz_rows, dz_raw)):
+            for name, rows, tiles in (("dz", dz_rows, dz_raw), ("w", w_rows, w_raw)) if h == 0 else (("w", w_rows, w_raw), ("dz", dz_rows, dz_raw)):
                 raw = sb.tile([P, PACK, HALF], F32, name=f"{name}_raw{h}")
                 nc.sync.dma_start(out=raw[:], in_=rows[:, :, h * HALF : (h + 1) * HALF])
                 tiles.append(raw)
@@ -142,8 +142,8 @@ def tile_attend_gtopk_pl_kernel(tc, xT, sc, W, dz, offs, out_0, out_1, out_2, ou
             return acc
 
         tanh_of_scores(0, "before_u0")
-        regroup_w(0)
         quantise_dz(0, "dz_grouped0")
+        regroup_w(0)
         regroup_w(1)
         quantise_w(0, 1)
         early = multiply(0, "acc3")

@@ -88,14 +88,14 @@ def tile_attend_gtopk_pl_kernel(tc, xT, sc, W, dz, offs, out_0, out_1, out_2, ou
         whole = [(slice(0, SLOTS), slice(0, SLOTS // 16))]
         halves = [(slice(h * HALF, (h + 1) * HALF), slice(h * HALF // 16, (h + 1) * HALF // 16)) for h in range(2)]
 
-        w_grouped = sb.tile([P, PACK, P, PACK], BF16, name="w_grouped", tag="vector_order", align_bytes=64)
+        w_grouped = sb.tile([P, PACK, P, PACK], BF16, name="w_grouped", align_bytes=64)
         w_codes = sb.tile([P, FEATS], U32, name="w_codes", align_bytes=64)
         w_scales = sb.tile([P, FEATS], U8, name="w_scales", align_bytes=64)
         dz_codes = sb.tile([P, SLOTS], U32, name="dz_codes", tag="before_window2", align_bytes=64)
         dz_scales = sb.tile([P, SLOTS], U8, name="dz_scales", align_bytes=64)
         nc.vector.memset(dz_codes[:, HALF:SLOTS].bitcast(I32), 0)
         nc.vector.memset(dz_scales[:, HALF:SLOTS].bitcast(I32), 0)
-        t_rows = sb.tile([P, SLOTS], F32, name="t_rows", tag="after_scatter")
+        t_rows = sb.tile([P, SLOTS], F32, name="t_rows")
 
         def regroup_w(h):
             nc.vector.tensor_copy(
@@ -151,7 +151,7 @@ def tile_attend_gtopk_pl_kernel(tc, xT, sc, W, dz, offs, out_0, out_1, out_2, ou
         quantise_w(2, 4)
         u_first = sb.tile([P, SLOTS], F32, name="u_first", tag="before_u0", align_bytes=64)
         nc.scalar.copy(u_first[:, 0:HALF], early[:, 0:HALF])
-        quantise_dz(1, "vector_order")
+        quantise_dz(1, "dz_grouped1")
         tanh_of_scores(1, "before_u_rest")
         accs = [multiply(t, f"acc{t}" if t < 3 else "acc4") for t in range(PACK)]
         nc.scalar.copy(u_first[:, HALF:SLOTS], accs[0][:, HALF:SLOTS])
@@ -204,7 +204,7 @@ def tile_attend_gtopk_pl_kernel(tc, xT, sc, W, dz, offs, out_0, out_1, out_2, ou
         regroup(1, nc.scalar.copy)
         regroup(2, nc.scalar.copy)
 
-        q = sb.tile([P, PACK, SLOTS], F32, name="q", tag="after_scatter")
+        q = sb.tile([P, PACK, SLOTS], F32, name="q", tag="window1")
         q_t = ps.tile([P, PACK, P], F32, name="q_t", tag="bank_a")
         for j in range(PACK):
             nc.vector.tensor_tensor(q[:, j, :], x_planes[j][:].indirect(offsets[:]), u_planes[j], MULT)
@@ -242,10 +242,11 @@ def tile_attend_gtopk_pl_kernel(tc, xT, sc, W, dz, offs, out_0, out_1, out_2, ou
         nc.tensor.transpose(result_t[:], result_cols[:], ident[:])
         result_rows = sb.tile([32, P], F32, name="result_rows")
         nc.scalar.copy(result_rows[:], result_t[0:32, :])
-        nc.sync.dma_start(out=out_1.rearrange("o (k n) -> (o k) n", k=PACK), in_=result_rows[0:PACK, :])
+        nc.scalar.dma_start(out=out_1.rearrange("o (k n) -> (o k) n", k=PACK), in_=result_rows[0:PACK, :])
         quantise(0, 512)
         regroup(3, nc.vector.tensor_copy)
-        quantise(512, 1024)
+        quantise(512, 768)
+        quantise(768, 1024)
         quantise(1024, 1280)
         quantise(1280, 1536)
         quantise(1536, 1792)

@@ -21,7 +21,7 @@ SLOTS = 512
 NODES = 2048
 FEATS = 512
 OUTS = 512
-CHUNKS = ((0, 512), (512, 1024), (1024, 1280), (1280, 2048))
+CHUNKS = ((0, 512), (512, 1024), (1024, 1792), (1792, 2048))
 STORES = {1024: 0, 1536: 1024, 2048: 1536}
 BAND = 512
 HALF = SLOTS // 2
@@ -76,7 +76,7 @@ def tile_attend_gtopk_pl_kernel(tc, xT, sc, W, dz, offs, out_0, out_1, out_2, ou
         windows[1] = sb.tile([P, NODES], F32, name="window1", tag="window1")
         nc.gpsimd.memset(windows[1][:].bitcast(I32), 0)
 
-        scores = sb.tile([P, NODES], F32, name="scores")
+        scores = sb.tile([P, NODES], F32, name="scores", tag="before_u0", align_bytes=64)
         scores_by_col = scores[:].rearrange("p (n k) -> p n k", k=NODES // P)
         for b in range(4):
             spread = ps.tile([P, 4, P], F32, name=f"spread{b}", tag=f"acc{b}")
@@ -97,10 +97,10 @@ def tile_attend_gtopk_pl_kernel(tc, xT, sc, W, dz, offs, out_0, out_1, out_2, ou
         nc.vector.memset(dz_scales[:, HALF:SLOTS].bitcast(I32), 0)
         t_rows = sb.tile([P, SLOTS], F32, name="t_rows")
 
-        def regroup_w(h):
+        def regroup_w(h, lo, hi):
             nc.vector.tensor_copy(
-                w_grouped[:, :, h * P // 2 : (h + 1) * P // 2, :].rearrange("p t m j -> p m j t"),
-                w_raw[h][:].rearrange("p j (m t) -> p m j t", t=PACK),
+                w_grouped[:, lo:hi, h * P // 2 : (h + 1) * P // 2, :].rearrange("p t m j -> p m j t"),
+                w_raw[h][:].rearrange("p j (m t) -> p m j t", t=PACK)[:, :, :, lo:hi],
             )
 
         def quantise_w(lo, hi):
@@ -111,12 +111,15 @@ def tile_attend_gtopk_pl_kernel(tc, xT, sc, W, dz, offs, out_0, out_1, out_2, ou
                 in_=w_grouped[:, lo:hi, :, :].rearrange("p t m j -> p (t m j)"),
             )
 
-        def quantise_dz(h, tag):
-            dz_grouped = sb.tile([P, HALF, PACK], BF16, name=f"dz_grouped{h}", tag=tag, align_bytes=64)
+        def regroup_dz(h):
+            dz_grouped = sb.tile([P, HALF, PACK], BF16, name=f"dz_grouped{h}", align_bytes=64)
             nc.vector.tensor_copy(
                 dz_grouped[:].rearrange("p (c i) j -> p c j i", i=4),
                 dz_raw[h][:].rearrange("p j (c i) -> p c j i", i=4),
             )
+            return dz_grouped
+
+        def quantise_dz(h, dz_grouped):
             cols = slice(h * HALF, (h + 1) * HALF)
             nc.vector.quantize_mx(
                 out=dz_codes[:, cols].bitcast(E5M2X4), scales=dz_scales[:, cols], in_=dz_grouped[:].rearrange("p c j -> p (c j)")
@@ -141,17 +144,19 @@ def tile_attend_gtopk_pl_kernel(tc, xT, sc, W, dz, offs, out_0, out_1, out_2, ou
             )
             return acc
 
-        tanh_of_scores(0, "before_u0")
-        quantise_dz(0, "dz_grouped0")
-        regroup_w(0)
-        regroup_w(1)
+        tanh_of_scores(0, "gate0")
+        quantise_dz(0, regroup_dz(0))
+        regroup_w(0, 0, PACK)
+        regroup_w(1, 0, 2)
+        regroup_w(1, 2, PACK)
         quantise_w(0, 1)
         early = multiply(0, "acc3")
         quantise_w(1, 2)
+        dz_second = regroup_dz(1)
         quantise_w(2, 4)
         u_first = sb.tile([P, SLOTS], F32, name="u_first", tag="before_u0", align_bytes=64)
         nc.scalar.copy(u_first[:, 0:HALF], early[:, 0:HALF])
-        quantise_dz(1, "dz_grouped1")
+        quantise_dz(1, dz_second)
         tanh_of_scores(1, "before_u_rest")
         accs = [multiply(t, f"acc{t}" if t < 3 else "acc4") for t in range(PACK)]
         nc.scalar.copy(u_first[:, HALF:SLOTS], accs[0][:, HALF:SLOTS])
@@ -199,10 +204,10 @@ def tile_attend_gtopk_pl_kernel(tc, xT, sc, W, dz, offs, out_0, out_1, out_2, ou
         round_plane(PACK - 1, 0)
         round_plane(PACK - 1, 1)
         regroup(0, nc.scalar.copy)
-        round_plane(PACK - 1, 3)
         round_plane(PACK - 1, 2)
+        round_plane(PACK - 1, 3)
         regroup(1, nc.scalar.copy)
-        regroup(2, nc.scalar.copy)
+        regroup(3, nc.scalar.copy)
 
         q = sb.tile([P, PACK, SLOTS], F32, name="q", tag="window1")
         q_t = ps.tile([P, PACK, P], F32, name="q_t", tag="bank_a")
@@ -244,7 +249,7 @@ def tile_attend_gtopk_pl_kernel(tc, xT, sc, W, dz, offs, out_0, out_1, out_2, ou
         nc.scalar.copy(result_rows[:], result_t[0:32, :])
         nc.scalar.dma_start(out=out_1.rearrange("o (k n) -> (o k) n", k=PACK), in_=result_rows[0:PACK, :])
         quantise(0, 512)
-        regroup(3, nc.vector.tensor_copy)
+        regroup(2, nc.vector.tensor_copy)
         quantise(512, 768)
         quantise(768, 1024)
         quantise(1024, 1280)

@@ -85,13 +85,12 @@ def tile_attend_gtopk_pl_kernel(tc, xT, sc, W, dz, offs, out_0, out_1, out_2, ou
                 nc.tensor.transpose(spread[:, k, :], score_cols[:, col : col + 1].to_broadcast([P, P]), ident[:])
             nc.scalar.activation(scores_by_col[:, :, 4 * b : 4 * b + 4], spread[:].rearrange("p k n -> p n k"), COPY)
 
-        whole = [(slice(0, SLOTS), slice(0, SLOTS // 16))]
         halves = [(slice(h * HALF, (h + 1) * HALF), slice(h * HALF // 16, (h + 1) * HALF // 16)) for h in range(2)]
 
         w_grouped = sb.tile([P, PACK, P, PACK], BF16, name="w_grouped", align_bytes=64)
         w_codes = sb.tile([P, FEATS], U32, name="w_codes", align_bytes=64)
         w_scales = sb.tile([P, FEATS], U8, name="w_scales", align_bytes=64)
-        dz_codes = sb.tile([P, SLOTS], U32, name="dz_codes", tag="before_window2", align_bytes=64)
+        dz_codes = sb.tile([P, SLOTS], U32, name="dz_codes", align_bytes=64)
         dz_scales = sb.tile([P, SLOTS], U8, name="dz_scales", align_bytes=64)
         nc.vector.memset(dz_codes[:, HALF:SLOTS].bitcast(I32), 0)
         nc.vector.memset(dz_scales[:, HALF:SLOTS].bitcast(I32), 0)
@@ -112,7 +111,7 @@ def tile_attend_gtopk_pl_kernel(tc, xT, sc, W, dz, offs, out_0, out_1, out_2, ou
             )
 
         def regroup_dz(h):
-            dz_grouped = sb.tile([P, HALF, PACK], BF16, name=f"dz_grouped{h}", align_bytes=64)
+            dz_grouped = sb.tile([P, HALF, PACK], BF16, name=f"dz_grouped{h}", tag=("dz_grouped0", "before_window2")[h], align_bytes=64)
             nc.vector.tensor_copy(
                 dz_grouped[:].rearrange("p (c i) j -> p c j i", i=4),
                 dz_raw[h][:].rearrange("p j (c i) -> p c j i", i=4),
@@ -193,9 +192,19 @@ def tile_attend_gtopk_pl_kernel(tc, xT, sc, W, dz, offs, out_0, out_1, out_2, ou
                 pairs[c][:].rearrange("p h c e -> p (h c e)").bitcast(F32).rearrange("p (h c) -> p c h", h=2),
             )
 
+        dx_planes = [sb.tile([P, SLOTS], F32, name=f"dx{j}") for j in range(PACK)]
+        for j in range(1, PACK):
+            nc.gpsimd.tensor_tensor(dx_planes[j][:], u_planes[j], t_rows[:], MULT)
+
         for j in range(PACK):
-            for slots, entries in halves if j == 0 else whole:
-                nc.vector.tensor_tensor(windows[j][:].indirect(offsets[:, entries]), u_planes[j][:, slots], t_rows[:, slots], MULT)
+            if j == 0:
+                slots, entries = halves[0]
+                nc.vector.tensor_tensor(windows[0][:].indirect(offsets[:, entries]), u_first[:, slots], t_rows[:, slots], MULT)
+                slots, entries = halves[1]
+                nc.vector.tensor_tensor(dx_planes[0][:, slots], accs[0][:, slots], t_rows[:, slots], MULT)
+                nc.vector.tensor_copy(windows[0][:].indirect(offsets[:, entries]), dx_planes[0][:, slots])
+            else:
+                nc.vector.tensor_copy(windows[j][:].indirect(offsets[:]), dx_planes[j][:])
             nc.sync.dma_start(out=out_rows[:, j, :], in_=windows[j][:])
             if j < PACK - 1:
                 for c in range(len(CHUNKS)):

@@ -21,7 +21,14 @@ SLOTS = 512
 NODES = 2048
 FEATS = 512
 OUTS = 512
-CHUNKS = ((0, 512), (512, 1024), (1024, 1792), (1792, 2048))
+ADD = mybir.AluOpType.add
+ORDER = (0, 2, 3, 1)
+PAIRED = ((0, 512), (512, 1024))
+VECTOR_LAST = (1024, 1280)
+POOL_FIRST = (1280, 1920)
+SCALAR_ONLY = (1920, 2048)
+CHUNKS = PAIRED + (VECTOR_LAST, POOL_FIRST, SCALAR_ONLY)
+CALLS = ((0, 256), (256, 512), (512, 768), (768, 1024), (1024, 1280), (1280, 1536), (1536, 1792), (1792, 1920), (1920, 2048))
 STORES = {1024: 0, 1536: 1024, 2048: 1536}
 BAND = 512
 HALF = SLOTS // 2
@@ -157,18 +164,16 @@ def tile_attend_gtopk_pl_kernel(tc, xT, sc, W, dz, offs, out_0, out_1, out_2, ou
         nc.scalar.copy(u_first[:, 0:HALF], early[:, 0:HALF])
         quantise_dz(1, dz_second)
         tanh_of_scores(1, "before_u_rest")
-        accs = [multiply(t, f"acc{t}" if t < 3 else "acc4") for t in range(PACK)]
+        accs = {t: multiply(t, f"acc{n}" if n < 3 else "acc4") for n, t in enumerate(ORDER)}
         nc.scalar.copy(u_first[:, HALF:SLOTS], accs[0][:, HALF:SLOTS])
         u_rest = sb.tile([P, PACK - 1, SLOTS], F32, name="u_rest", tag="before_u_rest", align_bytes=64)
-        u_planes = [u_first[:]]
-        for t in range(1, PACK):
-            nc.scalar.copy(u_rest[:, t - 1, :], accs[t][:])
-            u_planes.append(u_rest[:, t - 1, :])
+        u_planes = [u_first[:]] + [u_rest[:, t - 1, :] for t in range(1, PACK)]
+        for t in ORDER[1:]:
+            nc.scalar.copy(u_planes[t], accs[t][:])
 
         window = sb.tile([P, NODES], F32, name="window2", tag="before_window2", align_bytes=64)
         nc.gpsimd.memset(window[:], 0.0)
-        windows.append(window)
-        windows.append(windows[0])
+        windows = {ORDER[0]: windows[0], ORDER[1]: windows[1], ORDER[2]: window, ORDER[3]: windows[0]}
 
         t_cols = ps.tile([P, PACK, P], F32, name="t_cols", tag="bank_b")
         for k in range(PACK):
@@ -179,24 +184,30 @@ def tile_attend_gtopk_pl_kernel(tc, xT, sc, W, dz, offs, out_0, out_1, out_2, ou
         nc.scalar.activation(slope[:], t_sq[:], COPY, bias=1.0, scale=-1.0)
 
         out_rows = out_0.rearrange("(p j) c -> p j c", j=PACK)
-        pairs = [sb.tile([P, 2, hi - lo, 2], BF16, name=f"pairs{lo}") for lo, hi in CHUNKS]
-        grouped = [sb.tile([P, hi - lo, PACK], BF16, name=f"grouped{lo}", align_bytes=64) for lo, hi in CHUNKS]
+        pairs = {chunk: sb.tile([P, 2, chunk[1] - chunk[0], 2], BF16, name=f"pairs{chunk[0]}") for chunk in PAIRED}
+        grouped = {chunk: sb.tile([P, chunk[1] - chunk[0], PACK], BF16, name=f"grouped{chunk[0]}", align_bytes=64) for chunk in CHUNKS}
 
-        def round_plane(j, c):
-            lo, hi = CHUNKS[c]
-            nc.scalar.copy(pairs[c][:, j // 2, :, j % 2], windows[j][:, lo:hi])
+        def pool_copy(out, in_):
+            nc.gpsimd.tensor_scalar(out, in_, 1.0, -0.0, MULT, ADD)
 
-        def regroup(c, copy):
-            copy(
-                grouped[c][:].rearrange("p c t -> p (c t)").bitcast(F32).rearrange("p (c h) -> p c h", h=2),
-                pairs[c][:].rearrange("p h c e -> p (h c e)").bitcast(F32).rearrange("p (h c) -> p c h", h=2),
+        def round_paired(j, chunk):
+            nc.scalar.copy(pairs[chunk][:, j // 2, :, j % 2], windows[j][:, chunk[0] : chunk[1]])
+
+        def round_direct(j, chunk, copy):
+            copy(grouped[chunk][:, :, j], windows[j][:, chunk[0] : chunk[1]])
+
+        def weave(chunk):
+            nc.scalar.copy(
+                grouped[chunk][:].rearrange("p c t -> p (c t)").bitcast(F32).rearrange("p (c h) -> p c h", h=2),
+                pairs[chunk][:].rearrange("p h c e -> p (h c e)").bitcast(F32).rearrange("p (h c) -> p c h", h=2),
             )
 
         dx_planes = [sb.tile([P, SLOTS], F32, name=f"dx{j}") for j in range(PACK)]
-        for j in range(1, PACK):
+        for j in ORDER[1:]:
             nc.gpsimd.tensor_tensor(dx_planes[j][:], u_planes[j], t_rows[:], MULT)
 
-        for j in range(PACK):
+        last = ORDER[-1]
+        for j in ORDER:
             if j == 0:
                 slots, entries = halves[0]
                 nc.vector.tensor_tensor(windows[0][:].indirect(offsets[:, entries]), u_first[:, slots], t_rows[:, slots], MULT)
@@ -206,17 +217,19 @@ def tile_attend_gtopk_pl_kernel(tc, xT, sc, W, dz, offs, out_0, out_1, out_2, ou
             else:
                 nc.vector.tensor_copy(windows[j][:].indirect(offsets[:]), dx_planes[j][:])
             nc.sync.dma_start(out=out_rows[:, j, :], in_=windows[j][:])
-            if j < PACK - 1:
-                for c in range(len(CHUNKS)):
-                    round_plane(j, c)
+            if j != last:
+                round_direct(j, POOL_FIRST, pool_copy)
+                for chunk in PAIRED:
+                    round_paired(j, chunk)
+                round_direct(j, VECTOR_LAST, nc.scalar.copy)
+                round_direct(j, SCALAR_ONLY, nc.scalar.copy)
 
-        round_plane(PACK - 1, 0)
-        round_plane(PACK - 1, 1)
-        regroup(0, nc.scalar.copy)
-        round_plane(PACK - 1, 2)
-        round_plane(PACK - 1, 3)
-        regroup(1, nc.scalar.copy)
-        regroup(3, nc.scalar.copy)
+        for chunk in PAIRED:
+            round_paired(last, chunk)
+        for chunk in PAIRED:
+            weave(chunk)
+        round_direct(last, POOL_FIRST, nc.scalar.copy)
+        round_direct(last, SCALAR_ONLY, nc.scalar.copy)
 
         q = sb.tile([P, PACK, SLOTS], F32, name="q", tag="window1")
         q_t = ps.tile([P, PACK, P], F32, name="q_t", tag="bank_a")
@@ -231,6 +244,8 @@ def tile_attend_gtopk_pl_kernel(tc, xT, sc, W, dz, offs, out_0, out_1, out_2, ou
                     stop=(j == PACK - 1 and k == PACK - 1),
                     is_transpose=True,
                 )
+            if j == 0:
+                round_direct(last, VECTOR_LAST, nc.vector.tensor_copy)
 
         words_out = out_2.rearrange("o p c l -> p (o c l)").bitcast(I32)
         out_scales = sb.tile([P, BAND], U8, name="out_scales", align_bytes=64)
@@ -238,8 +253,8 @@ def tile_attend_gtopk_pl_kernel(tc, xT, sc, W, dz, offs, out_0, out_1, out_2, ou
         out_codes = sb.tile([P, NODES], U32, name="out_codes", align_bytes=64)
 
         def quantise(lo, hi):
-            c = max(k for k, chunk in enumerate(CHUNKS) if chunk[0] <= lo)
-            first = CHUNKS[c][0]
+            c = max(chunk for chunk in CHUNKS if chunk[0] <= lo)
+            first = c[0]
             nc.vector.quantize_mx(
                 out=out_codes[:, lo:hi].bitcast(E4M3X4),
                 scales=out_scales[4 * (lo // BAND) :, lo % BAND : lo % BAND + hi - lo],
@@ -257,14 +272,8 @@ def tile_attend_gtopk_pl_kernel(tc, xT, sc, W, dz, offs, out_0, out_1, out_2, ou
         result_rows = sb.tile([32, P], F32, name="result_rows")
         nc.scalar.copy(result_rows[:], result_t[0:32, :])
         nc.scalar.dma_start(out=out_1.rearrange("o (k n) -> (o k) n", k=PACK), in_=result_rows[0:PACK, :])
-        quantise(0, 512)
-        regroup(2, nc.vector.tensor_copy)
-        quantise(512, 768)
-        quantise(768, 1024)
-        quantise(1024, 1280)
-        quantise(1280, 1536)
-        quantise(1536, 1792)
-        quantise(1792, 2048)
+        for lo, hi in CALLS:
+            quantise(lo, hi)
         scales_out = out_3.bitcast(I32).rearrange("o r (b c) -> b (o r) c", b=NODES // BAND)
         for quadrant in range(4):
             queue = nc.scalar if quadrant % 2 == 0 else nc.sync

@@ -29,7 +29,7 @@ POOL_FIRST = (1280, 1920)
 SCALAR_ONLY = (1920, 2048)
 CHUNKS = PAIRED + (VECTOR_LAST, POOL_FIRST, SCALAR_ONLY)
 CALLS = ((0, 256), (256, 512), (512, 768), (768, 1024), (1024, 1280), (1280, 1536), (1536, 1792), (1792, 1920), (1920, 2048))
-STORES = {1024: 0, 1536: 1024, 2048: 1536}
+STORES = {768: 0, 1536: 768, 2048: 1536}
 BAND = 512
 HALF = SLOTS // 2
 

@@ -11,9 +11,10 @@ U8 = mybir.dt.uint8
 E4M3X4 = mybir.dt.float8_e4m3fn_x4
 E5M2X4 = mybir.dt.float8_e5m2_x4
 MULT = mybir.AluOpType.mult
+ADD = mybir.AluOpType.add
 COPY = mybir.ActivationFunctionType.Copy
 SQUARE = mybir.ActivationFunctionType.Square
-SIGMOID = mybir.ActivationFunctionType.Sigmoid
+TANH = mybir.ActivationFunctionType.Tanh
 
 P = 128
 PACK = 4
@@ -21,17 +22,13 @@ SLOTS = 512
 NODES = 2048
 FEATS = 512
 OUTS = 512
-ADD = mybir.AluOpType.add
-ORDER = (0, 2, 3, 1)
-PAIRED = ((0, 512), (512, 1024))
-VECTOR_LAST = (1024, 1280)
-POOL_FIRST = (1280, 1920)
-SCALAR_ONLY = (1920, 2048)
-CHUNKS = PAIRED + (VECTOR_LAST, POOL_FIRST, SCALAR_ONLY)
-CALLS = ((0, 256), (256, 512), (512, 768), (768, 1024), (1024, 1280), (1280, 1536), (1536, 1792), (1792, 1920), (1920, 2048))
-STORES = {768: 0, 1536: 768, 2048: 1536}
-BAND = 512
 HALF = SLOTS // 2
+BAND = 512
+BANDS = NODES // BAND
+POOL_BANDS = 3
+CALL = 256
+FUSED = 1
+STORES = {768: 0, 1536: 768, 2048: 1536}
 
 FLOPS = 2 * OUTS * FEATS * SLOTS
 BYTES = 4 * (2 * FEATS * NODES + NODES + OUTS * FEATS + OUTS * SLOTS + SLOTS) + 2 * P * SLOTS // 16 + FEATS * NODES + FEATS * NODES // 32
@@ -44,22 +41,21 @@ def tile_attend_gtopk_pl_kernel(tc, xT, sc, W, dz, offs, out_0, out_1, out_2, ou
         ps = ctx.enter_context(tc.psum_pool(name="ps", bufs=1))
 
         offsets = sb.tile([P, SLOTS // 16], U16, name="offsets")
-        score_cols = sb.tile([P, NODES // P], F32, name="score_cols")
+        score_cols = sb.tile([P, NODES // P], F32, name="score_cols", tag="w_codes", align_bytes=64)
         nc.sync.dma_start(out=score_cols[:], in_=sc[0:1, :].rearrange("o (p k) -> (o p) k", p=P))
         w_rows = W.rearrange("(p j) d -> p j d", j=PACK)
         dz_rows = dz.rearrange("(p j) i -> p j i", j=PACK)
-        w_raw, dz_raw = [], []
-        for h in range(2):
-            for name, rows, tiles in (("dz", dz_rows, dz_raw), ("w", w_rows, w_raw)) if h == 0 else (("w", w_rows, w_raw), ("dz", dz_rows, dz_raw)):
-                raw = sb.tile([P, PACK, HALF], F32, name=f"{name}_raw{h}")
-                nc.sync.dma_start(out=raw[:], in_=rows[:, :, h * HALF : (h + 1) * HALF])
-                tiles.append(raw)
-            if h == 0:
-                nc.sync.dma_start(offsets[:], offs)
+        dz_raw = [sb.tile([P, PACK, HALF], F32, name=f"dz_raw{h}") for h in range(2)]
+        w_raw = [sb.tile([P, PACK, HALF], F32, name=f"w_raw{h}") for h in range(2)]
+        nc.sync.dma_start(out=dz_raw[0][:], in_=dz_rows[:, :, 0:HALF])
+        nc.sync.dma_start(out=w_raw[0][:], in_=w_rows[:, :, 0:HALF])
+        nc.sync.dma_start(offsets[:], offs)
+        nc.sync.dma_start(out=w_raw[1][:], in_=w_rows[:, :, HALF:FEATS])
+        nc.sync.dma_start(out=dz_raw[1][:], in_=dz_rows[:, :, HALF:SLOTS])
         x_rows = xT.rearrange("(p j) c -> p j c", j=PACK)
         x_planes = []
         for j in range(PACK):
-            plane = sb.tile([P, NODES], F32, name=f"x_plane{j}")
+            plane = sb.tile([P, NODES], F32, name=f"x_plane{j}", tag=f"x_plane{j}", align_bytes=64)
             nc.sync.dma_start(out=plane[:], in_=x_rows[:, j, :])
             x_planes.append(plane)
 
@@ -76,14 +72,15 @@ def tile_attend_gtopk_pl_kernel(tc, xT, sc, W, dz, offs, out_0, out_1, out_2, ou
             channel_multiplier=1,
         )
         result_cols = sb.tile([P, P], F32, name="result_cols")
-        nc.scalar.activation(result_cols[:], ident[:], SIGMOID, scale=0.0)
+        nc.scalar.activation(result_cols[:], ident[:], TANH, scale=0.0)
 
-        windows = [sb.tile([P, NODES], F32, name="window0"), None]
+        windows = [sb.tile([P, NODES], F32, name="window0"), sb.tile([P, NODES], F32, name="window1", tag="window1")]
         nc.vector.memset(windows[0][:].bitcast(I32), 0)
-        windows[1] = sb.tile([P, NODES], F32, name="window1", tag="window1")
         nc.gpsimd.memset(windows[1][:].bitcast(I32), 0)
+        window_last = sb.tile([P, NODES], F32, name="window3")
+        nc.vector.memset(window_last[:].bitcast(I32), 0)
 
-        scores = sb.tile([P, NODES], F32, name="scores", tag="before_u0", align_bytes=64)
+        scores = sb.tile([P, NODES], F32, name="scores")
         scores_by_col = scores[:].rearrange("p (n k) -> p n k", k=NODES // P)
         for b in range(4):
             spread = ps.tile([P, 4, P], F32, name=f"spread{b}", tag=f"acc{b}")
@@ -94,13 +91,10 @@ def tile_attend_gtopk_pl_kernel(tc, xT, sc, W, dz, offs, out_0, out_1, out_2, ou
 
         halves = [(slice(h * HALF, (h + 1) * HALF), slice(h * HALF // 16, (h + 1) * HALF // 16)) for h in range(2)]
 
-        w_grouped = sb.tile([P, PACK, P, PACK], BF16, name="w_grouped", align_bytes=64)
-        w_codes = sb.tile([P, FEATS], U32, name="w_codes", align_bytes=64)
+        w_grouped = sb.tile([P, PACK, P, PACK], BF16, name="w_grouped", tag="window2", align_bytes=64)
+        w_codes = sb.tile([P, FEATS], U32, name="w_codes", tag="w_codes", align_bytes=64)
         w_scales = sb.tile([P, FEATS], U8, name="w_scales", align_bytes=64)
-        dz_codes = sb.tile([P, SLOTS], U32, name="dz_codes", align_bytes=64)
-        dz_scales = sb.tile([P, SLOTS], U8, name="dz_scales", align_bytes=64)
-        nc.vector.memset(dz_codes[:, HALF:SLOTS].bitcast(I32), 0)
-        nc.vector.memset(dz_scales[:, HALF:SLOTS].bitcast(I32), 0)
+        dz_mx = []
         t_rows = sb.tile([P, SLOTS], F32, name="t_rows")
 
         def regroup_w(h, lo, hi):
@@ -118,7 +112,7 @@ def tile_attend_gtopk_pl_kernel(tc, xT, sc, W, dz, offs, out_0, out_1, out_2, ou
             )
 
         def regroup_dz(h):
-            dz_grouped = sb.tile([P, HALF, PACK], BF16, name=f"dz_grouped{h}", tag=("dz_grouped0", "before_window2")[h], align_bytes=64)
+            dz_grouped = sb.tile([P, HALF, PACK], BF16, name=f"dz_grouped{h}", tag=("dz_grouped0", "window2")[h], align_bytes=64)
             nc.vector.tensor_copy(
                 dz_grouped[:].rearrange("p (c i) j -> p c j i", i=4),
                 dz_raw[h][:].rearrange("p j (c i) -> p c j i", i=4),
@@ -126,115 +120,122 @@ def tile_attend_gtopk_pl_kernel(tc, xT, sc, W, dz, offs, out_0, out_1, out_2, ou
             return dz_grouped
 
         def quantise_dz(h, dz_grouped):
-            cols = slice(h * HALF, (h + 1) * HALF)
-            nc.vector.quantize_mx(
-                out=dz_codes[:, cols].bitcast(E5M2X4), scales=dz_scales[:, cols], in_=dz_grouped[:].rearrange("p c j -> p (c j)")
-            )
+            codes = sb.tile([P, HALF], U32, name=f"dz_codes{h}", tag=("dz_codes0", "picked0")[h], align_bytes=64)
+            scales = sb.tile([P, HALF], U8, name=f"dz_scales{h}", align_bytes=64)
+            nc.vector.quantize_mx(out=codes[:].bitcast(E5M2X4), scales=scales[:], in_=dz_grouped[:].rearrange("p c j -> p (c j)"))
+            dz_mx.append((codes, scales))
 
-        def tanh_of_scores(h, tag):
-            slots, entries = halves[h]
-            gate = sb.tile([P, HALF], F32, name=f"gate{h}", tag=tag, align_bytes=64)
-            nc.scalar.activation(gate[:], scores[:].indirect(offsets[:, entries]), SIGMOID, scale=2.0)
-            nc.scalar.activation(t_rows[:, slots], gate[:], COPY, bias=-1.0, scale=2.0)
+        for h, (slots, entries) in enumerate(halves):
+            picked_scores = sb.tile([P, HALF], F32, name=f"picked_scores{h}", tag=("picked0", "u_fused")[h], align_bytes=64)
+            nc.scalar.activation(picked_scores[:], scores[:].indirect(offsets[:, entries]), COPY)
+            nc.scalar.activation(t_rows[:, slots], picked_scores[:], TANH)
 
-        def multiply(t, tag):
-            acc = ps.tile([P, SLOTS], F32, name=f"acc{t}_{tag}", tag=tag)
+        accs = [ps.tile([P, SLOTS], F32, name=f"u{j}", tag=f"acc{j}") for j in range(PACK)]
+
+        def multiply(j, h):
+            codes, scales = dz_mx[h]
             nc.tensor.matmul_mx(
-                out=acc[:],
-                lhsT=w_codes[:, t * P : (t + 1) * P].bitcast(E4M3X4),
-                lhsT_scale=w_scales[:, t * P : (t + 1) * P],
-                rhs=dz_codes[:].bitcast(E5M2X4),
-                rhs_scale=dz_scales[:],
+                out=accs[j][:, halves[h][0]],
+                lhsT=w_codes[:, j * P : (j + 1) * P].bitcast(E4M3X4),
+                lhsT_scale=w_scales[:, j * P : (j + 1) * P],
+                rhs=codes[:].bitcast(E5M2X4),
+                rhs_scale=scales[:],
                 start=True,
                 stop=True,
             )
-            return acc
 
-        tanh_of_scores(0, "gate0")
+        first, second, both = halves[0][0], halves[1][0], slice(0, SLOTS)
         quantise_dz(0, regroup_dz(0))
         regroup_w(0, 0, PACK)
         regroup_w(1, 0, 2)
         regroup_w(1, 2, PACK)
-        quantise_w(0, 1)
-        early = multiply(0, "acc3")
-        quantise_w(1, 2)
-        dz_second = regroup_dz(1)
+        quantise_w(0, 2)
         quantise_w(2, 4)
-        u_first = sb.tile([P, SLOTS], F32, name="u_first", tag="before_u0", align_bytes=64)
-        nc.scalar.copy(u_first[:, 0:HALF], early[:, 0:HALF])
+        for j in range(PACK):
+            multiply(j, 0)
+        dz_second = regroup_dz(1)
+        dx_planes = {j: sb.tile([P, SLOTS], F32, name=f"dx{j}", tag=f"dx{j}", align_bytes=64) for j in (0, 2, 3)}
+        u_fused = sb.tile([P, SLOTS], F32, name="u_fused", tag="u_fused", align_bytes=64)
+
+        def gate(j, slots):
+            nc.vector.tensor_tensor(dx_planes[j][:, slots], accs[j][:, slots], t_rows[:, slots], MULT)
+
+        gate(0, first)
+        nc.scalar.copy(u_fused[:, first], accs[FUSED][:, first])
         quantise_dz(1, dz_second)
-        tanh_of_scores(1, "before_u_rest")
-        accs = {t: multiply(t, f"acc{n}" if n < 3 else "acc4") for n, t in enumerate(ORDER)}
-        nc.scalar.copy(u_first[:, HALF:SLOTS], accs[0][:, HALF:SLOTS])
-        u_rest = sb.tile([P, PACK - 1, SLOTS], F32, name="u_rest", tag="before_u_rest", align_bytes=64)
-        u_planes = [u_first[:]] + [u_rest[:, t - 1, :] for t in range(1, PACK)]
-        for t in ORDER[1:]:
-            nc.scalar.copy(u_planes[t], accs[t][:])
+        for j in range(PACK):
+            multiply(j, 1)
+        gate(0, second)
 
-        window = sb.tile([P, NODES], F32, name="window2", tag="before_window2", align_bytes=64)
-        nc.gpsimd.memset(window[:], 0.0)
-        windows = {ORDER[0]: windows[0], ORDER[1]: windows[1], ORDER[2]: window, ORDER[3]: windows[0]}
-
-        t_cols = ps.tile([P, PACK, P], F32, name="t_cols", tag="bank_b")
-        for k in range(PACK):
-            nc.tensor.transpose(t_cols[:, k, :], t_rows[:, k * P : (k + 1) * P], ident[:])
-        t_sq = sb.tile([P, PACK], F32, name="t_sq")
-        nc.scalar.activation(t_sq[:], t_cols[:, :, 0], SQUARE)
-        slope = sb.tile([P, PACK], F32, name="slope")
-        nc.scalar.activation(slope[:], t_sq[:], COPY, bias=1.0, scale=-1.0)
+        windows += [sb.tile([P, NODES], F32, name="window2", tag="window2", align_bytes=64), window_last]
+        nc.gpsimd.memset(windows[2][:].bitcast(I32), 0)
 
         out_rows = out_0.rearrange("(p j) c -> p j c", j=PACK)
-        pairs = {chunk: sb.tile([P, 2, chunk[1] - chunk[0], 2], BF16, name=f"pairs{chunk[0]}") for chunk in PAIRED}
-        grouped = {chunk: sb.tile([P, chunk[1] - chunk[0], PACK], BF16, name=f"grouped{chunk[0]}", align_bytes=64) for chunk in CHUNKS}
+
+        def scatter_scalar(j, h):
+            slots, entries = halves[h]
+            nc.scalar.activation(windows[j][:].indirect(offsets[:, entries]), dx_planes[j][:, slots], COPY)
+
+        def scatter_fused(h):
+            slots, entries = halves[h]
+            nc.vector.tensor_tensor(windows[FUSED][:].indirect(offsets[:, entries]), u_fused[:, slots], t_rows[:, slots], MULT)
+
+        def store(j):
+            nc.sync.dma_start(out=out_rows[:, j, :], in_=windows[j][:])
+
+        scatter_scalar(0, 0)
+        nc.scalar.copy(u_fused[:, second], accs[FUSED][:, second])
+        scatter_fused(0)
+        scatter_scalar(0, 1)
+        store(0)
+        gate(2, both)
+        scatter_fused(1)
+        store(FUSED)
+        gate(3, both)
+        nc.vector.tensor_copy(windows[3][:].indirect(offsets[:]), dx_planes[3][:])
+        scatter_scalar(2, 0)
+        scatter_scalar(2, 1)
+        store(3)
+        store(2)
+
+        pairs = [sb.tile([P, 2, BAND, 2], BF16, name=f"pairs{b}") for b in range(POOL_BANDS)]
 
         def pool_copy(out, in_):
             nc.gpsimd.tensor_scalar(out, in_, 1.0, -0.0, MULT, ADD)
 
-        def round_paired(j, chunk):
-            nc.scalar.copy(pairs[chunk][:, j // 2, :, j % 2], windows[j][:, chunk[0] : chunk[1]])
+        def round_paired(j, b, copy):
+            copy(pairs[b][:, j // 2, :, j % 2], windows[j][:, b * BAND : (b + 1) * BAND])
 
-        def round_direct(j, chunk, copy):
-            copy(grouped[chunk][:, :, j], windows[j][:, chunk[0] : chunk[1]])
+        for j in (0, 1):
+            for b in range(POOL_BANDS):
+                round_paired(j, b, pool_copy)
 
-        def weave(chunk):
-            nc.scalar.copy(
-                grouped[chunk][:].rearrange("p c t -> p (c t)").bitcast(F32).rearrange("p (c h) -> p c h", h=2),
-                pairs[chunk][:].rearrange("p h c e -> p (h c e)").bitcast(F32).rearrange("p (h c) -> p c h", h=2),
-            )
+        picked_first = sb.tile([P, SLOTS], F32, name="picked_first", tag="dx0", align_bytes=64)
+        picked_rest = sb.tile([P, 2, SLOTS], F32, name="picked_rest", tag="dx2", align_bytes=64)
+        picked_x = {0: picked_first[:], 2: picked_rest[:, 0, :], 3: picked_rest[:, 1, :]}
+        for j in (0, 2, 3):
+            nc.scalar.activation(picked_x[j], x_planes[j][:].indirect(offsets[:]), COPY)
 
-        dx_planes = [sb.tile([P, SLOTS], F32, name=f"dx{j}") for j in range(PACK)]
-        for j in ORDER[1:]:
-            nc.gpsimd.tensor_tensor(dx_planes[j][:], u_planes[j], t_rows[:], MULT)
+        t_cols = ps.tile([P, PACK, P], F32, name="t_cols", tag=f"acc{FUSED}")
+        for k in range(PACK):
+            nc.tensor.transpose(t_cols[:, k, :], t_rows[:, k * P : (k + 1) * P], ident[:])
+        t_sq = sb.tile([P, PACK], F32, name="t_sq", tag="x_plane0", align_bytes=64)
+        nc.scalar.activation(t_sq[:], t_cols[:, :, 0], SQUARE)
+        slope = sb.tile([P, PACK], F32, name="slope")
+        nc.scalar.activation(slope[:], t_sq[:], COPY, bias=1.0, scale=-1.0)
 
-        last = ORDER[-1]
-        for j in ORDER:
-            if j == 0:
-                slots, entries = halves[0]
-                nc.vector.tensor_tensor(windows[0][:].indirect(offsets[:, entries]), u_first[:, slots], t_rows[:, slots], MULT)
-                slots, entries = halves[1]
-                nc.vector.tensor_tensor(dx_planes[0][:, slots], accs[0][:, slots], t_rows[:, slots], MULT)
-                nc.vector.tensor_copy(windows[0][:].indirect(offsets[:, entries]), dx_planes[0][:, slots])
-            else:
-                nc.vector.tensor_copy(windows[j][:].indirect(offsets[:]), dx_planes[j][:])
-            nc.sync.dma_start(out=out_rows[:, j, :], in_=windows[j][:])
-            if j != last:
-                round_direct(j, POOL_FIRST, pool_copy)
-                for chunk in PAIRED:
-                    round_paired(j, chunk)
-                round_direct(j, VECTOR_LAST, nc.scalar.copy)
-                round_direct(j, SCALAR_ONLY, nc.scalar.copy)
-
-        for chunk in PAIRED:
-            round_paired(last, chunk)
-        for chunk in PAIRED:
-            weave(chunk)
-        round_direct(last, POOL_FIRST, nc.scalar.copy)
-        round_direct(last, SCALAR_ONLY, nc.scalar.copy)
-
-        q = sb.tile([P, PACK, SLOTS], F32, name="q", tag="window1")
+        pairs.append(sb.tile([P, 2, BAND, 2], BF16, name="pairs3", tag="x_plane2", align_bytes=64))
+        for j in (0, 1):
+            round_paired(j, 3, nc.scalar.copy)
+        q = sb.tile([P, PACK, SLOTS], F32, name="q", tag="dx3", align_bytes=64)
         q_t = ps.tile([P, PACK, P], F32, name="q_t", tag="bank_a")
         for j in range(PACK):
-            nc.vector.tensor_tensor(q[:, j, :], x_planes[j][:].indirect(offsets[:]), u_planes[j], MULT)
+            for lower in (3, 2):
+                round_paired(lower, j, nc.vector.tensor_copy)
+            if j == FUSED:
+                nc.vector.tensor_tensor(q[:, j, :], x_planes[j][:].indirect(offsets[:]), u_fused[:], MULT)
+            else:
+                nc.vector.tensor_tensor(q[:, j, :], accs[j][:], picked_x[j], MULT)
             for k in range(PACK):
                 nc.tensor.matmul(
                     q_t[:, k, :],
@@ -244,37 +245,44 @@ def tile_attend_gtopk_pl_kernel(tc, xT, sc, W, dz, offs, out_0, out_1, out_2, ou
                     stop=(j == PACK - 1 and k == PACK - 1),
                     is_transpose=True,
                 )
-            if j == 0:
-                round_direct(last, VECTOR_LAST, nc.vector.tensor_copy)
+
+        grouped = sb.tile([P, NODES * PACK], BF16, name="grouped", tag=f"x_plane{PACK - 1}", align_bytes=64)
+
+        def weave(b):
+            nc.scalar.copy(
+                grouped[:, b * BAND * PACK : (b + 1) * BAND * PACK].bitcast(F32).rearrange("p (c h) -> p c h", h=2),
+                pairs[b][:].rearrange("p h c e -> p (h c e)").bitcast(F32).rearrange("p (h c) -> p c h", h=2),
+            )
 
         words_out = out_2.rearrange("o p c l -> p (o c l)").bitcast(I32)
         out_scales = sb.tile([P, BAND], U8, name="out_scales", align_bytes=64)
-
         out_codes = sb.tile([P, NODES], U32, name="out_codes", align_bytes=64)
 
         def quantise(lo, hi):
-            c = max(chunk for chunk in CHUNKS if chunk[0] <= lo)
-            first = c[0]
             nc.vector.quantize_mx(
                 out=out_codes[:, lo:hi].bitcast(E4M3X4),
                 scales=out_scales[4 * (lo // BAND) :, lo % BAND : lo % BAND + hi - lo],
-                in_=grouped[c][:, lo - first : hi - first, :].rearrange("p c t -> p (c t)"),
+                in_=grouped[:, lo * PACK : hi * PACK],
             )
             if hi in STORES:
                 lo = STORES[hi]
                 nc.sync.dma_start(out=words_out[:, lo:hi], in_=out_codes[:, lo:hi].bitcast(I32))
 
+        weave(0)
+        weave(1)
         scaled = sb.tile([P, PACK, P], F32, name="scaled")
         for k in range(PACK):
             nc.scalar.activation(scaled[:, k, :], q_t[:, k, :], COPY, scale=slope[:, k : k + 1], accum_out=result_cols[:, k : k + 1])
         result_t = ps.tile([P, P], F32, name="result_t", tag="bank_b")
         nc.tensor.transpose(result_t[:], result_cols[:], ident[:])
+        weave(2)
         result_rows = sb.tile([32, P], F32, name="result_rows")
         nc.scalar.copy(result_rows[:], result_t[0:32, :])
         nc.scalar.dma_start(out=out_1.rearrange("o (k n) -> (o k) n", k=PACK), in_=result_rows[0:PACK, :])
-        for lo, hi in CALLS:
-            quantise(lo, hi)
-        scales_out = out_3.bitcast(I32).rearrange("o r (b c) -> b (o r) c", b=NODES // BAND)
+        weave(3)
+        for lo in range(0, NODES, CALL):
+            quantise(lo, lo + CALL)
+        scales_out = out_3.bitcast(I32).rearrange("o r (b c) -> b (o r) c", b=BANDS)
         for quadrant in range(4):
             queue = nc.scalar if quadrant % 2 == 0 else nc.sync
             queue.dma_start(

@@ -25,7 +25,8 @@ OUTS = 512
 HALF = SLOTS // 2
 BAND = 512
 BANDS = NODES // BAND
-POOL_BANDS = 3
+WIDE = 1024
+SCALAR_FROM = 1536
 CALL = 256
 FUSED = 1
 STORES = {768: 0, 1536: 768, 2048: 1536}
@@ -198,17 +199,17 @@ def tile_attend_gtopk_pl_kernel(tc, xT, sc, W, dz, offs, out_0, out_1, out_2, ou
         store(3)
         store(2)
 
-        pairs = [sb.tile([P, 2, BAND, 2], BF16, name=f"pairs{b}") for b in range(POOL_BANDS)]
+        pairs = {0: sb.tile([P, 2, WIDE, 2], BF16, name="pairs_low")}
 
         def pool_copy(out, in_):
             nc.gpsimd.tensor_scalar(out, in_, 1.0, -0.0, MULT, ADD)
 
-        def round_paired(j, b, copy):
-            copy(pairs[b][:, j // 2, :, j % 2], windows[j][:, b * BAND : (b + 1) * BAND])
+        def round_paired(j, lo, hi, copy):
+            base = lo // WIDE * WIDE
+            copy(pairs[base][:, j // 2, lo - base : hi - base, j % 2], windows[j][:, lo:hi])
 
         for j in (0, 1):
-            for b in range(POOL_BANDS):
-                round_paired(j, b, pool_copy)
+            round_paired(j, 0, WIDE, pool_copy)
 
         picked_first = sb.tile([P, SLOTS], F32, name="picked_first", tag="dx0", align_bytes=64)
         picked_rest = sb.tile([P, 2, SLOTS], F32, name="picked_rest", tag="dx2", align_bytes=64)
@@ -224,14 +225,18 @@ def tile_attend_gtopk_pl_kernel(tc, xT, sc, W, dz, offs, out_0, out_1, out_2, ou
         slope = sb.tile([P, PACK], F32, name="slope")
         nc.scalar.activation(slope[:], t_sq[:], COPY, bias=1.0, scale=-1.0)
 
-        pairs.append(sb.tile([P, 2, BAND, 2], BF16, name="pairs3", tag="x_plane2", align_bytes=64))
+        pairs[WIDE] = sb.tile([P, 2, WIDE, 2], BF16, name="pairs_high", tag="x_plane2", align_bytes=64)
         for j in (0, 1):
-            round_paired(j, 3, nc.scalar.copy)
+            round_paired(j, SCALAR_FROM, NODES, nc.scalar.copy)
         q = sb.tile([P, PACK, SLOTS], F32, name="q", tag="dx3", align_bytes=64)
         q_t = ps.tile([P, PACK, P], F32, name="q_t", tag="bank_a")
         for j in range(PACK):
-            for lower in (3, 2):
-                round_paired(lower, j, nc.vector.tensor_copy)
+            if j % 2 == 0:
+                for lower in (3, 2):
+                    round_paired(lower, j // 2 * WIDE, (j // 2 + 1) * WIDE, nc.vector.tensor_copy)
+            if j == PACK - 1:
+                for lower in (0, 1):
+                    round_paired(lower, WIDE, SCALAR_FROM, nc.vector.tensor_copy)
             if j == FUSED:
                 nc.vector.tensor_tensor(q[:, j, :], x_planes[j][:].indirect(offsets[:]), u_fused[:], MULT)
             else:
@@ -248,10 +253,11 @@ def tile_attend_gtopk_pl_kernel(tc, xT, sc, W, dz, offs, out_0, out_1, out_2, ou
 
         grouped = sb.tile([P, NODES * PACK], BF16, name="grouped", tag=f"x_plane{PACK - 1}", align_bytes=64)
 
-        def weave(b):
+        def weave(lo, hi):
+            base = lo // WIDE * WIDE
             nc.scalar.copy(
-                grouped[:, b * BAND * PACK : (b + 1) * BAND * PACK].bitcast(F32).rearrange("p (c h) -> p c h", h=2),
-                pairs[b][:].rearrange("p h c e -> p (h c e)").bitcast(F32).rearrange("p (h c) -> p c h", h=2),
+                grouped[:, lo * PACK : hi * PACK].bitcast(F32).rearrange("p (c h) -> p c h", h=2),
+                pairs[base][:].rearrange("p h c e -> p (h c e)").bitcast(F32).rearrange("p (h c) -> p c h", h=2)[:, lo - base : hi - base, :],
             )
 
         words_out = out_2.rearrange("o p c l -> p (o c l)").bitcast(I32)
@@ -268,18 +274,18 @@ def tile_attend_gtopk_pl_kernel(tc, xT, sc, W, dz, offs, out_0, out_1, out_2, ou
                 lo = STORES[hi]
                 nc.sync.dma_start(out=words_out[:, lo:hi], in_=out_codes[:, lo:hi].bitcast(I32))
 
-        weave(0)
-        weave(1)
+        weave(0, 1024)
+        weave(1024, 1536)
         scaled = sb.tile([P, PACK, P], F32, name="scaled")
         for k in range(PACK):
             nc.scalar.activation(scaled[:, k, :], q_t[:, k, :], COPY, scale=slope[:, k : k + 1], accum_out=result_cols[:, k : k + 1])
         result_t = ps.tile([P, P], F32, name="result_t", tag="bank_b")
         nc.tensor.transpose(result_t[:], result_cols[:], ident[:])
-        weave(2)
+        weave(1536, 1792)
         result_rows = sb.tile([32, P], F32, name="result_rows")
         nc.scalar.copy(result_rows[:], result_t[0:32, :])
         nc.scalar.dma_start(out=out_1.rearrange("o (k n) -> (o k) n", k=PACK), in_=result_rows[0:PACK, :])
-        weave(3)
+        weave(1792, 2048)
         for lo in range(0, NODES, CALL):
             quantise(lo, lo + CALL)
         scales_out = out_3.bitcast(I32).rearrange("o r (b c) -> b (o r) c", b=BANDS)

@@ -23,13 +23,13 @@ NODES = 2048
 FEATS = 512
 OUTS = 512
 HALF = SLOTS // 2
-BAND = 512
+BAND = 1024
 BANDS = NODES // BAND
 WIDE = 1024
 SCALAR_FROM = 1536
-CALL = 256
+CALLS = (0, 512, 1024, 1536, 1792, 2048)
 FUSED = 1
-STORES = {768: 0, 1536: 768, 2048: 1536}
+STORES = {1024: 0, 1536: 1024, 2048: 1536}
 
 FLOPS = 2 * OUTS * FEATS * SLOTS
 BYTES = 4 * (2 * FEATS * NODES + NODES + OUTS * FEATS + OUTS * SLOTS + SLOTS) + 2 * P * SLOTS // 16 + FEATS * NODES + FEATS * NODES // 32
@@ -42,7 +42,7 @@ def tile_attend_gtopk_pl_kernel(tc, xT, sc, W, dz, offs, out_0, out_1, out_2, ou
         ps = ctx.enter_context(tc.psum_pool(name="ps", bufs=1))
 
         offsets = sb.tile([P, SLOTS // 16], U16, name="offsets")
-        score_cols = sb.tile([P, NODES // P], F32, name="score_cols", tag="w_codes", align_bytes=64)
+        score_cols = sb.tile([P, NODES // P], F32, name="score_cols", tag="window2", align_bytes=64)
         nc.sync.dma_start(out=score_cols[:], in_=sc[0:1, :].rearrange("o (p k) -> (o p) k", p=P))
         w_rows = W.rearrange("(p j) d -> p j d", j=PACK)
         dz_rows = dz.rearrange("(p j) i -> p j i", j=PACK)
@@ -78,8 +78,6 @@ def tile_attend_gtopk_pl_kernel(tc, xT, sc, W, dz, offs, out_0, out_1, out_2, ou
         windows = [sb.tile([P, NODES], F32, name="window0"), sb.tile([P, NODES], F32, name="window1", tag="window1")]
         nc.vector.memset(windows[0][:].bitcast(I32), 0)
         nc.gpsimd.memset(windows[1][:].bitcast(I32), 0)
-        window_last = sb.tile([P, NODES], F32, name="window3")
-        nc.vector.memset(window_last[:].bitcast(I32), 0)
 
         scores = sb.tile([P, NODES], F32, name="scores")
         scores_by_col = scores[:].rearrange("p (n k) -> p n k", k=NODES // P)
@@ -92,28 +90,28 @@ def tile_attend_gtopk_pl_kernel(tc, xT, sc, W, dz, offs, out_0, out_1, out_2, ou
 
         halves = [(slice(h * HALF, (h + 1) * HALF), slice(h * HALF // 16, (h + 1) * HALF // 16)) for h in range(2)]
 
-        w_grouped = sb.tile([P, PACK, P, PACK], BF16, name="w_grouped", tag="window2", align_bytes=64)
-        w_codes = sb.tile([P, FEATS], U32, name="w_codes", tag="w_codes", align_bytes=64)
+        w_grouped = [sb.tile([P, 2, P, PACK], BF16, name=f"w_grouped{g}", tag=("window3", "w_grouped1")[g], align_bytes=64) for g in range(2)]
+        w_codes = sb.tile([P, FEATS], U32, name="w_codes", tag="window2", align_bytes=64)
         w_scales = sb.tile([P, FEATS], U8, name="w_scales", align_bytes=64)
         dz_mx = []
         t_rows = sb.tile([P, SLOTS], F32, name="t_rows")
 
-        def regroup_w(h, lo, hi):
+        def regroup_w(h, g):
             nc.vector.tensor_copy(
-                w_grouped[:, lo:hi, h * P // 2 : (h + 1) * P // 2, :].rearrange("p t m j -> p m j t"),
-                w_raw[h][:].rearrange("p j (m t) -> p m j t", t=PACK)[:, :, :, lo:hi],
+                w_grouped[g][:, :, h * P // 2 : (h + 1) * P // 2, :].rearrange("p t m j -> p m j t"),
+                w_raw[h][:].rearrange("p j (m t) -> p m j t", t=PACK)[:, :, :, 2 * g : 2 * g + 2],
             )
 
-        def quantise_w(lo, hi):
-            cols = slice(lo * P, hi * P)
+        def quantise_w(g):
+            cols = slice(2 * g * P, 2 * (g + 1) * P)
             nc.vector.quantize_mx(
                 out=w_codes[:, cols].bitcast(E4M3X4),
                 scales=w_scales[:, cols],
-                in_=w_grouped[:, lo:hi, :, :].rearrange("p t m j -> p (t m j)"),
+                in_=w_grouped[g][:].rearrange("p t m j -> p (t m j)"),
             )
 
         def regroup_dz(h):
-            dz_grouped = sb.tile([P, HALF, PACK], BF16, name=f"dz_grouped{h}", tag=("dz_grouped0", "window2")[h], align_bytes=64)
+            dz_grouped = sb.tile([P, HALF, PACK], BF16, name=f"dz_grouped{h}", tag=("dz_grouped0", "window3")[h], align_bytes=64)
             nc.vector.tensor_copy(
                 dz_grouped[:].rearrange("p (c i) j -> p c j i", i=4),
                 dz_raw[h][:].rearrange("p j (c i) -> p c j i", i=4),
@@ -121,13 +119,13 @@ def tile_attend_gtopk_pl_kernel(tc, xT, sc, W, dz, offs, out_0, out_1, out_2, ou
             return dz_grouped
 
         def quantise_dz(h, dz_grouped):
-            codes = sb.tile([P, HALF], U32, name=f"dz_codes{h}", tag=("dz_codes0", "picked0")[h], align_bytes=64)
+            codes = sb.tile([P, HALF], U32, name=f"dz_codes{h}", tag=("dz_codes0", "picked1")[h], align_bytes=64)
             scales = sb.tile([P, HALF], U8, name=f"dz_scales{h}", align_bytes=64)
             nc.vector.quantize_mx(out=codes[:].bitcast(E5M2X4), scales=scales[:], in_=dz_grouped[:].rearrange("p c j -> p (c j)"))
             dz_mx.append((codes, scales))
 
         for h, (slots, entries) in enumerate(halves):
-            picked_scores = sb.tile([P, HALF], F32, name=f"picked_scores{h}", tag=("picked0", "u_fused")[h], align_bytes=64)
+            picked_scores = sb.tile([P, HALF], F32, name=f"picked_scores{h}", tag=("u_fused", "picked1")[h], align_bytes=64)
             nc.scalar.activation(picked_scores[:], scores[:].indirect(offsets[:, entries]), COPY)
             nc.scalar.activation(t_rows[:, slots], picked_scores[:], TANH)
 
@@ -145,37 +143,40 @@ def tile_attend_gtopk_pl_kernel(tc, xT, sc, W, dz, offs, out_0, out_1, out_2, ou
                 stop=True,
             )
 
-        first, second, both = halves[0][0], halves[1][0], slice(0, SLOTS)
+        first, second = halves[0][0], halves[1][0]
         quantise_dz(0, regroup_dz(0))
-        regroup_w(0, 0, PACK)
-        regroup_w(1, 0, 2)
-        regroup_w(1, 2, PACK)
-        quantise_w(0, 2)
-        quantise_w(2, 4)
+        for h in range(2):
+            for g in range(2):
+                regroup_w(h, g)
+        for g in range(2):
+            quantise_w(g)
         for j in range(PACK):
             multiply(j, 0)
         dz_second = regroup_dz(1)
-        dx_planes = {j: sb.tile([P, SLOTS], F32, name=f"dx{j}", tag=f"dx{j}", align_bytes=64) for j in (0, 2, 3)}
+        dx_last = sb.tile([P, SLOTS], F32, name="dx3", tag="dx3", align_bytes=64)
+        dx_halves = {(j, h): sb.tile([P, HALF], F32, name=f"dx{j}_{h}", tag=f"dx{j}_{h}", align_bytes=64) for j in (0, 2) for h in range(2)}
         u_fused = sb.tile([P, SLOTS], F32, name="u_fused", tag="u_fused", align_bytes=64)
 
-        def gate(j, slots):
-            nc.vector.tensor_tensor(dx_planes[j][:, slots], accs[j][:, slots], t_rows[:, slots], MULT)
+        def gate(j, h):
+            slots = halves[h][0]
+            nc.vector.tensor_tensor(dx_halves[j, h][:], accs[j][:, slots], t_rows[:, slots], MULT)
 
-        gate(0, first)
+        gate(0, 0)
         nc.scalar.copy(u_fused[:, first], accs[FUSED][:, first])
         quantise_dz(1, dz_second)
         for j in range(PACK):
             multiply(j, 1)
-        gate(0, second)
+        gate(0, 1)
 
-        windows += [sb.tile([P, NODES], F32, name="window2", tag="window2", align_bytes=64), window_last]
-        nc.gpsimd.memset(windows[2][:].bitcast(I32), 0)
+        windows += [sb.tile([P, NODES], F32, name=f"window{j}", tag=f"window{j}", align_bytes=64) for j in (2, 3)]
+        for j in (3, 2):
+            nc.gpsimd.memset(windows[j][:].bitcast(I32), 0)
 
         out_rows = out_0.rearrange("(p j) c -> p j c", j=PACK)
 
         def scatter_scalar(j, h):
             slots, entries = halves[h]
-            nc.scalar.activation(windows[j][:].indirect(offsets[:, entries]), dx_planes[j][:, slots], COPY)
+            nc.scalar.activation(windows[j][:].indirect(offsets[:, entries]), dx_halves[j, h][:], COPY)
 
         def scatter_fused(h):
             slots, entries = halves[h]
@@ -189,15 +190,13 @@ def tile_attend_gtopk_pl_kernel(tc, xT, sc, W, dz, offs, out_0, out_1, out_2, ou
         scatter_fused(0)
         scatter_scalar(0, 1)
         store(0)
-        gate(2, both)
+        gate(2, 0)
+        gate(2, 1)
+        nc.vector.tensor_tensor(dx_last[:], accs[3][:], t_rows[:], MULT)
         scatter_fused(1)
         store(FUSED)
-        gate(3, both)
-        nc.vector.tensor_copy(windows[3][:].indirect(offsets[:]), dx_planes[3][:])
-        scatter_scalar(2, 0)
-        scatter_scalar(2, 1)
+        nc.vector.tensor_copy(windows[3][:].indirect(offsets[:]), dx_last[:])
         store(3)
-        store(2)
 
         pairs = {0: sb.tile([P, 2, WIDE, 2], BF16, name="pairs_low")}
 
@@ -211,10 +210,15 @@ def tile_attend_gtopk_pl_kernel(tc, xT, sc, W, dz, offs, out_0, out_1, out_2, ou
         for j in (0, 1):
             round_paired(j, 0, WIDE, pool_copy)
 
-        picked_first = sb.tile([P, SLOTS], F32, name="picked_first", tag="dx0", align_bytes=64)
-        picked_rest = sb.tile([P, 2, SLOTS], F32, name="picked_rest", tag="dx2", align_bytes=64)
+        picked_first = sb.tile([P, SLOTS], F32, name="picked_first", tag="dx0_0", align_bytes=64)
+        nc.scalar.activation(picked_first[:], x_planes[0][:].indirect(offsets[:]), COPY)
+        scatter_scalar(2, 0)
+        picked_rest = sb.tile([P, 2, SLOTS], F32, name="picked_rest", tag="dx2_0", align_bytes=64)
         picked_x = {0: picked_first[:], 2: picked_rest[:, 0, :], 3: picked_rest[:, 1, :]}
-        for j in (0, 2, 3):
+        for j in (2, 3):
+            if j == 3:
+                scatter_scalar(2, 1)
+                store(2)
             nc.scalar.activation(picked_x[j], x_planes[j][:].indirect(offsets[:]), COPY)
 
         t_cols = ps.tile([P, PACK, P], F32, name="t_cols", tag=f"acc{FUSED}")
@@ -223,20 +227,19 @@ def tile_attend_gtopk_pl_kernel(tc, xT, sc, W, dz, offs, out_0, out_1, out_2, ou
         t_sq = sb.tile([P, PACK], F32, name="t_sq", tag="x_plane0", align_bytes=64)
         nc.scalar.activation(t_sq[:], t_cols[:, :, 0], SQUARE)
         slope = sb.tile([P, PACK], F32, name="slope")
-        nc.scalar.activation(slope[:], t_sq[:], COPY, bias=1.0, scale=-1.0)
+        nc.gpsimd.tensor_scalar(slope[:], t_sq[:], -1.0, 1.0, MULT, ADD)
 
         pairs[WIDE] = sb.tile([P, 2, WIDE, 2], BF16, name="pairs_high", tag="x_plane2", align_bytes=64)
         for j in (0, 1):
             round_paired(j, SCALAR_FROM, NODES, nc.scalar.copy)
-        q = sb.tile([P, PACK, SLOTS], F32, name="q", tag="dx3", align_bytes=64)
+        for lo in (0, WIDE):
+            for j in (3, 2):
+                round_paired(j, lo, lo + WIDE, nc.vector.tensor_copy)
+        for j in (0, 1):
+            round_paired(j, WIDE, SCALAR_FROM, nc.vector.tensor_copy)
+        q = sb.tile([P, PACK, SLOTS], F32, name="q", tag="dx2_1", align_bytes=64)
         q_t = ps.tile([P, PACK, P], F32, name="q_t", tag="bank_a")
         for j in range(PACK):
-            if j % 2 == 0:
-                for lower in (3, 2):
-                    round_paired(lower, j // 2 * WIDE, (j // 2 + 1) * WIDE, nc.vector.tensor_copy)
-            if j == PACK - 1:
-                for lower in (0, 1):
-                    round_paired(lower, WIDE, SCALAR_FROM, nc.vector.tensor_copy)
             if j == FUSED:
                 nc.vector.tensor_tensor(q[:, j, :], x_planes[j][:].indirect(offsets[:]), u_fused[:], MULT)
             else:
@@ -286,12 +289,12 @@ def tile_attend_gtopk_pl_kernel(tc, xT, sc, W, dz, offs, out_0, out_1, out_2, ou
         nc.scalar.copy(result_rows[:], result_t[0:32, :])
         nc.scalar.dma_start(out=out_1.rearrange("o (k n) -> (o k) n", k=PACK), in_=result_rows[0:PACK, :])
         weave(1792, 2048)
-        for lo in range(0, NODES, CALL):
-            quantise(lo, lo + CALL)
+        for lo, hi in zip(CALLS, CALLS[1:]):
+            quantise(lo, hi)
         scales_out = out_3.bitcast(I32).rearrange("o r (b c) -> b (o r) c", b=BANDS)
         for quadrant in range(4):
             queue = nc.scalar if quadrant % 2 == 0 else nc.sync
             queue.dma_start(
                 out=scales_out[:, 4 * quadrant : 4 * quadrant + 4, :],
-                in_=out_scales[32 * quadrant : 32 * quadrant + 16, :].bitcast(I32),
+                in_=out_scales[32 * quadrant : 32 * quadrant + 4 * BANDS, :].bitcast(I32),
             )

@@ -25,11 +25,10 @@ OUTS = 512
 HALF = SLOTS // 2
 BAND = 1024
 BANDS = NODES // BAND
-WIDE = 1024
-SCALAR_FROM = 1536
+PARTS = ((0, 512), (512, 1536), (1536, 2048))
+PRODUCTS = (0, 2, 3, 1)
 CALLS = (0, 512, 1024, 1536, 1792, 2048)
 FUSED = 1
-STORES = {1024: 0, 1536: 1024, 2048: 1536}
 
 FLOPS = 2 * OUTS * FEATS * SLOTS
 BYTES = 4 * (2 * FEATS * NODES + NODES + OUTS * FEATS + OUTS * SLOTS + SLOTS) + 2 * P * SLOTS // 16 + FEATS * NODES + FEATS * NODES // 32
@@ -42,7 +41,7 @@ def tile_attend_gtopk_pl_kernel(tc, xT, sc, W, dz, offs, out_0, out_1, out_2, ou
         ps = ctx.enter_context(tc.psum_pool(name="ps", bufs=1))
 
         offsets = sb.tile([P, SLOTS // 16], U16, name="offsets")
-        score_cols = sb.tile([P, NODES // P], F32, name="score_cols", tag="window2", align_bytes=64)
+        score_cols = sb.tile([P, NODES // P], F32, name="score_cols", tag="window3", align_bytes=64)
         nc.sync.dma_start(out=score_cols[:], in_=sc[0:1, :].rearrange("o (p k) -> (o p) k", p=P))
         w_rows = W.rearrange("(p j) d -> p j d", j=PACK)
         dz_rows = dz.rearrange("(p j) i -> p j i", j=PACK)
@@ -90,8 +89,8 @@ def tile_attend_gtopk_pl_kernel(tc, xT, sc, W, dz, offs, out_0, out_1, out_2, ou
 
         halves = [(slice(h * HALF, (h + 1) * HALF), slice(h * HALF // 16, (h + 1) * HALF // 16)) for h in range(2)]
 
-        w_grouped = [sb.tile([P, 2, P, PACK], BF16, name=f"w_grouped{g}", tag=("window3", "w_grouped1")[g], align_bytes=64) for g in range(2)]
-        w_codes = sb.tile([P, FEATS], U32, name="w_codes", tag="window2", align_bytes=64)
+        w_grouped = [sb.tile([P, 2, P, PACK], BF16, name=f"w_grouped{g}", tag=("window2", "w_grouped1")[g], align_bytes=64) for g in range(2)]
+        w_codes = sb.tile([P, FEATS], U32, name="w_codes", tag="window3", align_bytes=64)
         w_scales = sb.tile([P, FEATS], U8, name="w_scales", align_bytes=64)
         dz_mx = []
         t_rows = sb.tile([P, SLOTS], F32, name="t_rows")
@@ -111,7 +110,7 @@ def tile_attend_gtopk_pl_kernel(tc, xT, sc, W, dz, offs, out_0, out_1, out_2, ou
             )
 
         def regroup_dz(h):
-            dz_grouped = sb.tile([P, HALF, PACK], BF16, name=f"dz_grouped{h}", tag=("dz_grouped0", "window3")[h], align_bytes=64)
+            dz_grouped = sb.tile([P, HALF, PACK], BF16, name=f"dz_grouped{h}", tag=("dz_grouped0", "window2")[h], align_bytes=64)
             nc.vector.tensor_copy(
                 dz_grouped[:].rearrange("p (c i) j -> p c j i", i=4),
                 dz_raw[h][:].rearrange("p j (c i) -> p c j i", i=4),
@@ -154,12 +153,20 @@ def tile_attend_gtopk_pl_kernel(tc, xT, sc, W, dz, offs, out_0, out_1, out_2, ou
             multiply(j, 0)
         dz_second = regroup_dz(1)
         dx_last = sb.tile([P, SLOTS], F32, name="dx3", tag="dx3", align_bytes=64)
-        dx_halves = {(j, h): sb.tile([P, HALF], F32, name=f"dx{j}_{h}", tag=f"dx{j}_{h}", align_bytes=64) for j in (0, 2) for h in range(2)}
-        u_fused = sb.tile([P, SLOTS], F32, name="u_fused", tag="u_fused", align_bytes=64)
+        pairs = {}
+
+        def pair_tile(part, tag):
+            pairs[part] = sb.tile([P, 2 * (part[1] - part[0])], F32, name=f"pairs{part[0]}", tag=tag, align_bytes=64)
+            return pairs[part]
+
+        last_pairs = pair_tile(PARTS[2], "u_fused")
+        u_fused = last_pairs[:, SLOTS : 2 * SLOTS]
+        dx_halves = {(j, h): sb.tile([P, HALF], F32, name=f"dx{j}_{h}", tag=f"dx{j}_{h}", align_bytes=64)[:] for j, h in ((0, 0), (0, 1), (2, 0))}
+        dx_halves[2, 1] = last_pairs[:, 0:HALF]
 
         def gate(j, h):
             slots = halves[h][0]
-            nc.vector.tensor_tensor(dx_halves[j, h][:], accs[j][:, slots], t_rows[:, slots], MULT)
+            nc.vector.tensor_tensor(dx_halves[j, h], accs[j][:, slots], t_rows[:, slots], MULT)
 
         gate(0, 0)
         nc.scalar.copy(u_fused[:, first], accs[FUSED][:, first])
@@ -169,14 +176,14 @@ def tile_attend_gtopk_pl_kernel(tc, xT, sc, W, dz, offs, out_0, out_1, out_2, ou
         gate(0, 1)
 
         windows += [sb.tile([P, NODES], F32, name=f"window{j}", tag=f"window{j}", align_bytes=64) for j in (2, 3)]
-        for j in (3, 2):
+        for j in (2, 3):
             nc.gpsimd.memset(windows[j][:].bitcast(I32), 0)
 
         out_rows = out_0.rearrange("(p j) c -> p j c", j=PACK)
 
         def scatter_scalar(j, h):
             slots, entries = halves[h]
-            nc.scalar.activation(windows[j][:].indirect(offsets[:, entries]), dx_halves[j, h][:], COPY)
+            nc.scalar.activation(windows[j][:].indirect(offsets[:, entries]), dx_halves[j, h], COPY)
 
         def scatter_fused(h):
             slots, entries = halves[h]
@@ -195,31 +202,34 @@ def tile_attend_gtopk_pl_kernel(tc, xT, sc, W, dz, offs, out_0, out_1, out_2, ou
         nc.vector.tensor_tensor(dx_last[:], accs[3][:], t_rows[:], MULT)
         scatter_fused(1)
         store(FUSED)
-        nc.vector.tensor_copy(windows[3][:].indirect(offsets[:]), dx_last[:])
-        store(3)
-
-        pairs = {0: sb.tile([P, 2, WIDE, 2], BF16, name="pairs_low")}
 
         def pool_copy(out, in_):
             nc.gpsimd.tensor_scalar(out, in_, 1.0, -0.0, MULT, ADD)
 
-        def round_paired(j, lo, hi, copy):
-            base = lo // WIDE * WIDE
-            copy(pairs[base][:, j // 2, lo - base : hi - base, j % 2], windows[j][:, lo:hi])
+        def round_paired(j, part, copy):
+            width = part[1] - part[0]
+            words = pairs[part][:, j // 2 * width : (j // 2 + 1) * width]
+            copy(words.bitcast(BF16).rearrange("p (c e) -> p c e", e=2)[:, :, j % 2], windows[j][:, part[0] : part[1]])
 
-        for j in (0, 1):
-            round_paired(j, 0, WIDE, pool_copy)
-
-        picked_first = sb.tile([P, SLOTS], F32, name="picked_first", tag="dx0_0", align_bytes=64)
-        nc.scalar.activation(picked_first[:], x_planes[0][:].indirect(offsets[:]), COPY)
-        scatter_scalar(2, 0)
-        picked_rest = sb.tile([P, 2, SLOTS], F32, name="picked_rest", tag="dx2_0", align_bytes=64)
-        picked_x = {0: picked_first[:], 2: picked_rest[:, 0, :], 3: picked_rest[:, 1, :]}
-        for j in (2, 3):
-            if j == 3:
-                scatter_scalar(2, 1)
-                store(2)
+        def gather_x(j):
             nc.scalar.activation(picked_x[j], x_planes[j][:].indirect(offsets[:]), COPY)
+
+        picked_x = {0: pair_tile(PARTS[0], "dx0_0")[:, SLOTS : 2 * SLOTS]}
+        gather_x(0)
+        scatter_scalar(2, 0)
+        middle_pairs = pair_tile(PARTS[1], "dx2_0")
+        picked_x[2] = middle_pairs[:, 2 * SLOTS : 3 * SLOTS]
+        gather_x(2)
+        scatter_scalar(2, 1)
+        store(2)
+        picked_last = middle_pairs[:, 3 * SLOTS : 3 * SLOTS + HALF]
+        nc.scalar.activation(picked_last, x_planes[3][:].indirect(offsets[:, halves[1][1]]), COPY)
+        nc.vector.tensor_copy(windows[3][:].indirect(offsets[:]), dx_last[:])
+        store(3)
+        q = sb.tile([P, PACK, SLOTS], F32, name="q", tag="dx3", align_bytes=64)
+        for part in PARTS[:2]:
+            for j in (0, 1):
+                round_paired(j, part, pool_copy)
 
         t_cols = ps.tile([P, PACK, P], F32, name="t_cols", tag=f"acc{FUSED}")
         for k in range(PACK):
@@ -229,38 +239,16 @@ def tile_attend_gtopk_pl_kernel(tc, xT, sc, W, dz, offs, out_0, out_1, out_2, ou
         slope = sb.tile([P, PACK], F32, name="slope")
         nc.gpsimd.tensor_scalar(slope[:], t_sq[:], -1.0, 1.0, MULT, ADD)
 
-        pairs[WIDE] = sb.tile([P, 2, WIDE, 2], BF16, name="pairs_high", tag="x_plane2", align_bytes=64)
         for j in (0, 1):
-            round_paired(j, SCALAR_FROM, NODES, nc.scalar.copy)
-        for lo in (0, WIDE):
-            for j in (3, 2):
-                round_paired(j, lo, lo + WIDE, nc.vector.tensor_copy)
-        for j in (0, 1):
-            round_paired(j, WIDE, SCALAR_FROM, nc.vector.tensor_copy)
-        q = sb.tile([P, PACK, SLOTS], F32, name="q", tag="dx2_1", align_bytes=64)
-        q_t = ps.tile([P, PACK, P], F32, name="q_t", tag="bank_a")
-        for j in range(PACK):
-            if j == FUSED:
-                nc.vector.tensor_tensor(q[:, j, :], x_planes[j][:].indirect(offsets[:]), u_fused[:], MULT)
-            else:
-                nc.vector.tensor_tensor(q[:, j, :], accs[j][:], picked_x[j], MULT)
-            for k in range(PACK):
-                nc.tensor.matmul(
-                    q_t[:, k, :],
-                    q[:, j, k * P : (k + 1) * P],
-                    ident[:],
-                    start=(j == 0 and k == 0),
-                    stop=(j == PACK - 1 and k == PACK - 1),
-                    is_transpose=True,
-                )
-
+            round_paired(j, PARTS[2], nc.scalar.copy)
         grouped = sb.tile([P, NODES * PACK], BF16, name="grouped", tag=f"x_plane{PACK - 1}", align_bytes=64)
 
         def weave(lo, hi):
-            base = lo // WIDE * WIDE
+            part = max(part for part in PARTS if part[0] <= lo)
+            base = part[0]
             nc.scalar.copy(
                 grouped[:, lo * PACK : hi * PACK].bitcast(F32).rearrange("p (c h) -> p c h", h=2),
-                pairs[base][:].rearrange("p h c e -> p (h c e)").bitcast(F32).rearrange("p (h c) -> p c h", h=2)[:, lo - base : hi - base, :],
+                pairs[part][:].rearrange("p (h c) -> p c h", h=2)[:, lo - base : hi - base, :],
             )
 
         words_out = out_2.rearrange("o p c l -> p (o c l)").bitcast(I32)
@@ -273,11 +261,36 @@ def tile_attend_gtopk_pl_kernel(tc, xT, sc, W, dz, offs, out_0, out_1, out_2, ou
                 scales=out_scales[4 * (lo // BAND) :, lo % BAND : lo % BAND + hi - lo],
                 in_=grouped[:, lo * PACK : hi * PACK],
             )
-            if hi in STORES:
-                lo = STORES[hi]
-                nc.sync.dma_start(out=words_out[:, lo:hi], in_=out_codes[:, lo:hi].bitcast(I32))
+            nc.sync.dma_start(out=words_out[:, lo:hi], in_=out_codes[:, lo:hi].bitcast(I32))
 
-        weave(0, 1024)
+        q_t = ps.tile([P, PACK, P], F32, name="q_t", tag="bank_a")
+        for j in PRODUCTS:
+            if j == FUSED:
+                for part in PARTS[:2]:
+                    for upper in (3, 2):
+                        round_paired(upper, part, nc.vector.tensor_copy)
+                weave(0, 512)
+                quantise(0, 512)
+                nc.vector.tensor_tensor(q[:, j, :], x_planes[j][:].indirect(offsets[:]), u_fused, MULT)
+            elif j == 3:
+                nc.vector.tensor_copy(q[:, FUSED, first], x_planes[3][:].indirect(offsets[:, halves[0][1]]))
+                nc.vector.tensor_tensor(q[:, j, second], accs[j][:, second], picked_last, MULT)
+                nc.vector.tensor_tensor(q[:, j, first], accs[j][:, first], q[:, FUSED, first], MULT)
+            else:
+                nc.vector.tensor_tensor(q[:, j, :], accs[j][:], picked_x[j], MULT)
+            for k in range(PACK):
+                nc.tensor.matmul(
+                    q_t[:, k, :],
+                    q[:, j, k * P : (k + 1) * P],
+                    ident[:],
+                    start=(j == PRODUCTS[0] and k == 0),
+                    stop=(j == PRODUCTS[-1] and k == PACK - 1),
+                    is_transpose=True,
+                )
+        for upper in (3, 2):
+            round_paired(upper, PARTS[2], nc.vector.tensor_copy)
+
+        weave(512, 1024)
         weave(1024, 1536)
         scaled = sb.tile([P, PACK, P], F32, name="scaled")
         for k in range(PACK):
@@ -289,7 +302,7 @@ def tile_attend_gtopk_pl_kernel(tc, xT, sc, W, dz, offs, out_0, out_1, out_2, ou
         nc.scalar.copy(result_rows[:], result_t[0:32, :])
         nc.scalar.dma_start(out=out_1.rearrange("o (k n) -> (o k) n", k=PACK), in_=result_rows[0:PACK, :])
         weave(1792, 2048)
-        for lo, hi in zip(CALLS, CALLS[1:]):
+        for lo, hi in zip(CALLS[1:], CALLS[2:]):
             quantise(lo, hi)
         scales_out = out_3.bitcast(I32).rearrange("o r (b c) -> b (o r) c", b=BANDS)
         for quadrant in range(4):

@@ -26,6 +26,7 @@ HALF = SLOTS // 2
 BAND = 1024
 BANDS = NODES // BAND
 PARTS = ((0, 512), (512, 1536), (1536, 2048))
+SCALAR_UPPER = 256
 PRODUCTS = (0, 2, 3, 1)
 CALLS = (0, 512, 1024, 1536, 1792, 2048)
 FUSED = 1
@@ -156,7 +157,7 @@ def tile_attend_gtopk_pl_kernel(tc, xT, sc, W, dz, offs, out_0, out_1, out_2, ou
         pairs = {}
 
         def pair_tile(part, tag):
-            pairs[part] = sb.tile([P, 2 * (part[1] - part[0])], F32, name=f"pairs{part[0]}", tag=tag, align_bytes=64)
+            pairs[part] = sb.tile([P, 2 * max(part[1] - part[0], SLOTS)], F32, name=f"pairs{part[0]}", tag=tag, align_bytes=64)
             return pairs[part]
 
         last_pairs = pair_tile(PARTS[2], "u_fused")
@@ -206,10 +207,11 @@ def tile_attend_gtopk_pl_kernel(tc, xT, sc, W, dz, offs, out_0, out_1, out_2, ou
         def pool_copy(out, in_):
             nc.gpsimd.tensor_scalar(out, in_, 1.0, -0.0, MULT, ADD)
 
-        def round_paired(j, part, copy):
-            width = part[1] - part[0]
-            words = pairs[part][:, j // 2 * width : (j // 2 + 1) * width]
-            copy(words.bitcast(BF16).rearrange("p (c e) -> p c e", e=2)[:, :, j % 2], windows[j][:, part[0] : part[1]])
+        def round_paired(j, lo, hi, copy):
+            part = max(part for part in PARTS if part[0] <= lo)
+            start = j // 2 * max(part[1] - part[0], SLOTS) - part[0]
+            words = pairs[part][:, start + lo : start + hi]
+            copy(words.bitcast(BF16).rearrange("p (c e) -> p c e", e=2)[:, :, j % 2], windows[j][:, lo:hi])
 
         def gather_x(j):
             nc.scalar.activation(picked_x[j], x_planes[j][:].indirect(offsets[:]), COPY)
@@ -218,18 +220,18 @@ def tile_attend_gtopk_pl_kernel(tc, xT, sc, W, dz, offs, out_0, out_1, out_2, ou
         gather_x(0)
         scatter_scalar(2, 0)
         middle_pairs = pair_tile(PARTS[1], "dx2_0")
-        picked_x[2] = middle_pairs[:, 2 * SLOTS : 3 * SLOTS]
+        picked_x[2] = middle_pairs[:, PARTS[1][1] - PARTS[1][0] :][:, HALF : HALF + SLOTS]
         gather_x(2)
         scatter_scalar(2, 1)
         store(2)
-        picked_last = middle_pairs[:, 3 * SLOTS : 3 * SLOTS + HALF]
-        nc.scalar.activation(picked_last, x_planes[3][:].indirect(offsets[:, halves[1][1]]), COPY)
         nc.vector.tensor_copy(windows[3][:].indirect(offsets[:]), dx_last[:])
         store(3)
         q = sb.tile([P, PACK, SLOTS], F32, name="q", tag="dx3", align_bytes=64)
+        picked_x[3] = q[:, FUSED, :]
+        nc.vector.tensor_copy(picked_x[3], x_planes[3][:].indirect(offsets[:]))
         for part in PARTS[:2]:
             for j in (0, 1):
-                round_paired(j, part, pool_copy)
+                round_paired(j, *part, pool_copy)
 
         t_cols = ps.tile([P, PACK, P], F32, name="t_cols", tag=f"acc{FUSED}")
         for k in range(PACK):
@@ -240,14 +242,14 @@ def tile_attend_gtopk_pl_kernel(tc, xT, sc, W, dz, offs, out_0, out_1, out_2, ou
         nc.gpsimd.tensor_scalar(slope[:], t_sq[:], -1.0, 1.0, MULT, ADD)
 
         for j in (0, 1):
-            round_paired(j, PARTS[2], nc.scalar.copy)
-        grouped = sb.tile([P, NODES * PACK], BF16, name="grouped", tag=f"x_plane{PACK - 1}", align_bytes=64)
+            round_paired(j, *PARTS[2], nc.scalar.copy)
+        grouped = [sb.tile([P, BAND * PACK], BF16, name=f"grouped{b}", tag=(f"x_plane{PACK - 1}", "grouped1")[b], align_bytes=64) for b in range(BANDS)]
 
         def weave(lo, hi):
             part = max(part for part in PARTS if part[0] <= lo)
             base = part[0]
             nc.scalar.copy(
-                grouped[:, lo * PACK : hi * PACK].bitcast(F32).rearrange("p (c h) -> p c h", h=2),
+                grouped[lo // BAND][:, lo % BAND * PACK : (lo % BAND + hi - lo) * PACK].bitcast(F32).rearrange("p (c h) -> p c h", h=2),
                 pairs[part][:].rearrange("p (h c) -> p c h", h=2)[:, lo - base : hi - base, :],
             )
 
@@ -259,23 +261,21 @@ def tile_attend_gtopk_pl_kernel(tc, xT, sc, W, dz, offs, out_0, out_1, out_2, ou
             nc.vector.quantize_mx(
                 out=out_codes[:, lo:hi].bitcast(E4M3X4),
                 scales=out_scales[4 * (lo // BAND) :, lo % BAND : lo % BAND + hi - lo],
-                in_=grouped[:, lo * PACK : hi * PACK],
+                in_=grouped[lo // BAND][:, lo % BAND * PACK : (lo % BAND + hi - lo) * PACK],
             )
             nc.sync.dma_start(out=words_out[:, lo:hi], in_=out_codes[:, lo:hi].bitcast(I32))
 
         q_t = ps.tile([P, PACK, P], F32, name="q_t", tag="bank_a")
         for j in PRODUCTS:
             if j == FUSED:
-                for part in PARTS[:2]:
+                for upper in (2, 3):
+                    round_paired(upper, 0, SCALAR_UPPER, nc.scalar.copy)
+                for lo, hi in ((SCALAR_UPPER, PARTS[0][1]), PARTS[1]):
                     for upper in (3, 2):
-                        round_paired(upper, part, nc.vector.tensor_copy)
-                weave(0, 512)
+                        round_paired(upper, lo, hi, nc.vector.tensor_copy)
+                weave(*PARTS[0])
                 quantise(0, 512)
                 nc.vector.tensor_tensor(q[:, j, :], x_planes[j][:].indirect(offsets[:]), u_fused, MULT)
-            elif j == 3:
-                nc.vector.tensor_copy(q[:, FUSED, first], x_planes[3][:].indirect(offsets[:, halves[0][1]]))
-                nc.vector.tensor_tensor(q[:, j, second], accs[j][:, second], picked_last, MULT)
-                nc.vector.tensor_tensor(q[:, j, first], accs[j][:, first], q[:, FUSED, first], MULT)
             else:
                 nc.vector.tensor_tensor(q[:, j, :], accs[j][:], picked_x[j], MULT)
             for k in range(PACK):
@@ -288,9 +288,10 @@ def tile_attend_gtopk_pl_kernel(tc, xT, sc, W, dz, offs, out_0, out_1, out_2, ou
                     is_transpose=True,
                 )
         for upper in (3, 2):
-            round_paired(upper, PARTS[2], nc.vector.tensor_copy)
+            round_paired(upper, *PARTS[2], nc.vector.tensor_copy)
 
         weave(512, 1024)
+        quantise(512, 1024)
         weave(1024, 1536)
         scaled = sb.tile([P, PACK, P], F32, name="scaled")
         for k in range(PACK):
@@ -298,11 +299,11 @@ def tile_attend_gtopk_pl_kernel(tc, xT, sc, W, dz, offs, out_0, out_1, out_2, ou
         result_t = ps.tile([P, P], F32, name="result_t", tag="bank_b")
         nc.tensor.transpose(result_t[:], result_cols[:], ident[:])
         weave(1536, 1792)
-        result_rows = sb.tile([32, P], F32, name="result_rows")
+        result_rows = sb.tile([32, P], F32, name="result_rows", tag=f"x_plane{PACK - 1}", align_bytes=64)
         nc.scalar.copy(result_rows[:], result_t[0:32, :])
         nc.scalar.dma_start(out=out_1.rearrange("o (k n) -> (o k) n", k=PACK), in_=result_rows[0:PACK, :])
         weave(1792, 2048)
-        for lo, hi in zip(CALLS[1:], CALLS[2:]):
+        for lo, hi in zip(CALLS[2:], CALLS[3:]):
             quantise(lo, hi)
         scales_out = out_3.bitcast(I32).rearrange("o r (b c) -> b (o r) c", b=BANDS)
         for quadrant in range(4):

@@ -26,7 +26,8 @@ HALF = SLOTS // 2
 BAND = 1024
 BANDS = NODES // BAND
 PARTS = ((0, 512), (512, 1536), (1536, 2048))
-SCALAR_UPPER = 256
+SCALAR_TO = 1792
+STORE = 512
 PRODUCTS = (0, 2, 3, 1)
 CALLS = (0, 512, 1024, 1536, 1792, 2048)
 FUSED = 1
@@ -54,11 +55,10 @@ def tile_attend_gtopk_pl_kernel(tc, xT, sc, W, dz, offs, out_0, out_1, out_2, ou
         nc.sync.dma_start(out=w_raw[1][:], in_=w_rows[:, :, HALF:FEATS])
         nc.sync.dma_start(out=dz_raw[1][:], in_=dz_rows[:, :, HALF:SLOTS])
         x_rows = xT.rearrange("(p j) c -> p j c", j=PACK)
-        x_planes = []
-        for j in range(PACK):
-            plane = sb.tile([P, NODES], F32, name=f"x_plane{j}", tag=f"x_plane{j}", align_bytes=64)
-            nc.sync.dma_start(out=plane[:], in_=x_rows[:, j, :])
-            x_planes.append(plane)
+        x_planes = {}
+        for j in PRODUCTS:
+            x_planes[j] = sb.tile([P, NODES], F32, name=f"x_plane{j}", tag=f"x_plane{j}", align_bytes=64)
+            nc.sync.dma_start(out=x_planes[j][:], in_=x_rows[:, j, :])
 
         blank = sb.tile([P, P], F32, name="blank", tag="window1")
         nc.gpsimd.memset(blank[:], 0.0)
@@ -161,7 +161,7 @@ def tile_attend_gtopk_pl_kernel(tc, xT, sc, W, dz, offs, out_0, out_1, out_2, ou
             return pairs[part]
 
         last_pairs = pair_tile(PARTS[2], "u_fused")
-        u_fused = last_pairs[:, SLOTS : 2 * SLOTS]
+        u_fused = last_pairs[:, HALF : HALF + SLOTS]
         dx_halves = {(j, h): sb.tile([P, HALF], F32, name=f"dx{j}_{h}", tag=f"dx{j}_{h}", align_bytes=64)[:] for j, h in ((0, 0), (0, 1), (2, 0))}
         dx_halves[2, 1] = last_pairs[:, 0:HALF]
 
@@ -220,15 +220,14 @@ def tile_attend_gtopk_pl_kernel(tc, xT, sc, W, dz, offs, out_0, out_1, out_2, ou
         gather_x(0)
         scatter_scalar(2, 0)
         middle_pairs = pair_tile(PARTS[1], "dx2_0")
-        picked_x[2] = middle_pairs[:, PARTS[1][1] - PARTS[1][0] :][:, HALF : HALF + SLOTS]
-        gather_x(2)
+        for j in (2, 3):
+            picked_x[j] = middle_pairs[:, j * SLOTS : (j + 1) * SLOTS]
+            gather_x(j)
         scatter_scalar(2, 1)
         store(2)
         nc.vector.tensor_copy(windows[3][:].indirect(offsets[:]), dx_last[:])
         store(3)
         q = sb.tile([P, PACK, SLOTS], F32, name="q", tag="dx3", align_bytes=64)
-        picked_x[3] = q[:, FUSED, :]
-        nc.vector.tensor_copy(picked_x[3], x_planes[3][:].indirect(offsets[:]))
         for part in PARTS[:2]:
             for j in (0, 1):
                 round_paired(j, *part, pool_copy)
@@ -242,7 +241,7 @@ def tile_attend_gtopk_pl_kernel(tc, xT, sc, W, dz, offs, out_0, out_1, out_2, ou
         nc.gpsimd.tensor_scalar(slope[:], t_sq[:], -1.0, 1.0, MULT, ADD)
 
         for j in (0, 1):
-            round_paired(j, *PARTS[2], nc.scalar.copy)
+            round_paired(j, PARTS[2][0], SCALAR_TO, nc.scalar.copy)
         grouped = [sb.tile([P, BAND * PACK], BF16, name=f"grouped{b}", tag=(f"x_plane{PACK - 1}", "grouped1")[b], align_bytes=64) for b in range(BANDS)]
 
         def weave(lo, hi):
@@ -263,16 +262,15 @@ def tile_attend_gtopk_pl_kernel(tc, xT, sc, W, dz, offs, out_0, out_1, out_2, ou
                 scales=out_scales[4 * (lo // BAND) :, lo % BAND : lo % BAND + hi - lo],
                 in_=grouped[lo // BAND][:, lo % BAND * PACK : (lo % BAND + hi - lo) * PACK],
             )
-            nc.sync.dma_start(out=words_out[:, lo:hi], in_=out_codes[:, lo:hi].bitcast(I32))
+            if hi % STORE == 0:
+                nc.sync.dma_start(out=words_out[:, hi - STORE : hi], in_=out_codes[:, hi - STORE : hi].bitcast(I32))
 
         q_t = ps.tile([P, PACK, P], F32, name="q_t", tag="bank_a")
         for j in PRODUCTS:
             if j == FUSED:
-                for upper in (2, 3):
-                    round_paired(upper, 0, SCALAR_UPPER, nc.scalar.copy)
-                for lo, hi in ((SCALAR_UPPER, PARTS[0][1]), PARTS[1]):
+                for part in PARTS[:2]:
                     for upper in (3, 2):
-                        round_paired(upper, lo, hi, nc.vector.tensor_copy)
+                        round_paired(upper, *part, nc.vector.tensor_copy)
                 weave(*PARTS[0])
                 quantise(0, 512)
                 nc.vector.tensor_tensor(q[:, j, :], x_planes[j][:].indirect(offsets[:]), u_fused, MULT)
@@ -289,6 +287,8 @@ def tile_attend_gtopk_pl_kernel(tc, xT, sc, W, dz, offs, out_0, out_1, out_2, ou
                 )
         for upper in (3, 2):
             round_paired(upper, *PARTS[2], nc.vector.tensor_copy)
+        for lower in (0, 1):
+            round_paired(lower, SCALAR_TO, NODES, nc.vector.tensor_copy)
 
         weave(512, 1024)
         quantise(512, 1024)

@@ -26,6 +26,7 @@ HALF = SLOTS // 2
 BAND = 1024
 BANDS = NODES // BAND
 PARTS = ((0, 512), (512, 1536), (1536, 2048))
+POOL_TO = 1280
 SCALAR_TO = 1792
 STORE = 512
 PRODUCTS = (0, 2, 3, 1)
@@ -228,9 +229,9 @@ def tile_attend_gtopk_pl_kernel(tc, xT, sc, W, dz, offs, out_0, out_1, out_2, ou
         nc.vector.tensor_copy(windows[3][:].indirect(offsets[:]), dx_last[:])
         store(3)
         q = sb.tile([P, PACK, SLOTS], F32, name="q", tag="dx3", align_bytes=64)
-        for part in PARTS[:2]:
+        for lo, hi in (PARTS[0], (PARTS[1][0], POOL_TO)):
             for j in (0, 1):
-                round_paired(j, *part, pool_copy)
+                round_paired(j, lo, hi, pool_copy)
 
         t_cols = ps.tile([P, PACK, P], F32, name="t_cols", tag=f"acc{FUSED}")
         for k in range(PACK):
@@ -240,8 +241,9 @@ def tile_attend_gtopk_pl_kernel(tc, xT, sc, W, dz, offs, out_0, out_1, out_2, ou
         slope = sb.tile([P, PACK], F32, name="slope")
         nc.gpsimd.tensor_scalar(slope[:], t_sq[:], -1.0, 1.0, MULT, ADD)
 
-        for j in (0, 1):
-            round_paired(j, PARTS[2][0], SCALAR_TO, nc.scalar.copy)
+        for lo, hi in ((POOL_TO, PARTS[1][1]), (PARTS[2][0], SCALAR_TO)):
+            for j in (0, 1):
+                round_paired(j, lo, hi, nc.scalar.copy)
         grouped = [sb.tile([P, BAND * PACK], BF16, name=f"grouped{b}", tag=(f"x_plane{PACK - 1}", "grouped1")[b], align_bytes=64) for b in range(BANDS)]
 
         def weave(lo, hi):

@@ -217,7 +217,7 @@ def tile_attend_gtopk_pl_kernel(tc, xT, sc, W, dz, offs, out_0, out_1, out_2, ou
         def gather_x(j):
             nc.scalar.activation(picked_x[j], x_planes[j][:].indirect(offsets[:]), COPY)
 
-        picked_x = {0: pair_tile(PARTS[0], "dx0_0")[:, SLOTS : 2 * SLOTS]}
+        picked_x = {0: pair_tile(PARTS[0], "picked1")[:, SLOTS : 2 * SLOTS]}
         gather_x(0)
         scatter_scalar(2, 0)
         middle_pairs = pair_tile(PARTS[1], "dx2_0")
@@ -230,7 +230,7 @@ def tile_attend_gtopk_pl_kernel(tc, xT, sc, W, dz, offs, out_0, out_1, out_2, ou
         store(3)
         q = sb.tile([P, PACK, SLOTS], F32, name="q", tag="dx3", align_bytes=64)
         for lo, hi in (PARTS[0], (PARTS[1][0], POOL_TO)):
-            for j in (0, 1):
+            for j in (1, 0):
                 round_paired(j, lo, hi, pool_copy)
 
         t_cols = ps.tile([P, PACK, P], F32, name="t_cols", tag=f"acc{FUSED}")
@@ -270,8 +270,8 @@ def tile_attend_gtopk_pl_kernel(tc, xT, sc, W, dz, offs, out_0, out_1, out_2, ou
         q_t = ps.tile([P, PACK, P], F32, name="q_t", tag="bank_a")
         for j in PRODUCTS:
             if j == FUSED:
-                for part in PARTS[:2]:
-                    for upper in (3, 2):
+                for upper in (3, 2):
+                    for part in PARTS[:2]:
                         round_paired(upper, *part, nc.vector.tensor_copy)
                 weave(*PARTS[0])
                 quantise(0, 512)

@@ -44,7 +44,7 @@ def tile_attend_gtopk_pl_kernel(tc, xT, sc, W, dz, offs, out_0, out_1, out_2, ou
         ps = ctx.enter_context(tc.psum_pool(name="ps", bufs=1))
 
         offsets = sb.tile([P, SLOTS // 16], U16, name="offsets")
-        score_cols = sb.tile([P, NODES // P], F32, name="score_cols", tag="window3", align_bytes=64)
+        score_cols = sb.tile([P, NODES // P], F32, name="score_cols", tag="window2", align_bytes=64)
         nc.sync.dma_start(out=score_cols[:], in_=sc[0:1, :].rearrange("o (p k) -> (o p) k", p=P))
         w_rows = W.rearrange("(p j) d -> p j d", j=PACK)
         dz_rows = dz.rearrange("(p j) i -> p j i", j=PACK)
@@ -61,7 +61,7 @@ def tile_attend_gtopk_pl_kernel(tc, xT, sc, W, dz, offs, out_0, out_1, out_2, ou
             x_planes[j] = sb.tile([P, NODES], F32, name=f"x_plane{j}", tag=f"x_plane{j}", align_bytes=64)
             nc.sync.dma_start(out=x_planes[j][:], in_=x_rows[:, j, :])
 
-        blank = sb.tile([P, P], F32, name="blank", tag="window1")
+        blank = sb.tile([P, P], F32, name="blank", tag="window1", align_bytes=64)
         nc.gpsimd.memset(blank[:], 0.0)
         ident = sb.tile([P, P], F32, name="ident")
         nc.gpsimd.affine_select(
@@ -76,7 +76,7 @@ def tile_attend_gtopk_pl_kernel(tc, xT, sc, W, dz, offs, out_0, out_1, out_2, ou
         result_cols = sb.tile([P, P], F32, name="result_cols")
         nc.scalar.activation(result_cols[:], ident[:], TANH, scale=0.0)
 
-        windows = [sb.tile([P, NODES], F32, name="window0"), sb.tile([P, NODES], F32, name="window1", tag="window1")]
+        windows = [sb.tile([P, NODES], F32, name="window0"), sb.tile([P, NODES], F32, name="window1", tag="window1", align_bytes=64)]
         nc.vector.memset(windows[0][:].bitcast(I32), 0)
         nc.gpsimd.memset(windows[1][:].bitcast(I32), 0)
 
@@ -91,8 +91,8 @@ def tile_attend_gtopk_pl_kernel(tc, xT, sc, W, dz, offs, out_0, out_1, out_2, ou
 
         halves = [(slice(h * HALF, (h + 1) * HALF), slice(h * HALF // 16, (h + 1) * HALF // 16)) for h in range(2)]
 
-        w_grouped = [sb.tile([P, 2, P, PACK], BF16, name=f"w_grouped{g}", tag=("window2", "w_grouped1")[g], align_bytes=64) for g in range(2)]
-        w_codes = sb.tile([P, FEATS], U32, name="w_codes", tag="window3", align_bytes=64)
+        w_grouped = [sb.tile([P, 2, P, PACK], BF16, name=f"w_grouped{g}", tag=("window3", "w_grouped1")[g], align_bytes=64) for g in range(2)]
+        w_codes = sb.tile([P, FEATS], U32, name="w_codes", tag="window2", align_bytes=64)
         w_scales = sb.tile([P, FEATS], U8, name="w_scales", align_bytes=64)
         dz_mx = []
         t_rows = sb.tile([P, SLOTS], F32, name="t_rows")
@@ -112,7 +112,7 @@ def tile_attend_gtopk_pl_kernel(tc, xT, sc, W, dz, offs, out_0, out_1, out_2, ou
             )
 
         def regroup_dz(h):
-            dz_grouped = sb.tile([P, HALF, PACK], BF16, name=f"dz_grouped{h}", tag=("dz_grouped0", "window2")[h], align_bytes=64)
+            dz_grouped = sb.tile([P, HALF, PACK], BF16, name=f"dz_grouped{h}", tag=("dz_grouped0", "window3")[h], align_bytes=64)
             nc.vector.tensor_copy(
                 dz_grouped[:].rearrange("p (c i) j -> p c j i", i=4),
                 dz_raw[h][:].rearrange("p j (c i) -> p c j i", i=4),
@@ -178,7 +178,7 @@ def tile_attend_gtopk_pl_kernel(tc, xT, sc, W, dz, offs, out_0, out_1, out_2, ou
         gate(0, 1)
 
         windows += [sb.tile([P, NODES], F32, name=f"window{j}", tag=f"window{j}", align_bytes=64) for j in (2, 3)]
-        for j in (2, 3):
+        for j in (3, 2):
             nc.gpsimd.memset(windows[j][:].bitcast(I32), 0)
 
         out_rows = out_0.rearrange("(p j) c -> p j c", j=PACK)
@@ -204,6 +204,8 @@ def tile_attend_gtopk_pl_kernel(tc, xT, sc, W, dz, offs, out_0, out_1, out_2, ou
         nc.vector.tensor_tensor(dx_last[:], accs[3][:], t_rows[:], MULT)
         scatter_fused(1)
         store(FUSED)
+        nc.vector.tensor_copy(windows[3][:].indirect(offsets[:]), dx_last[:])
+        store(3)
 
         def pool_copy(out, in_):
             nc.gpsimd.tensor_scalar(out, in_, 1.0, -0.0, MULT, ADD)
@@ -226,9 +228,9 @@ def tile_attend_gtopk_pl_kernel(tc, xT, sc, W, dz, offs, out_0, out_1, out_2, ou
             gather_x(j)
         scatter_scalar(2, 1)
         store(2)
-        nc.vector.tensor_copy(windows[3][:].indirect(offsets[:]), dx_last[:])
-        store(3)
-        q = sb.tile([P, PACK, SLOTS], F32, name="q", tag="dx3", align_bytes=64)
+        q_plain = sb.tile([P, PACK - 1, SLOTS], F32, name="q_plain", tag="dx3", align_bytes=64)
+        q = {j: q_plain[:, n, :] for n, j in enumerate(PRODUCTS[:-1])}
+        q[FUSED] = sb.tile([P, SLOTS], F32, name="q_fused", tag=f"x_plane{PRODUCTS[-2]}", align_bytes=64)[:]
         for lo, hi in (PARTS[0], (PARTS[1][0], POOL_TO)):
             for j in (1, 0):
                 round_paired(j, lo, hi, pool_copy)
@@ -244,13 +246,13 @@ def tile_attend_gtopk_pl_kernel(tc, xT, sc, W, dz, offs, out_0, out_1, out_2, ou
         for lo, hi in ((POOL_TO, PARTS[1][1]), (PARTS[2][0], SCALAR_TO)):
             for j in (0, 1):
                 round_paired(j, lo, hi, nc.scalar.copy)
-        grouped = [sb.tile([P, BAND * PACK], BF16, name=f"grouped{b}", tag=(f"x_plane{PACK - 1}", "grouped1")[b], align_bytes=64) for b in range(BANDS)]
+        grouped = {lo: sb.tile([P, (hi - lo) * PACK], BF16, name=f"grouped{lo}", tag="window1" if hi == NODES else f"grouped{lo}", align_bytes=64) for lo, hi in zip(CALLS, CALLS[1:])}
 
         def weave(lo, hi):
             part = max(part for part in PARTS if part[0] <= lo)
             base = part[0]
             nc.scalar.copy(
-                grouped[lo // BAND][:, lo % BAND * PACK : (lo % BAND + hi - lo) * PACK].bitcast(F32).rearrange("p (c h) -> p c h", h=2),
+                grouped[lo][:].bitcast(F32).rearrange("p (c h) -> p c h", h=2),
                 pairs[part][:].rearrange("p (h c) -> p c h", h=2)[:, lo - base : hi - base, :],
             )
 
@@ -262,7 +264,7 @@ def tile_attend_gtopk_pl_kernel(tc, xT, sc, W, dz, offs, out_0, out_1, out_2, ou
             nc.vector.quantize_mx(
                 out=out_codes[:, lo:hi].bitcast(E4M3X4),
                 scales=out_scales[4 * (lo // BAND) :, lo % BAND : lo % BAND + hi - lo],
-                in_=grouped[lo // BAND][:, lo % BAND * PACK : (lo % BAND + hi - lo) * PACK],
+                in_=grouped[lo][:],
             )
             if hi % STORE == 0:
                 nc.sync.dma_start(out=words_out[:, hi - STORE : hi], in_=out_codes[:, hi - STORE : hi].bitcast(I32))
@@ -275,13 +277,13 @@ def tile_attend_gtopk_pl_kernel(tc, xT, sc, W, dz, offs, out_0, out_1, out_2, ou
                         round_paired(upper, *part, nc.vector.tensor_copy)
                 weave(*PARTS[0])
                 quantise(0, 512)
-                nc.vector.tensor_tensor(q[:, j, :], x_planes[j][:].indirect(offsets[:]), u_fused, MULT)
+                nc.vector.tensor_tensor(q[j], x_planes[j][:].indirect(offsets[:]), u_fused, MULT)
             else:
-                nc.vector.tensor_tensor(q[:, j, :], accs[j][:], picked_x[j], MULT)
+                nc.vector.tensor_tensor(q[j], accs[j][:], picked_x[j], MULT)
             for k in range(PACK):
                 nc.tensor.matmul(
                     q_t[:, k, :],
-                    q[:, j, k * P : (k + 1) * P],
+                    q[j][:, k * P : (k + 1) * P],
                     ident[:],
                     start=(j == PRODUCTS[0] and k == 0),
                     stop=(j == PRODUCTS[-1] and k == PACK - 1),
@@ -301,12 +303,13 @@ def tile_attend_gtopk_pl_kernel(tc, xT, sc, W, dz, offs, out_0, out_1, out_2, ou
         result_t = ps.tile([P, P], F32, name="result_t", tag="bank_b")
         nc.tensor.transpose(result_t[:], result_cols[:], ident[:])
         weave(1536, 1792)
-        result_rows = sb.tile([32, P], F32, name="result_rows", tag=f"x_plane{PACK - 1}", align_bytes=64)
+        weave(1792, 2048)
+        for lo, hi in zip(CALLS[2:-2], CALLS[3:-1]):
+            quantise(lo, hi)
+        result_rows = sb.tile([32, P], F32, name="result_rows", tag="u_fused", align_bytes=64)
         nc.scalar.copy(result_rows[:], result_t[0:32, :])
         nc.scalar.dma_start(out=out_1.rearrange("o (k n) -> (o k) n", k=PACK), in_=result_rows[0:PACK, :])
-        weave(1792, 2048)
-        for lo, hi in zip(CALLS[2:], CALLS[3:]):
-            quantise(lo, hi)
+        quantise(*CALLS[-2:])
         scales_out = out_3.bitcast(I32).rearrange("o r (b c) -> b (o r) c", b=BANDS)
         for quadrant in range(4):
             queue = nc.scalar if quadrant % 2 == 0 else nc.sync

from contextlib import ExitStack

import concourse.mybir as mybir

F32 = mybir.dt.float32
BF16 = mybir.dt.bfloat16
I32 = mybir.dt.int32
U32 = mybir.dt.uint32
U16 = mybir.dt.uint16
U8 = mybir.dt.uint8
E4M3X4 = mybir.dt.float8_e4m3fn_x4
E5M2X4 = mybir.dt.float8_e5m2_x4
MULT = mybir.AluOpType.mult
ADD = mybir.AluOpType.add
COPY = mybir.ActivationFunctionType.Copy
SQUARE = mybir.ActivationFunctionType.Square
TANH = mybir.ActivationFunctionType.Tanh

P = 128
PACK = 4
SLOTS = 512
NODES = 2048
FEATS = 512
OUTS = 512
HALF = SLOTS // 2
BAND = 1024
BANDS = NODES // BAND
PARTS = ((0, 512), (512, 1536), (1536, 2048))
POOL_TO = 1280
SCALAR_TO = 1792
STORE = 512
PRODUCTS = (0, 2, 3, 1)
CALLS = (0, 512, 1024, 1536, 1792, 2048)
FUSED = 1

FLOPS = 2 * OUTS * FEATS * SLOTS
BYTES = 4 * (2 * FEATS * NODES + NODES + OUTS * FEATS + OUTS * SLOTS + SLOTS) + 2 * P * SLOTS // 16 + FEATS * NODES + FEATS * NODES // 32


def tile_attend_gtopk_pl_kernel(tc, xT, sc, W, dz, offs, out_0, out_1, out_2, out_3):
    nc = tc.nc
    with ExitStack() as ctx:
        sb = ctx.enter_context(tc.tile_pool(name="sb", bufs=1))
        ps = ctx.enter_context(tc.psum_pool(name="ps", bufs=1))

        offsets = sb.tile([P, SLOTS // 16], U16, name="offsets")
        score_cols = sb.tile([P, NODES // P], F32, name="score_cols", tag="window2", align_bytes=64)
        nc.sync.dma_start(out=score_cols[:], in_=sc[0:1, :].rearrange("o (p k) -> (o p) k", p=P))
        w_rows = W.rearrange("(p j) d -> p j d", j=PACK)
        dz_rows = dz.rearrange("(p j) i -> p j i", j=PACK)
        dz_raw = [sb.tile([P, PACK, HALF], F32, name=f"dz_raw{h}") for h in range(2)]
        w_raw = [sb.tile([P, PACK, HALF], F32, name=f"w_raw{h}") for h in range(2)]
        nc.sync.dma_start(out=dz_raw[0][:], in_=dz_rows[:, :, 0:HALF])
        nc.sync.dma_start(out=w_raw[0][:], in_=w_rows[:, :, 0:HALF])
        nc.sync.dma_start(offsets[:], offs)
        nc.sync.dma_start(out=w_raw[1][:], in_=w_rows[:, :, HALF:FEATS])
        nc.sync.dma_start(out=dz_raw[1][:], in_=dz_rows[:, :, HALF:SLOTS])
        x_rows = xT.rearrange("(p j) c -> p j c", j=PACK)
        x_planes = {}
        for j in PRODUCTS:
            x_planes[j] = sb.tile([P, NODES], F32, name=f"x_plane{j}", tag=f"x_plane{j}", align_bytes=64)
            nc.sync.dma_start(out=x_planes[j][:], in_=x_rows[:, j, :])

        blank = sb.tile([P, P], F32, name="blank", tag="window1", align_bytes=64)
        nc.gpsimd.memset(blank[:], 0.0)
        ident = sb.tile([P, P], F32, name="ident")
        nc.gpsimd.affine_select(
            out=ident[:],
            in_=blank[:],
            compare_op=mybir.AluOpType.not_equal,
            fill=1.0,
            base=0,
            pattern=[[-1, P]],
            channel_multiplier=1,
        )
        result_cols = sb.tile([P, P], F32, name="result_cols")
        nc.scalar.activation(result_cols[:], ident[:], TANH, scale=0.0)

        windows = [sb.tile([P, NODES], F32, name="window0"), sb.tile([P, NODES], F32, name="window1", tag="window1", align_bytes=64)]
        nc.vector.memset(windows[0][:].bitcast(I32), 0)
        nc.gpsimd.memset(windows[1][:].bitcast(I32), 0)

        scores = sb.tile([P, NODES], F32, name="scores")
        scores_by_col = scores[:].rearrange("p (n k) -> p n k", k=NODES // P)
        for b in range(4):
            spread = ps.tile([P, 4, P], F32, name=f"spread{b}", tag=f"acc{b}")
            for k in range(4):
                col = 4 * b + k
                nc.tensor.transpose(spread[:, k, :], score_cols[:, col : col + 1].to_broadcast([P, P]), ident[:])
            nc.scalar.activation(scores_by_col[:, :, 4 * b : 4 * b + 4], spread[:].rearrange("p k n -> p n k"), COPY)

        halves = [(slice(h * HALF, (h + 1) * HALF), slice(h * HALF // 16, (h + 1) * HALF // 16)) for h in range(2)]

        w_grouped = [sb.tile([P, 2, P, PACK], BF16, name=f"w_grouped{g}", tag=("window3", "w_grouped1")[g], align_bytes=64) for g in range(2)]
        w_codes = sb.tile([P, FEATS], U32, name="w_codes", tag="window2", align_bytes=64)
        w_scales = sb.tile([P, FEATS], U8, name="w_scales", align_bytes=64)
        dz_mx = []
        t_rows = sb.tile([P, SLOTS], F32, name="t_rows")

        def regroup_w(h, g):
            nc.vector.tensor_copy(
                w_grouped[g][:, :, h * P // 2 : (h + 1) * P // 2, :].rearrange("p t m j -> p m j t"),
                w_raw[h][:].rearrange("p j (m t) -> p m j t", t=PACK)[:, :, :, 2 * g : 2 * g + 2],
            )

        def quantise_w(g):
            cols = slice(2 * g * P, 2 * (g + 1) * P)
            nc.vector.quantize_mx(
                out=w_codes[:, cols].bitcast(E4M3X4),
                scales=w_scales[:, cols],
                in_=w_grouped[g][:].rearrange("p t m j -> p (t m j)"),
            )

        def regroup_dz(h):
            dz_grouped = sb.tile([P, HALF, PACK], BF16, name=f"dz_grouped{h}", tag=("dz_grouped0", "window3")[h], align_bytes=64)
            nc.vector.tensor_copy(
                dz_grouped[:].rearrange("p (c i) j -> p c j i", i=4),
                dz_raw[h][:].rearrange("p j (c i) -> p c j i", i=4),
            )
            return dz_grouped

        def quantise_dz(h, dz_grouped):
            codes = sb.tile([P, HALF], U32, name=f"dz_codes{h}", tag=("dz_codes0", "picked1")[h], align_bytes=64)
            scales = sb.tile([P, HALF], U8, name=f"dz_scales{h}", align_bytes=64)
            nc.vector.quantize_mx(out=codes[:].bitcast(E5M2X4), scales=scales[:], in_=dz_grouped[:].rearrange("p c j -> p (c j)"))
            dz_mx.append((codes, scales))

        for h, (slots, entries) in enumerate(halves):
            picked_scores = sb.tile([P, HALF], F32, name=f"picked_scores{h}", tag=("u_fused", "picked1")[h], align_bytes=64)
            nc.scalar.activation(picked_scores[:], scores[:].indirect(offsets[:, entries]), COPY)
            nc.scalar.activation(t_rows[:, slots], picked_scores[:], TANH)

        accs = [ps.tile([P, SLOTS], F32, name=f"u{j}", tag=f"acc{j}") for j in range(PACK)]

        def multiply(j, h):
            codes, scales = dz_mx[h]
            nc.tensor.matmul_mx(
                out=accs[j][:, halves[h][0]],
                lhsT=w_codes[:, j * P : (j + 1) * P].bitcast(E4M3X4),
                lhsT_scale=w_scales[:, j * P : (j + 1) * P],
                rhs=codes[:].bitcast(E5M2X4),
                rhs_scale=scales[:],
                start=True,
                stop=True,
            )

        first, second = halves[0][0], halves[1][0]
        quantise_dz(0, regroup_dz(0))
        for h in range(2):
            for g in range(2):
                regroup_w(h, g)
        for g in range(2):
            quantise_w(g)
        for j in range(PACK):
            multiply(j, 0)
        dz_second = regroup_dz(1)
        dx_last = sb.tile([P, SLOTS], F32, name="dx3", tag="dx3", align_bytes=64)
        pairs = {}

        def pair_tile(part, tag):
            pairs[part] = sb.tile([P, 2 * max(part[1] - part[0], SLOTS)], F32, name=f"pairs{part[0]}", tag=tag, align_bytes=64)
            return pairs[part]

        last_pairs = pair_tile(PARTS[2], "u_fused")
        u_fused = last_pairs[:, HALF : HALF + SLOTS]
        dx_halves = {(j, h): sb.tile([P, HALF], F32, name=f"dx{j}_{h}", tag=f"dx{j}_{h}", align_bytes=64)[:] for j, h in ((0, 0), (0, 1), (2, 0))}
        dx_halves[2, 1] = last_pairs[:, 0:HALF]

        def gate(j, h):
            slots = halves[h][0]
            nc.vector.tensor_tensor(dx_halves[j, h], accs[j][:, slots], t_rows[:, slots], MULT)

        gate(0, 0)
        nc.scalar.copy(u_fused[:, first], accs[FUSED][:, first])
        quantise_dz(1, dz_second)
        for j in range(PACK):
            multiply(j, 1)
        gate(0, 1)

        windows += [sb.tile([P, NODES], F32, name=f"window{j}", tag=f"window{j}", align_bytes=64) for j in (2, 3)]
        for j in (3, 2):
            nc.gpsimd.memset(windows[j][:].bitcast(I32), 0)

        out_rows = out_0.rearrange("(p j) c -> p j c", j=PACK)

        def scatter_scalar(j, h):
            slots, entries = halves[h]
            nc.scalar.activation(windows[j][:].indirect(offsets[:, entries]), dx_halves[j, h], COPY)

        def scatter_fused(h):
            slots, entries = halves[h]
            nc.vector.tensor_tensor(windows[FUSED][:].indirect(offsets[:, entries]), u_fused[:, slots], t_rows[:, slots], MULT)

        def store(j):
            nc.sync.dma_start(out=out_rows[:, j, :], in_=windows[j][:])

        scatter_scalar(0, 0)
        nc.scalar.copy(u_fused[:, second], accs[FUSED][:, second])
        scatter_fused(0)
        scatter_scalar(0, 1)
        store(0)
        gate(2, 0)
        gate(2, 1)
        nc.vector.tensor_tensor(dx_last[:], accs[3][:], t_rows[:], MULT)
        scatter_fused(1)
        store(FUSED)
        nc.vector.tensor_copy(windows[3][:].indirect(offsets[:]), dx_last[:])
        store(3)

        def pool_copy(out, in_):
            nc.gpsimd.tensor_scalar(out, in_, 1.0, -0.0, MULT, ADD)

        def round_paired(j, lo, hi, copy):
            part = max(part for part in PARTS if part[0] <= lo)
            start = j // 2 * max(part[1] - part[0], SLOTS) - part[0]
            words = pairs[part][:, start + lo : start + hi]
            copy(words.bitcast(BF16).rearrange("p (c e) -> p c e", e=2)[:, :, j % 2], windows[j][:, lo:hi])

        def gather_x(j):
            nc.scalar.activation(picked_x[j], x_planes[j][:].indirect(offsets[:]), COPY)

        picked_x = {0: pair_tile(PARTS[0], "picked1")[:, SLOTS : 2 * SLOTS]}
        gather_x(0)
        scatter_scalar(2, 0)
        middle_pairs = pair_tile(PARTS[1], "dx2_0")
        for j in (2, 3):
            picked_x[j] = middle_pairs[:, j * SLOTS : (j + 1) * SLOTS]
            gather_x(j)
        scatter_scalar(2, 1)
        store(2)
        q_plain = sb.tile([P, PACK - 1, SLOTS], F32, name="q_plain", tag="dx3", align_bytes=64)
        q = {j: q_plain[:, n, :] for n, j in enumerate(PRODUCTS[:-1])}
        q[FUSED] = sb.tile([P, SLOTS], F32, name="q_fused", tag=f"x_plane{PRODUCTS[-2]}", align_bytes=64)[:]
        for lo, hi in (PARTS[0], (PARTS[1][0], POOL_TO)):
            for j in (1, 0):
                round_paired(j, lo, hi, pool_copy)

        t_cols = ps.tile([P, PACK, P], F32, name="t_cols", tag=f"acc{FUSED}")
        for k in range(PACK):
            nc.tensor.transpose(t_cols[:, k, :], t_rows[:, k * P : (k + 1) * P], ident[:])
        t_sq = sb.tile([P, PACK], F32, name="t_sq", tag="x_plane0", align_bytes=64)
        nc.scalar.activation(t_sq[:], t_cols[:, :, 0], SQUARE)
        slope = sb.tile([P, PACK], F32, name="slope")
        nc.gpsimd.tensor_scalar(slope[:], t_sq[:], -1.0, 1.0, MULT, ADD)

        for lo, hi in ((POOL_TO, PARTS[1][1]), (PARTS[2][0], SCALAR_TO)):
            for j in (0, 1):
                round_paired(j, lo, hi, nc.scalar.copy)
        grouped = {lo: sb.tile([P, (hi - lo) * PACK], BF16, name=f"grouped{lo}", tag="window1" if hi == NODES else f"grouped{lo}", align_bytes=64) for lo, hi in zip(CALLS, CALLS[1:])}

        def weave(lo, hi):
            part = max(part for part in PARTS if part[0] <= lo)
            base = part[0]
            nc.scalar.copy(
                grouped[lo][:].bitcast(F32).rearrange("p (c h) -> p c h", h=2),
                pairs[part][:].rearrange("p (h c) -> p c h", h=2)[:, lo - base : hi - base, :],
            )

        words_out = out_2.rearrange("o p c l -> p (o c l)").bitcast(I32)
        out_scales = sb.tile([P, BAND], U8, name="out_scales", align_bytes=64)
        out_codes = sb.tile([P, NODES], U32, name="out_codes", align_bytes=64)

        def quantise(lo, hi):
            nc.vector.quantize_mx(
                out=out_codes[:, lo:hi].bitcast(E4M3X4),
                scales=out_scales[4 * (lo // BAND) :, lo % BAND : lo % BAND + hi - lo],
                in_=grouped[lo][:],
            )
            if hi % STORE == 0:
                nc.sync.dma_start(out=words_out[:, hi - STORE : hi], in_=out_codes[:, hi - STORE : hi].bitcast(I32))

        q_t = ps.tile([P, PACK, P], F32, name="q_t", tag="bank_a")
        for j in PRODUCTS:
            if j == FUSED:
                for upper in (3, 2):
                    for part in PARTS[:2]:
                        round_paired(upper, *part, nc.vector.tensor_copy)
                weave(*PARTS[0])
                quantise(0, 512)
                nc.vector.tensor_tensor(q[j], x_planes[j][:].indirect(offsets[:]), u_fused, MULT)
            else:
                nc.vector.tensor_tensor(q[j], accs[j][:], picked_x[j], MULT)
            for k in range(PACK):
                nc.tensor.matmul(
                    q_t[:, k, :],
                    q[j][:, k * P : (k + 1) * P],
                    ident[:],
                    start=(j == PRODUCTS[0] and k == 0),
                    stop=(j == PRODUCTS[-1] and k == PACK - 1),
                    is_transpose=True,
                )
        for upper in (3, 2):
            round_paired(upper, *PARTS[2], nc.vector.tensor_copy)
        for lower in (0, 1):
            round_paired(lower, SCALAR_TO, NODES, nc.vector.tensor_copy)

        weave(512, 1024)
        quantise(512, 1024)
        weave(1024, 1536)
        scaled = sb.tile([P, PACK, P], F32, name="scaled")
        for k in range(PACK):
            nc.scalar.activation(scaled[:, k, :], q_t[:, k, :], COPY, scale=slope[:, k : k + 1], accum_out=result_cols[:, k : k + 1])
        result_t = ps.tile([P, P], F32, name="result_t", tag="bank_b")
        nc.tensor.transpose(result_t[:], result_cols[:], ident[:])
        weave(1536, 1792)
        weave(1792, 2048)
        for lo, hi in zip(CALLS[2:-2], CALLS[3:-1]):
            quantise(lo, hi)
        result_rows = sb.tile([32, P], F32, name="result_rows", tag="u_fused", align_bytes=64)
        nc.scalar.copy(result_rows[:], result_t[0:32, :])
        nc.scalar.dma_start(out=out_1.rearrange("o (k n) -> (o k) n", k=PACK), in_=result_rows[0:PACK, :])
        quantise(*CALLS[-2:])
        scales_out = out_3.bitcast(I32).rearrange("o r (b c) -> b (o r) c", b=BANDS)
        for quadrant in range(4):
            queue = nc.scalar if quadrant % 2 == 0 else nc.sync
            queue.dma_start(
                out=scales_out[:, 4 * quadrant : 4 * quadrant + 4, :],
                in_=out_scales[32 * quadrant : 32 * quadrant + 4 * BANDS, :].bitcast(I32),
            )
